import numpy as np, ml_dtypes
CORES = [16,18,20,22]
N = 4
import mx_ref
BF = ml_dtypes.bfloat16
def tile(rs):
    return np.stack(rs, axis=2).reshape(128, -1).astype(BF)
def pick(q, e):
    c = np.concatenate([q[0].reshape(128, -1, 4), np.zeros((128, 1, 4), np.uint8)], axis=1); s = np.concatenate([q[1], np.ones((16, 1), np.uint8)], axis=1)
    return (np.ascontiguousarray(c[:, e].reshape(128, -1)), np.ascontiguousarray(s[:, e]))
def join(*qs):
    return (np.concatenate([q[0] for q in qs], axis=1), np.concatenate([q[1] for q in qs], axis=1))
def put(q, e, v):
    c, s = q[0].reshape(128, -1, 4).copy(), q[1].copy(); c[:, e] = v[0].reshape(128, -1, 4); s[:, e] = v[1]
    return (c.reshape(128, -1), s)
def pk(c, s):
    return (np.ascontiguousarray(c), mx_ref.live(s))
def emit(q):
    return q[0], q[1]
def packed(v, rng):
    q = [mx_ref.quantize(np.ascontiguousarray(v[r])) for r in range(N)]
    return np.stack([a for a, b in q]), np.stack([mx_ref.plane(b, rng) for a, b in q])
def values_of_codes():
    e, c = np.zeros((128, 128, 4), np.float32), np.zeros((128, 2, 4), np.uint8)
    e[np.arange(128), np.arange(128), 0] = 1
    c[:127, :, 0] = np.arange(256).reshape(2, 128).T[:127]
    return mx_ref.matmul(mx_ref.quantize(e.reshape(128, 512).astype(BF)), (c.reshape(128, 8), np.full((16, 2), 127, np.uint8))).T.reshape(-1).astype(np.float64)
CODE_VALUE, SCALE_VALUE = values_of_codes(), 2.0 ** (np.arange(256) - 127.0)
def decode(q):
    return (CODE_VALUE[q[0]].reshape(16, 8, -1, 4) * SCALE_VALUE[q[1]][:, None, :, None] + 0.0).reshape(128, -1).astype(np.float32)
def f(rng, *shape):
    return mx_ref.flush((rng.standard_normal(shape, dtype=np.float32) * np.exp2(rng.integers(-2, 3, shape[:-1] + (1,)))).astype(BF))
def wide(rng, *shape, cols=0):
    v = rng.standard_normal(shape, dtype=np.float32) * np.exp2(rng.integers(-12, 13, shape)).astype(np.float32)
    if cols: v *= np.repeat(np.exp2(rng.integers(-cols, cols + 1, shape[:-2] + (1, shape[-1] // 4))) * (rng.random(shape[:-2] + (1, shape[-1] // 4)) > 0.0625), 4, axis=-1).astype(np.float32)
    return mx_ref.flush(v.astype(BF))
C, H = 320, 96
DIST = [1, 2, 3]
def numbers_of(rng):
    return {"x": np.array(f(rng, N, 128, 4 * C)), "u": np.array(f(rng, N, 128, 512)), "v": np.array(f(rng, N, 128, 512))}
def changes(rng):
    return np.argsort(rng.random((N, 8, 8)), axis=2).astype(np.int32)
def layers(rng, still=[]):
    k = np.exp2(np.argsort(rng.random((N, 128, 1)), axis=1) % 5 - 6.0).astype(np.float32)
    w = np.array(mx_ref.flush((rng.standard_normal((N, 128, 2048), dtype=np.float32) * k).astype(BF))).reshape(N, 8, 16, 4, 8, 16, 4)
    for i in still:
        w[:, :, i] = 0
        w[:, :, :, :, :, i] = 0
    return w
def weights(rng, w):
    c, p = packed(np.ascontiguousarray(w).reshape(N, 128, 2048), rng)
    return {"wc": c, "ws": p}
def edges(rng, x):
    x = x.astype(np.float32).reshape(N, 8, 16, C, 4)
    k = (N, 8, 8, C, 4)
    a = (2 * rng.integers(64, 128, k) + 1) * np.exp2(-7.0 - rng.integers(8, 15, k)) * (rng.integers(0, 2, k) * 2.0 - 1.0)
    a[:, :, 0, :, 0] = 1.96875
    x[:, :, 8:] = a * np.exp2(rng.integers(-2, 3, (N, 8, 1, C, 1)))
    return x
def undecided(u):
    u = u.reshape(N, 128, 128, 4)
    u[:, :, ::16] = 0
    u[:, :, 1:4] = 0
    return u
def setup_inputs(rng):
    return {**numbers_of(rng), "ch": changes(rng), **weights(rng, layers(rng))}
def setup_inputs_ties(rng):
    d = numbers_of(rng)
    x = edges(rng, d["x"])
    k = rng.integers(-1, 2, (N, 8, C)).astype(np.float32)
    o = rng.permutation(N)
    k[o[0]] = 0
    k[o[1]] = rng.integers(0, 2, (8, 1)) * 2.0 - 1.0
    x[:, :, 0] = 0
    x[:, :, 0, :, 0] = k
    u = undecided(d["u"])
    for h in range(0, 128, 16): u[:, h, h, 0] = 1.0
    for b in range(3): u[:, 16 * b, 1 + b, 0] = 1.0
    return {"x": x.reshape(N, 128, 4 * C).astype(BF), "u": u.reshape(N, 128, 512), "v": d["v"], "ch": changes(rng), **weights(rng, layers(rng, [0]))}
def setup_inputs_near(rng):
    d = numbers_of(rng)
    x = d["x"].astype(np.float32).reshape(N, 8, 16, C, 4)
    s = rng.integers(0, 256, (N, 8, C))
    x[:, :, 0] = 0
    x[:, :, 8:] = 0
    x[:, :, 0, :, 0] = rng.integers(0, 2, (N, 8, C)) * 2.0 - 1.0
    for i in range(2): x[:, :, 8 + i] = ((s[:, :, :, None] >> (4 * i + np.arange(4))) & 1) * np.exp2(4.0 * i + np.arange(4) - 23.0)
    x[:, :, 11, :, 0] = 2.0 ** -10
    x[:, :, 12, :, :3] = rng.integers(-1, 2, (N, 8, C, 3)) * 2.0 ** -22
    o = rng.permutation(N) % 4
    x[o == 3, :, 8:] *= np.float32(2.0 ** -7)
    x[o == 3, :, 12:13] *= np.float32(0.5)
    u = undecided(d["u"])
    for r in range(N):
        k = 1.0 if o[r] == 0 else 2.0 ** -30
        for h in range(0, 128, 16):
            u[r, h + 8:h + 10, h] = k
            if o[r] < 2:
                u[r, h, h, 0] = k
                u[r, h + 11, h, 0] = k
        for b in range(3): u[r, 16 * b + 12, 1 + b, b] = k
    return {"x": x.reshape(N, 128, 4 * C).astype(BF), "u": u.reshape(N, 128, 512), "v": d["v"], "ch": changes(rng), **weights(rng, layers(rng, [0, 8, 9, 10, 11, 12, 13, 14, 15]))}
def setup_inputs_calls(rng):
    d = numbers_of(rng)
    x = edges(rng, d["x"])
    x[:, :, 0] = (-(1.0 + 0.125 * rng.permutation(N)) * 2.0 ** -6)[:, None, None, None]
    o = rng.permutation(N) % 2 * 2.0 - 1.0
    u = d["u"].reshape(N, 128, 128, 4)
    u[:, :, 1:4] = 0
    for r in range(N):
        for b in range(3): u[r, 16 * b, 1 + b, b] = float(o[r])
    return {"x": x.reshape(N, 128, 4 * C).astype(BF), "u": u.reshape(N, 128, 512), "v": d["v"], "ch": changes(rng), **weights(rng, layers(rng))}
def setup_inputs_ends(rng):
    d = numbers_of(rng)
    o = np.array([0, 2, 3, 1])[(np.arange(N) + rng.integers(4)) % 4]
    x = 2.0 ** 25 * (1.0 - 0.125 * rng.integers(0, 3, (N, 8, 16, C, 4)))
    x = np.where((o < 2)[:, None, None, None, None], x, 2.0 ** -30 * (1.0 + 0.125 * rng.integers(0, 8, (N, 1, 1, C, 1))))
    x[o == 1] *= rng.integers(0, 2, (1, 1, 1, C, 1)) * 2.0 - 1.0
    u = d["u"].astype(np.float32).reshape(N, 128, 128, 4)
    v = np.zeros((N, 128, 512), np.float32)
    w = np.zeros((N, 128, 4, 128, 4), np.float32)
    i, e = np.arange(128), np.arange(8)
    for r in range(N):
        a = 2.0 ** 30 if o[r] < 2 else 2.0 ** -30
        k = np.full((128, 8, 4), a)
        if o[r] < 2: k *= 1.0 - 0.125 * rng.integers(0, 3, (128, 8, 4))
        t = np.ones(8) if o[r] == 2 else rng.permutation(8) % 2 * 2.0 - 1.0
        u[r][:, ::16] = k * t[None, :, None]
        if o[r] > 1: u[r][:, 16 * rng.permutation(8)[:2]] = 0
        u[r][:, 1:4] = -a if o[r] == 3 else a
        v[r] = a * (rng.integers(0, 2, (128, 512)) * 2.0 - 1.0)
        if o[r] % 2 == 0: w[r] = 0.125
        else:
            for b in range(4): w[r, i, b, i, b] = 64.0 if o[r] == 1 else 2.0 ** -30
    ch = changes(rng)
    ch[o == 0] = (e + 1) % 8
    ch[o == 1] = e
    ch[o == 2] = 7 - e
    return {"x": x.astype(np.float32).reshape(N, 128, 4 * C).astype(BF), "u": u.reshape(N, 128, 512).astype(BF), "v": v.astype(BF), "ch": ch, **weights(rng, w.astype(BF))}
def setup_inputs_spread(rng):
    d = setup_inputs(rng)
    d["x"] = wide(rng, N, 128, 4 * C, cols=6)
    return d
def check_inputs(d):
    b = []
    for k, most in (("x", 2.0 ** 25), ("u", 2.0 ** 30), ("v", 2.0 ** 30)):
        a = np.abs(d[k].astype(np.float32))
        if not (np.isfinite(a).all() and ((a == 0) | (a >= 2.0 ** -30) & (a <= most)).all()): b.append("a value of " + k)
    if not (np.sort(d["ch"], axis=2) == np.arange(8)).all(): b.append("a row of ch")
    none, least, most = [emit(mx_ref.quantize(np.full((128, 16), k, np.float32).astype(BF)))[1][0, 0] for k in (0.0, 2.0 ** -30, 2.0 ** 30)]
    for r in range(N):
        if ((d["wc"][r] == 0x7F) | (d["wc"][r] == 0xFF)).any(): b.append("wc: a code that is no number")
        s = mx_ref.live(d["ws"][r])
        if ((s != none) & ((s < least) | (s > most))).any(): b.append("ws: a scale out of range")
        a = np.abs(decode(pk(d["wc"][r], d["ws"][r])).astype(np.float64)).reshape(128, 512, 4)
        if not (np.sum(a, axis=(0, 2)) <= 64).all(): b.append("sizes in a column of W")
    return b
def reference(x, u, v, ch, wc, ws):
    qu = [mx_ref.quantize(u[r]) for r in range(N)]
    lay = [pk(wc[r], ws[r]) for r in range(N)]
    now = [x[r] for r in range(N)]
    last = [None] * N
    for d in DIST:
        rung = []
        for r in range(N):
            q = mx_ref.quantize(now[r])
            s = mx_ref.matmul(qu[r], q) + np.float32(0.0)
            order = np.argsort(-s[::16], axis=1, kind="stable")
            a = ch[r][4 * (s[1] > 0) + 2 * (s[2] > 0) + (s[3] > 0)]
            row = np.array(a)
            for j in range(1, C): row[j] = row[j - 1][a[j]]
            h = np.ascontiguousarray(row.T)
            c = np.take_along_axis(order, h, axis=0)
            parts = decode(q).astype(BF).reshape(8, 16, C, 4)
            rung.append(np.ascontiguousarray(parts[h, :, c].transpose(0, 2, 1, 3)).reshape(128, 4 * C))
            last[r] = h
        sent = [mx_ref.quantize(np.ascontiguousarray(rung[r][:, :4 * H])) for r in range(N)]
        for r in range(N):
            came = sent[(r - d) % N]
            own = decode(came)
            first = tile([np.maximum(mx_ref.matmul(pick(lay[r], np.arange(128 * b, 128 * b + 128)), came), np.float32(0.0)) * np.float32(0.03125) + own[:, b::4] for b in range(4)])
            now[r] = np.concatenate([first, rung[r][:, 4 * H:]], axis=1)
    y, rw = np.zeros((N, 128, C), np.float32), np.zeros((N, 8, C), np.float32)
    oc, osc = np.zeros((N, 128, 4 * C), np.uint8), np.zeros((N, 16, C), np.uint8)
    for r in range(N):
        q = mx_ref.quantize(now[r])
        y[r] = mx_ref.matmul(mx_ref.quantize(v[r]), q)
        rw[r] = last[r]
        oc[r], osc[r] = emit(q)
    return {"y": y, "rw": rw, "oc": oc, "osc": osc}

@@ -1,0 +1,682 @@
+from concourse.mybir import dt, AluOpType, AxisListType, ActivationFunctionType
+
+STEP = 16384.0
+LOW = 4194304.0
+SLACK = 60.0
+CY = 0.83
+CHAIN = {"o": "s", "n": "x"}
+ROUNDS = 3
+NP = {"o": 224, "n": 96}
+ST = {"o": 8, "n": 4}
+F32, BF, I32, U16 = "float32", "bfloat16", "int32", "uint16"
+CODE, SC = "float8_e4m3fn_x4", "uint8"
+
+
+def _scratch():
+    d = {}
+
+    def sb(name, n, t=F32):
+        d[name] = ("sbuf", [128, n], t)
+
+    def mx(name, n):
+        sb(name + "c", n, CODE)
+        sb(name + "s", n, SC)
+    for b in range(8):
+        d["ps%d" % b] = ("psum", [128, 512], F32)
+    for n, w in (("xb", 1280), ("ub", 512), ("vb", 512), ("eb", 2048), ("mvb", 1536), ("zb", 512), ("ccb", 1024), ("xnb", 512), ("tb", 1280),
+                 ("win", 10240), ("sto", 1024), ("stn", 512), ("mao", 128), ("man", 128), ("mb", 128), ("go", 3584), ("gn", 2560), ("jk", 1280)):
+        sb(n, w, BF)
+    for n, w in (("uq", 128), ("ur", 128), ("vq", 128), ("eq", 512), ("mv", 384), ("zq", 128), ("wq", 512), ("cc", 256), ("sqo", 256), ("sqn", 128),
+                 ("gq", 896), ("gw", 448)):
+        mx(n, w)
+    for r in range(ROUNDS + 1):
+        mx("qt%d" % r, 320)
+        if r:
+            mx("ld%d" % r, 128)
+            mx("xn%d" % r, 128)
+    for n in ("pi", "gi", "ii", "e1", "e2", "e3", "e4", "i7i"):
+        sb(n, 1, I32)
+    for n in ("m16", "dr", "dl", "sd", "ob", "ol", "row", "rol", "ro4", "os1", "os2", "yb", "rwa", "rwb"):
+        sb(n, 320)
+    for n in ("chf", "m8", "k8", "d8", "cht", "chs", "t1"):
+        sb(n, 64)
+    for n, w in (("mk", 224), ("mg", 224), ("ml", 96), ("cf", 48), ("rl", 384), ("bt0", 3), ("bt1", 3), ("cn", 20), ("nn", 128), ("m64", 512),
+                 ("ones", 128), ("eye", 128), ("ulf", 8), ("clo", 8), ("chh", 8), ("rr", 224), ("rv", 224), ("acl", 6), ("aft", 14), ("cs", 14),
+                 ("rkc", 14), ("rko", 14), ("cl", 224), ("ow", 160), ("rxf", 20)):
+        sb(n, w)
+    sb("chi", 64, I32), sb("chb", 64, I32), sb("rwi", 320, I32)
+    for n, w in (("ul", 8), ("rlst", 14), ("rk16", 20), ("rx", 20), ("fl0", 20), ("fl1", 20), ("fl2", 20), ("fl3", 20)):
+        sb(n, w, U16)
+    for p, n in NP.items():
+        S, nc, st = n // 16, n // 32, ST[p]
+        for k, w in (("id", 16 * nc), ("xw", 256 * nc), ("tw", 16 * nc), ("tv", nc), ("lf", 16 * st), ("ac", 16 * st), ("ta", 16 * S + 16), ("cb", nc),
+                     ("f1f", S), ("lr", n), ("lw", n), ("zz", 224 if p == "o" else 192), ("ab", n), ("am", n), ("sx", n), ("so", n), ("sg", n)):
+            sb(k + p, w)
+        for k, w in (("ix", st), ("li", 16 * st), ("tl", 2 * nc), ("f1", S), ("ll", S)):
+            sb(k + p, w, U16)
+    return d
+
+
+def _pack(d):
+    place, at, rest = {}, {}, {}
+    for name, (where, shape, t) in d.items():
+        host = {F32: "kf", U16: "ku", I32: "ki"}.get(t)
+        if where != "sbuf" or host is None or name in ("chi", "ow", "yb", "rwb"):
+            rest[name] = (where, shape, t)
+            continue
+        place[name] = (host, at.get(host, 0))
+        at[host] = at.get(host, 0) + (shape[1] + 15) // 16 * 16
+    for host, t in (("kf", F32), ("ku", U16), ("ki", I32)):
+        rest[host] = ("sbuf", [128, at[host]], t)
+    return rest, place
+
+
+BUFS = _scratch()
+SCRATCH, PLACE = _pack(BUFS)
+SEMAPHORES = (["cv", "ct", "cs", "cg", "dx", "du", "dv", "dw", "dc", "zf", "out", "ls"]
+              + [k + "%d" % r for k in ("fo", "fn", "od") for r in range(3)] + ["rc%d" % r for r in range(1, 4)])
+
+
+def _make(g, T):
+    queues = {"v": g.vector, "t": g.tensor, "s": g.scalar, "g": g, "y": g.sync}
+    comp = {"v": "cv", "t": "ct", "s": "cs", "g": "cg"}
+    total, known, recs, jobs = {}, {q: {} for q in queues}, {}, []
+
+    def view(a):
+        n, lo, hi, st = a
+        return T[n][:, lo:hi] if st == 1 else T[n][:, lo:hi:st]
+
+    def span(a):
+        return (a[0], 0, 512, 1, True) if a[0][:2] == "ps" else (a[0], a[1], a[2], a[3], False)
+
+    def meet(lo, hi, st, x):
+        return x[0] < hi and lo < x[1] and not (st == x[2] and st > 1 and (lo - x[0]) % st)
+
+    def cover(lo, hi, st, x):
+        return lo <= x[0] and x[1] <= hi and (st == 1 or (st == x[2] and (lo - x[0]) % st == 0))
+
+    def wait(q, sem, val, clk):
+        k = known[q]
+        if k.get(sem, 0) >= val:
+            return
+        queues[q].wait_ge(T.sem[sem], int(val))
+        k[sem] = val
+        for s, x in clk.items():
+            if k.get(s, 0) < x:
+                k[s] = x
+
+    def need(q, reads, writes, sem, self_ok):
+        deps = []
+        for lst, isw in ((reads, False), (writes, True)):
+            for a in lst:
+                n, lo, hi, st, ps = span(a)
+                for x in recs.get(n, []):
+                    rw, rq, rsem = x[3], x[4], x[5]
+                    if not meet(lo, hi, st, x) or not (isw or rw or (ps and rq != q)):
+                        continue
+                    if rq == q == "t" and rw and isw:
+                        continue
+                    if rsem == sem and not self_ok:
+                        continue
+                    deps.append((rsem, x[6], x[7]))
+        deps.sort(key=lambda d: -sum(d[2].values()))
+        for s, v, c in deps:
+            wait(q, s, v if s in comp.values() else total[s], c)
+
+    def note(q, reads, writes, sem, val):
+        clk = dict(known[q])
+        for lst, isw in ((reads, False), (writes, True)):
+            for a in lst:
+                n, lo, hi, st, ps = span(a)
+                old = recs.get(n, [])
+                if isw:
+                    old = [x for x in old if not cover(lo, hi, st, x) or (x[5] == sem and sem not in comp.values())]
+                else:
+                    old = [x for x in old if not (not x[3] and x[4] == q and x[5] == sem and cover(lo, hi, st, x))]
+                recs[n] = old + [(lo, hi, st, isw, q, sem, val, clk)]
+
+    def put(q, reads, writes, fn):
+        sem = comp[q]
+        need(q, reads, writes, sem, True)
+        total[sem] = total.get(sem, 0) + 1
+        fn(queues[q]).then_inc(T.sem[sem], 1)
+        note(q, reads, writes, sem, total[sem])
+
+    def put_dma(q, sem, reads, writes, out, in_):
+        need(q, reads, writes, sem, False)
+        total[sem] = total.get(sem, 0) + 16
+        queues[q].dma_start(out, in_).then_inc(T.sem[sem], 16)
+        note(q, reads, writes, sem, total[sem])
+
+    def op(q, reads, writes, fn, cost=60.0):
+        jobs.append(dict(q=q, r=reads, w=writes, fn=fn, cost=cost, lat=0.0, sem=None))
+
+    def dma(q, sem, reads, writes, out, in_, lat=2000.0):
+        jobs.append(dict(q=q, r=reads, w=writes, fn=(out, in_), cost=60.0, lat=lat, sem=sem))
+
+    def raw(q, reads, writes, fn, cost, lat):
+        jobs.append(dict(q=q, r=reads, w=writes, fn=fn, cost=cost, lat=lat, sem="raw"))
+
+    def run():
+        table, groups, n = {}, {}, len(jobs)
+        for i, j in enumerate(jobs):
+            pre = set()
+            grp = j["sem"] if j["sem"] not in (None, "raw") else None
+            acc = [(span(a), False) for a in j["r"]] + [(span(a), True) for a in j["w"]]
+            for (nm, lo, hi, st, ps), isw in acc:
+                for x in table.get(nm, []):
+                    k = x[4]
+                    if k != i and meet(lo, hi, st, x) and (x[3] or isw or ps) and (grp is None or jobs[k]["sem"] != grp):
+                        pre.add(k)
+            for (nm, lo, hi, st, ps), isw in acc:
+                old = table.get(nm, [])
+                if isw and grp is None:
+                    old = [x for x in old if not cover(lo, hi, st, x)]
+                table[nm] = old + [(lo, hi, st, isw, i)]
+            for k in list(pre):
+                if jobs[k]["sem"] not in (None, "raw"):
+                    pre.update(groups[jobs[k]["sem"]])
+            pre.discard(i)
+            j["pre"] = pre
+            if grp:
+                groups.setdefault(grp, []).append(i)
+        after = [[] for _ in jobs]
+        for i, j in enumerate(jobs):
+            for k in j["pre"]:
+                after[k].append(i)
+        way = [0.0] * n
+        for i in range(n - 1, -1, -1):
+            way[i] = jobs[i]["cost"] + jobs[i]["lat"] + max([way[k] + 100.0 for k in after[i]] or [0.0])
+        free = {q: 0.0 for q in queues}
+        fin, qof, left = {}, {}, [len(j["pre"]) for j in jobs]
+        ready = [i for i in range(n) if not left[i]]
+        while ready:
+            best = None
+            for i in ready:
+                for q in (("v", "s") if jobs[i]["q"] == "x" else (jobs[i]["q"],)):
+                    t = 0.0
+                    for k in jobs[i]["pre"]:
+                        t = max(t, fin[k] + (80.0 if qof[k] == q else 150.0))
+                    key = (max(free[q], t - SLACK), -way[i], max(free[q], t))
+                    if best is None or key < best[0]:
+                        best = (key, i, q)
+            key, i, q = best
+            j = jobs[i]
+            ready.remove(i)
+            free[q] = key[2] + j["cost"]
+            fin[i] = free[q] + j["lat"]
+            qof[i] = q
+            if j["sem"] is None:
+                put(q, j["r"], j["w"], j["fn"])
+            elif j["sem"] == "raw":
+                j["fn"]()
+            else:
+                put_dma(q, j["sem"], j["r"], j["w"], j["fn"][0], j["fn"][1])
+            for k in after[i]:
+                left[k] -= 1
+                if not left[k]:
+                    ready.append(k)
+        jobs.clear()
+    return dict(view=view, wait=wait, need=need, op=op, dma=dma, raw=raw, run=run, total=total)
+
+
+def rank_program(g, core, T, topo):
+    rank = T.rank_of(core)
+    if rank is None:
+        return
+    K = _make(g, T)
+    view, op, dma, raw = K["view"], K["op"], K["dma"], K["raw"]
+    A, ACT = AluOpType, ActivationFunctionType
+
+    def B(n, lo=0, hi=None, st=1):
+        h, at = PLACE.get(n, (n, 0))
+        return (h, at + lo, at + (BUFS[n][1][1] if hi is None else hi), st)
+
+    def cf(j):
+        return B("cf", j, j + 1)
+
+    def ps(b, lo, hi):
+        return ("ps%d" % b, lo, hi, 1)
+
+    def width(a):
+        return (a[2] - a[1] + a[3] - 1) // a[3]
+
+    def small(a):
+        return SCRATCH[a[0]][2] in (BF, U16)
+
+    def vc(out, ins, two=False):
+        n = width(out)
+        if any(a[0] == "@" for a in ins):
+            return 50 + 1.5 * CY * n
+        if two and not any(a[0][:2] == "ps" for a in ins):
+            return max(64, 2 * n) * CY
+        return max(64, n * (0.5 if small(out) and all(small(a) for a in ins) else 1.0)) * CY
+
+    def acost(out, ins):
+        return (65 + 1.5 * CY * width(out)) if any(a[0] == "@" for a in ins) else 50 + CY * width(out)
+
+    def sc(x):
+        return (view(x), [x]) if isinstance(x, tuple) else (x, [])
+
+    def src(a):
+        if a[0] == "@":
+            return view(a[1]).indirect(view(a[2])), [a[1], a[2]]
+        return view(a), [a]
+
+    def ts(out, in0, s1, op0, s2=None, op1=None):
+        iv, ir = src(in0)
+        (x1, r1), (x2, r2) = sc(s1), sc(s2)
+
+        def vec(e):
+            if op1 is None:
+                return e.tensor_scalar(view(out), iv, x1, None, op0)
+            return e.tensor_scalar(view(out), iv, x1, x2, op0, op1)
+
+        def either(e):
+            if e is g.vector:
+                return vec(e)
+            m, a = (x1, 0.0 if op1 is None else x2) if op0 == A.mult else (1.0, x1)
+            return e.activation(view(out), iv, ACT.Identity, bias=a, scale=m)
+        plain = SCRATCH[out[0]][2] == F32 and SCRATCH[in0[0]][2] == F32 and (op0 == A.mult and op1 in (None, A.add) or op0 == A.add and op1 is None)
+        if plain:
+            op("x", ir + r1 + r2, [out], either, 10 + vc(out, [in0]))
+        else:
+            op("v", ir + r1 + r2, [out], vec, vc(out, [in0]))
+
+    def tt(out, in0, in1, o):
+        iv, ir = src(in0)
+        op("v", ir + [in1], [out], lambda e: e.tensor_tensor(view(out), iv, view(in1), o), vc(out, [in0, in1], True))
+
+    def cp(out, in_, q="v"):
+        iv, ir = src(in_)
+
+        def fn(e):
+            if e is g.vector:
+                return e.tensor_copy(view(out), iv)
+            return e.activation(view(out), iv, ACT.Copy)
+        op(q, ir, [out], fn, vc(out, [in_]) if q == "v" else acost(out, [in_]))
+
+    def lay(out, in_, col):
+        def fn(e):
+            if e is g.vector:
+                return e.tensor_scalar(view(out), view(in_), view(col), None, A.mult)
+            return e.activation(view(out), view(in_), ACT.Copy, scale=view(col))
+        op("x", [in_, col], [out], fn, 90.0)
+
+    def scan(out, d0, d1, o0, o1):
+        op("v", [d0, d1], [out], lambda e: e.tensor_tensor_scan(view(out), view(d0), view(d1), 0.0, o0, o1), CY * width(out))
+
+    def latch(out, d1):
+        scan(out, B("dl", 0, width(d1)), d1, A.add, A.max)
+
+    def fill(out, x):
+        op("v", [], [out], lambda e: e.memset(view(out), x), vc(out, []))
+
+    def iota(out, pat, base=0, cm=0):
+        if SCRATCH[out[0]][2] == I32:
+            op("g", [], [out], lambda e: e.iota(view(out), pat, base, cm), 150.0)
+        else:
+            op("g", [], [out], lambda e: e.iota(view(out), pat, base, cm, allow_small_or_imprecise_dtypes=True), 130 + 2 * CY * width(out))
+
+    def quant(name, lo, hi, tile, tlo):
+        t = (tile, tlo, tlo + 4 * (hi - lo), 1)
+        c, s = (name + "c", lo, hi, 1), (name + "s", lo, hi, 1)
+        op("v", [t], [c, s], lambda e: e.quantize_mx(view(c), view(s), view(t)), 12 + 0.88 * (hi - lo))
+
+    def mm(bank, n, w, wlo, x, xlo, start=True, stop=True):
+        lc, ls = (w + "c", wlo, wlo + 128, 1), (w + "s", wlo, wlo + 128, 1)
+        rc, rs = (x + "c", xlo, xlo + n, 1), (x + "s", xlo, xlo + n, 1)
+        o = ps(bank, 0, n)
+        op("t", [lc, ls, rc, rs], [o], lambda e: e.matmul_mx(view(o), view(lc), view(ls), view(rc), view(rs), start, stop), 0.6 * (n + 16))
+
+    dma("y", "dx", [], [B("xb")], view(B("xb")), T.x[:, :])
+    dma("s", "du", [], [B("ub")], view(B("ub")), T.u[:, :])
+    dma("y", "dc", [], [B("chi")], T.chi[0:1, 0:64], T.ch[:, :])
+    dma("y", "dv", [], [B("vb")], view(B("vb")), T.v[:, :])
+    dma("y", "dw", [], [B("wqc")], T.wqc[:, 0:512].bitcast(dt.uint8), T.wc[:, :])
+    dma("y", "dw", [], [B("wqs")], view(B("wqs")), T.ws[:, :])
+
+    iota(B("pi"), [[1, 1]], 0, 1)
+    iota(B("ulf"), [[16, 8]])
+    iota(B("m16"), [[0, 20], [1, 16]])
+    iota(B("nn"), [[1, 128]])
+    fill(B("eb"), 0.0)
+    fill(B("ones"), 1.0)
+    op("g", [B("ones")], [B("eye")], lambda e: e.affine_select(view(B("eye")), view(B("ones")), [[-1, 128]], A.is_equal, 0.0, 0, 1), 400.0)
+    cp(B("ul"), B("ulf"))
+    quant("uq", 0, 128, "ub", 0)
+    quant("qt0", 0, 320, "xb", 0)
+    op("v", [B("uqc"), B("ul")], [B("urc")], lambda e: e.tensor_copy(T.urc[:, 0:128].bitcast(dt.uint32), T.uqc[:, 0:128].bitcast(dt.uint32).indirect(view(B("ul")))), 210.0)
+    op("v", [B("uqs"), B("ul")], [B("urs")], lambda e: e.tensor_copy(T.urs[:, 0:128], T.uqs[:, 0:128].indirect(view(B("ul")))), 210.0)
+    for b in range(4):
+        cp(B("eb", 512 * b + b, 512 * (b + 1), 4), B("eye"), "x")
+    quant("eq", 0, 512, "eb", 0)
+    ts(B("gi"), B("pi"), 4, A.arith_shift_right)
+    ts(B("ii"), B("pi"), 15, A.bitwise_and)
+    ts(B("e1"), B("ii"), 1, A.bitwise_and)
+    ts(B("e2"), B("ii"), 3, A.bitwise_and)
+    ts(B("e3"), B("ii"), 1, A.arith_shift_right)
+    ts(B("e4"), B("ii"), 2, A.arith_shift_right)
+    ts(B("i7i"), B("ii"), 7, A.bitwise_and)
+    G_, I_, E1, E2, E3, E4, I7, CORR, NCORR, H8, H88 = (cf(j) for j in range(11))
+    for j, n in enumerate(("gi", "ii", "e1", "e2", "e3", "e4", "i7i")):
+        cp(cf(j), B(n))
+    ts(CORR, I_, -STEP, A.mult, 15.0 * STEP, A.add)
+    ts(NCORR, CORR, -1.0, A.mult)
+    for b in range(4):
+        ts(cf(40 + b), NCORR, float(b), A.add)
+    ts(H8, I_, 8.0, A.is_ge)
+    ts(H88, H8, 8.0, A.mult)
+    ts(B("mk"), B("m16", 0, 224), I_, A.is_equal)
+    ts(B("ml"), B("m16", 0, 96), I_, A.is_lt)
+    ts(B("mg"), B("m16", 0, 224), I_, A.is_gt)
+    ts(B("dr"), B("m16"), 0.0, A.is_gt)
+    t0, t1, t2, t3, t4, t5, RN, RA, RB, FN, FA = (cf(j) for j in range(11, 22))
+    ts(t0, G_, 3.0, A.is_ge)
+    ts(FN, t0, -7.0, A.mult, 8.0, A.add)
+    ts(t0, t0, -3.0, A.mult, G_, A.add)
+    ts(t1, E2, 4.0, A.mult, t0, A.add)
+    ts(t2, G_, 6.0, A.is_ge, 100.0, A.mult)
+    tt(RN, t1, t2, A.add)
+    ts(t3, G_, 7.0, A.is_ge)
+    ts(FA, t3, -7.0, A.mult, 8.0, A.add)
+    ts(t3, t3, -7.0, A.mult, G_, A.add)
+    ts(RA, E1, 8.0, A.mult, t3, A.add)
+    ts(t4, E1, 8.0, A.mult, G_, A.add)
+    ts(t5, G_, 2.0, A.is_lt, 100.0, A.mult)
+    ts(t4, t4, -1.0, A.add)
+    tt(RB, t4, t5, A.add)
+    for n, r in (("mao", RA), ("mb", RB), ("man", RN)):
+        ts(B(n), B("m16", 0, 128), r, A.is_equal)
+    fill(B("mvb"), 0.0)
+    fill(B("sto", 3, 1024, 4), 0.0)
+    fill(B("stn", 3, 512, 4), 0.0)
+    for t, w in enumerate((4.0, 2.0, 1.0)):
+        ts(cf(22 + t), FN, w, A.mult)
+        ts(cf(25 + t), FA, w, A.mult)
+        ts(B("mvb", t, 32, 4), B("nn", 0, 8), E3, A.is_equal, cf(25 + t), A.mult)
+        ts(B("mvb", 512 + t, 544, 4), B("nn", 0, 8), E4, A.is_equal, cf(22 + t), A.mult)
+        ts(B("mvb", 1024 + t, 1056, 4), B("nn", 0, 8), E3, A.is_equal, w, A.mult)
+    quant("mv", 0, 384, "mvb", 0)
+    ts(B("dl"), B("m16"), I_, A.is_gt, LOW + STEP, A.mult)
+    ts(B("dl"), B("dl"), -LOW, A.add)
+    iota(B("m64"), [[1, 8], [0, 64]])
+    ts(B("ccb", 0, 512), B("m64"), G_, A.is_equal)
+    ts(B("ccb", 512, 1024), B("m64"), G_, A.is_equal, -1.0, A.mult)
+    quant("cc", 0, 256, "ccb", 0)
+    fill(B("zb"), 0.0)
+    for q in range(4):
+        fill(B("go", 896 * q + 4 * min(64 * q, 96), 896 * q + 4 * min(64 * q + 64, 224)), 0.0)
+        if q:
+            quant("gq", 224 * q, 224 * q + 128, "zb", 0)
+    for t in (2, 3):
+        fill(B("gn", 1280 + t, 2560, 4), 0.0)
+    fill(B("aft"), 0.0)
+    iota(B("cs"), [[16, 14]], -304)
+    ts(B("cs"), B("cs"), CORR, A.add)
+    op("g", [B("chi")], [B("chb")], lambda e: e.partition_broadcast(view(B("chb")), T.chi[0:1, 0:64], 128), 350.0)
+    iota(B("m8"), [[0, 8], [1, 8]])
+    cp(B("chf"), B("chb"))
+    ts(B("k8"), B("m8"), I7, A.is_equal)
+    ts(B("d8"), B("m8"), 0.0, A.is_gt)
+    tt(B("cht"), B("chf"), B("k8"), A.mult)
+    scan(B("chs"), B("d8"), B("cht"), A.mult, A.add)
+    CHV = B("chs", 7, 64, 8)
+    ts(B("chh"), CHV, H8, A.mult)
+    tt(B("clo"), CHV, B("chh"), A.subtract)
+    for a in range(8):
+        ts(B("t1", 8 * a, 8 * a + 8), B("chh"), B("clo", a, a + 1), A.add)
+    iota(B("tao", 0, 16), [[0, 2], [1, 8]])
+    for p in NP:
+        nc, j = NP[p] // 32, 28 + 3 * "on".index(p)
+        iota(B("id" + p), [[16, nc], [16 * nc + 8, 2], [1, 8]])
+        iota(B("id" + p, 8, 16), [[1, 8]], 16 * nc)
+        iota(B("ac" + p), [[0, 16], [16, ST[p]]])
+        ts(B("ac" + p), B("ac" + p), H88, A.add)
+        iota(B("f1f" + p), [[8, 2], [16, nc]])
+        ts(cf(j), I_, 16.0 * nc, A.mult, G_, A.add)
+        ts(B("f1" + p), B("f1f" + p), cf(j), A.add)
+        iota(B("cb" + p), [[16, nc]])
+        ts(cf(j + 1), H8, 16.0 * nc + 8, A.mult, CORR, A.add)
+        ts(cf(j + 2), H8, 16.0 * nc, A.mult, CORR, A.add)
+        ts(B("cb" + p, 1, nc), B("cb" + p, 1, nc), cf(j + 1), A.add)
+        ts(B("cb" + p, 0, 1), B("cb" + p, 0, 1), cf(j + 2), A.add)
+    TI = B("tan", 0, 16)
+    iota(TI, [[0, 2], [1, 8]])
+    ts(TI, TI, G_, A.subtract)
+    ts(B("rxf", 0, 16), TI, 0.0, A.is_lt, 8.0, A.mult)
+    tt(TI, TI, B("rxf", 0, 16), A.add)
+    ts(TI, TI, 20.0, A.mult)
+    iota(B("sd"), [[4, 320]])
+    ts(B("sd"), B("sd"), NCORR, A.add)
+    iota(B("cn"), [[-1, 20]])
+    ts(B("cn"), B("cn"), CORR, A.add)
+    fill(B("xnb", 384, 512), 0.0)
+    quant("zq", 0, 128, "zb", 0)
+    for r in range(1, ROUNDS + 1):
+        dma("y", "zf", [B("zqc", 0, 32)], [B("ld%dc" % r, 96, 128)], T["ld%dc" % r][:, 96:128].bitcast(dt.uint8), T.zqc[:, 0:32].bitcast(dt.uint8))
+        dma("y", "zf", [B("zqs", 0, 32)], [B("ld%ds" % r, 96, 128)], T["ld%ds" % r][:, 96:128], T.zqs[:, 0:32])
+    quant("vq", 0, 128, "vb", 0)
+
+    def products(p, x, xlo):
+        n = 224 if p == "o" else 128
+        mm(0, n, "ur", 0, x, xlo)
+        mm(1, n, "ur", 0, x, xlo)
+        mm(2, 128, x, xlo, "uq", 0)
+        if p == "o":
+            mm(7, 128, x, xlo + 96, "uq", 0)
+
+    def calls(p):
+        s = "st" + p
+        for b, m, o in [(2, "ma" + p, 0)] + ([(7, "mb", 512)] if p == "o" else []):
+            bits = "bt%d" % (o // 512)
+            ts(B(bits), ps(b, 1, 4), 0.0, A.is_gt)
+            for t in range(3):
+                lay(B(s, o + t, o + 512, 4), B(m), B(bits, t, t + 1))
+        if p == "o":
+            quant("sqo", 0, 256, s, 0)
+            mm(2, 128, "sqo", 0, "mv", 0, True, False)
+            mm(2, 128, "sqo", 128, "mv", 256, False, True)
+        else:
+            quant("sqn", 0, 128, s, 0)
+            mm(2, 128, "sqn", 0, "mv", 128)
+        cp(B("ix" + p), ps(2, 0, ST[p]))
+        tt(B("lf" + p), ("@", B("t1"), B("ix" + p)), B("ac" + p), A.add)
+        cp(B("li" + p), B("lf" + p))
+
+    def pieces(p):
+        nc, st, n = NP[p] // 32, ST[p], NP[p]
+        w = 16 * nc
+        for e in range(16):
+            b = B("id" + p) if e == 0 else B("xw" + p, w * e - w, w * e)
+            cp(B("xw" + p, w * e, w * e + w), ("@", b, B("li" + p, st * e, st * e + nc)), CHAIN[p])
+        latch(B("tw" + p), B("xw" + p, 15 * w, 16 * w))
+        tt(B("tv" + p), B("tw" + p, 15, w, 16), B("cb" + p), A.subtract)
+        cp(B("tl" + p, 0, 2 * nc, 2), B("tv" + p))
+        for s in range(2 * nc):
+            b, j = 16 * s + (8 if s > nc else 0), 2 * (s % nc)
+            cp(B("ta" + p, 16 * s + 16, 16 * s + 32), ("@", B("ta" + p, b, b + 8), B("tl" + p, j, j + 1)), CHAIN[p])
+        cp(B("lr" + p), ("@", B("xw" + p), B("f1" + p)), "x")
+        latch(B("lw" + p), B("lr" + p))
+        ts(B("ll" + p), B("lw" + p, 15, n, 16), CORR, A.subtract)
+
+    def rows_own():
+        pieces("o")
+        cp(B("rr"), ("@", B("tao"), B("llo")), "x")
+        latch(B("rv"), B("rr"))
+        ts(B("rlst"), B("rv", 15, 224, 16), CORR, A.subtract)
+
+    def rows_new():
+        pieces("n")
+        cp(B("row", 0, 96), ("@", B("tan"), B("lln")), "x")
+        cp(B("row", 96, 320), ("@", B("tan", 104, 112), B("rlst")), "x")
+        latch(B("rol"), B("row"))
+        tt(B("rxf"), B("rol", 15, 320, 16), B("cn"), A.subtract)
+        cp(B("rx"), B("rxf"))
+        ts(B("ro4"), B("row"), 64.0, A.mult)
+
+    def scores(p):
+        n = NP[p]
+        tt(B("sx" + p), ps(0, 0, n), B("mk", 0, n), A.mult)
+        scan(B("so" + p), B("dr", 0, n), B("sx" + p), A.mult, A.add)
+        ab, z = B("ab" + p), "zz" + p
+        op("s", [ps(1, 0, n)], [ab], lambda e: e.activation(view(ab), view(ps(1, 0, n)), ACT.Abs, bias=2.0 ** -120, scale=0.6 * 2.0 ** -23), acost(ab, []))
+        cp(B(z, 0, n), ps(1, 0, n), "s")
+        if p == "n":
+            tt(B(z, 96, 192), ps(0, 0, n), ab, A.add)
+        tt(B("am" + p), ab, B("ml" if p == "n" else "mg", 0, n), A.mult)
+        tt(B("sg" + p), ps(0, 0, n), B("am" + p), A.add if p == "n" else A.subtract)
+
+    def parts_out(p, x, xlo):
+        c0, n = (96, 224) if p == "o" else (0, 96)
+        for b in range(4):
+            mm(4 + b, max(n, 128), "eq", 128 * b, x, xlo)
+        for b in range(4):
+            cp(B("win", 4 * c0 + b, 4 * (c0 + n), 4), ps(4 + b, 0, n), "x")
+
+    def turn(p, r):
+        lo, hi = (384, 1280) if p == "o" else (0, 384)
+        for s in range(1, 8):
+            o = 1280 * s
+            for d0, d1, s0 in ((0, 128 - 16 * s, 16 * s), (128 - 16 * s, 128, 0)):
+                dma("y", "f%s%d" % (p, r), [("win", lo, hi, 1)], [("win", o + lo, o + hi, 1)], T.win[d0:d1, o + lo:o + hi], T.win[s0:s0 + d1 - d0, lo:hi], 14000.0 if p == "o" else 9000.0)
+
+    turns = []
+
+    def count(i, acc):
+        n = 320 * (len(turns) % 4)
+        turns.append(0)
+        j = B("jk", n, n + width(i))
+
+        def fn(e):
+            if e is g.vector:
+                return e.tensor_reduce(view(acc), view(i), AxisListType.X, A.add)
+            return e.activation(view(j), view(i), ACT.Copy, accum_out=view(acc))
+        op("x", [i], [j, acc], fn, 20 + acost(j, []))
+
+    def compare_own():
+        for k in range(14):
+            own = B("soo", 16 * k + 15, 16 * k + 16)
+            o = 896 * (k // 4) + k % 4
+            for z, lo, hi, f in (("sgo", 16 * k, 16 * k + 16, A.is_lt), ("zzo", 16 * k + 16, 224, A.is_le)):
+                if lo < hi:
+                    ts(B("go", o + 4 * lo, o - k % 4 + 4 * hi, 4), B(z, lo, hi), own, f)
+            if k < 13:
+                count(B("go", o + 4 * (16 * k + 16), o - k % 4 + 896, 4), B("aft", k, k + 1))
+        for q in range(4):
+            lo = min(64 * q, 96)
+            quant("gq", 224 * q + lo, 224 * q + 224, "go", 896 * q + 4 * lo)
+            mm(3, 224, "cc", 0, "gq", 224 * q, q == 0, False)
+
+    def compare_new():
+        for k in range(6):
+            own = B("son", 16 * k + 15, 16 * k + 16)
+            q, t = divmod(k, 4)
+            o = 1280 * q
+            ts(B("gn", o + t, o + 896, 4), B("zzo"), own, A.is_gt)
+            ts(B("gn", o + 896 + t, o + 1216, 4), B("zzn", 16 * k + 16, 96 + 16 * k), own, A.is_gt)
+            ts(B("gn", o + 1216 + t, o + 1280, 4), B("sgn", 16 * k, 16 * k + 16), own, A.is_gt)
+            count(B("gn", o + t, o + 1280, 4), B("acl", k, k + 1))
+        for q in range(2):
+            quant("gw", 224 * q, 224 * q + 224, "gn", 1280 * q)
+            mm(3, 224, "cc", 128, "gw", 224 * q, False, q == 1)
+
+    def early(r):
+        x = "qt%d" % r
+        products("o", x, 96)
+        calls("o")
+        scores("o")
+        parts_out("o", x, 96)
+        turn("o", r)
+        compare_own()
+        rows_own()
+
+    def late(r, x):
+        products("n", x, 0)
+        calls("n")
+        scores("n")
+        parts_out("n", x, 0)
+        turn("n", r)
+        compare_new()
+        cp(B("rk16", 0, 6), B("acl"))
+        tt(B("rkc"), B("aft"), B("cs"), A.add)
+        latch(B("cl"), ps(3, 0, 224))
+        tt(B("rko"), B("cl", 15, 224, 16), B("rkc"), A.subtract)
+        cp(B("rk16", 6, 20), B("rko"))
+        op("v", [B("rk16"), B("sd")], [B("ob")], lambda e: e.tensor_copy(view(B("ob")).indirect(view(B("rk16"))), view(B("sd"))), 50 + 3.3 * CY * 320)
+        latch(B("ol"), B("ob"))
+        cp(B("ow", 0, 20), B("ol", 15, 320, 16))
+        for s in range(1, 8):
+            for d0, d1, s0 in ((0, 128 - 16 * s, 16 * s), (128 - 16 * s, 128, 0)):
+                dma("y" if s % 2 else "s", "od%d" % r, [B("ow", 0, 20)], [B("ow", 20 * s, 20 * s + 20)], T.ow[d0:d1, 20 * s:20 * s + 20], T.ow[s0:s0 + d1 - d0, 0:20], 3500.0)
+        rows_new()
+        tt(B("os1"), ("@", B("ow"), B("rx")), B("ro4"), A.add)
+        latch(B("os2"), B("os1"))
+        for b in range(4):
+            ts(B("fl%d" % b), B("os2", 15, 320, 16), cf(40 + b), A.add)
+        t = "qt%d" % (r + 1)
+        for (l0, l1) in ((0, 8), (8, 20)):
+            for b in range(4):
+                cp(B("tb", 64 * l0 + b, 64 * l1, 4), ("@", B("win"), B("fl%d" % b, l0, l1)), "x")
+            quant(t, 16 * l0, 16 * l1, "tb", 64 * l0)
+            if l0 == 0:
+                send(r + 1)
+
+    def send(r):
+        t = "qt%d" % r
+        dst = T.cores[(rank + r) % len(T.cores)]
+        rid, pid = topo.addr(dst)[:2]
+        m = topo.mask(core, dst)
+
+        def fn():
+            K["need"]("g", [B(t + "c", 0, 96), B(t + "s", 0, 96)], [], "ls", True)
+            for k in "cs":
+                o, i = T["ld%d%s" % (r, k)][:, 0:96], T[t + k][:, 0:96]
+                if k == "c":
+                    o, i = o.bitcast(dt.uint8), i.bitcast(dt.uint8)
+                g.remote_dma(o, i, T.sem["rc%d" % r], T.sem["ls"], pid, rid, m)
+                K["total"]["ls"] = K["total"].get("ls", 0) + len(topo.engines(core, dst))
+        raw("g", [B(t + "c", 0, 96), B(t + "s", 0, 96)], [("sent%d" % r, 0, 1, 1)], fn, 600.0, 2000.0)
+
+    def arrive(r):
+        frm = T.cores[(rank - r) % len(T.cores)]
+        n = 2 * len(topo.engines(frm, core))
+        raw("t", [("sent%d" % r, 0, 1, 1)], [B("ld%dc" % r, 0, 96), B("ld%ds" % r, 0, 96)], lambda: K["wait"]("t", "rc%d" % r, n, {}), 1.0, 0.0)
+        for b in range(4):
+            a = (0, 1, 2, 0)[b]
+            mm(4 + b, 128, "wq", 128 * b, "ld%d" % r, 0)
+            mm(a, 128, "eq", 128 * b, "ld%d" % r, 0)
+            o, i = B("rl", 96 * b, 96 * b + 96), ps(4 + b, 0, 96)
+            op("s", [i], [o], lambda e, o=o, i=i: e.activation(view(o), view(i), ACT.Relu, scale=0.03125), acost(o, []))
+            tt(B("xnb", b, 384, 4), o, ps(a, 0, 96), A.add)
+        quant("xn%d" % r, 0, 128, "xnb", 0)
+
+    early(0)
+    late(0, "qt0")
+    for r in (1, 2):
+        early(r)
+        arrive(r)
+        late(r, "xn%d" % r)
+    x = "qt3"
+    mm(3, 224, "vq", 0, x, 96)
+    cp(B("yb", 96, 320), ps(3, 0, 224), "s")
+    ts(B("rwa"), B("row"), 0.05, A.mult, G_, A.add)
+    cp(B("rwi"), B("rwa"))
+    ts(B("rwa"), B("rwi"), 7.5, A.is_ge, -8.0, A.mult)
+    tt(B("rwb"), B("rwa"), B("rwi"), A.add)
+    dma("y", "out", [B(x + "c", 96, 320)], [], T.oc[:, 384:1280], T[x + "c"][:, 96:320].bitcast(dt.uint8))
+    for k in range(4):
+        dma("y", "out", [B(x + "s", 96, 320)], [], T.osc[4 * k:4 * k + 4, 96:320], T[x + "s"][32 * k:32 * k + 4, 96:320])
+    dma("y", "out", [B("yb", 96, 320)], [], T.y[:, 96:320], T.yb[:, 96:320])
+    dma("s", "out", [B("rwb")], [], T.rw[:, :], T.rwb[0:128:16, :])
+    arrive(3)
+    x = "xn3"
+    mm(3, 128, "vq", 0, x, 0)
+    cp(B("yb", 0, 96), ps(3, 0, 96), "s")
+    dma("s", "out", [B(x + "c", 0, 96)], [], T.oc[:, 0:384], T[x + "c"][:, 0:96].bitcast(dt.uint8))
+    for k in range(4):
+        dma("s" if k % 2 else "y", "out", [B(x + "s", 0, 96)], [], T.osc[4 * k:4 * k + 4, 0:96], T[x + "s"][32 * k:32 * k + 4, 0:96])
+    dma("y", "out", [B("yb", 0, 96)], [], T.y[:, 0:96], T.yb[:, 0:96])
+    K["run"]()
+    for sem, n in sorted(K["total"].items()):
+        K["wait"]("g", sem, n, {})

@@ -1,15 +1,16 @@
 from concourse.mybir import dt, AluOpType, AxisListType, ActivationFunctionType
 
-STEP = 16384.0
-LOW = 4194304.0
-SLACK = 60.0
 CY = 0.83
-CHAIN = {"o": "s", "n": "x"}
+SLACK = 60.0
+HOP, SELF = 130.0, 80.0
 ROUNDS = 3
-NP = {"o": 224, "n": 96}
-ST = {"o": 8, "n": 4}
+STEP, LOW = 512.0, 16384.0
+STEP8, LOW8 = 8.0, 256.0
+BIG = 16384.0
 F32, BF, I32, U16 = "float32", "bfloat16", "int32", "uint16"
 CODE, SC = "float8_e4m3fn_x4", "uint8"
+GO = ((0, 96), (896, 160), (1536, 192))
+GN = ((0, 0), (1280, 64))
 
 
 def _scratch():
@@ -23,58 +24,52 @@ def _scratch():
         sb(name + "s", n, SC)
     for b in range(8):
         d["ps%d" % b] = ("psum", [128, 512], F32)
-    for n, w in (("xb", 1280), ("ub", 512), ("vb", 512), ("eb", 2048), ("mvb", 1536), ("zb", 512), ("ccb", 1024), ("xnb", 512), ("tb", 1280),
-                 ("win", 10240), ("sto", 1024), ("stn", 512), ("mao", 128), ("man", 128), ("mb", 128), ("go", 3584), ("gn", 2560), ("jk", 1280)):
+    for n, w in (("xb", 1280), ("ub", 512), ("vb", 512), ("eb", 2048), ("lb", 2048), ("zb", 768), ("ccb", 512), ("cab", 1024), ("one", 512),
+                 ("bt", 520), ("eye", 32), ("i32b", 32), ("ta", 512), ("tb", 1280), ("st", 1280), ("win", 3840), ("go", 2048), ("gn", 2304), ("jk", 1280),
+                 ("m64", 512), ("ico", 256)):
         sb(n, w, BF)
-    for n, w in (("uq", 128), ("ur", 128), ("vq", 128), ("eq", 512), ("mv", 384), ("zq", 128), ("wq", 512), ("cc", 256), ("sqo", 256), ("sqn", 128),
-                 ("gq", 896), ("gw", 448)):
+    for n, w in (("uq", 128), ("ur", 128), ("vq", 128), ("eq", 512), ("lq", 512), ("zq", 192), ("wq", 512), ("cc", 128), ("ca", 256), ("bqo", 128),
+                 ("bqn", 128), ("gq", 1600)):
         mx(n, w)
     for r in range(ROUNDS + 1):
-        mx("qt%d" % r, 320)
+        mx("qx%d" % r, 320)
         if r:
             mx("ld%d" % r, 128)
-            mx("xn%d" % r, 128)
-    for n in ("pi", "gi", "ii", "e1", "e2", "e3", "e4", "i7i"):
-        sb(n, 1, I32)
-    for n in ("m16", "dr", "dl", "sd", "ob", "ol", "row", "rol", "ro4", "os1", "os2", "yb", "rwa", "rwb"):
-        sb(n, 320)
-    for n in ("chf", "m8", "k8", "d8", "cht", "chs", "t1"):
-        sb(n, 64)
-    for n, w in (("mk", 224), ("mg", 224), ("ml", 96), ("cf", 48), ("rl", 384), ("bt0", 3), ("bt1", 3), ("cn", 20), ("nn", 128), ("m64", 512),
-                 ("ones", 128), ("eye", 128), ("ulf", 8), ("clo", 8), ("chh", 8), ("rr", 224), ("rv", 224), ("acl", 6), ("aft", 14), ("cs", 14),
-                 ("rkc", 14), ("rko", 14), ("cl", 224), ("ow", 160), ("rxf", 20)):
+            mx("qs%d" % r, 128)
+    sb("pi", 1, I32), sb("bi", 11, I32), sb("chi", 64, I32), sb("chb", 64, I32)
+    for n, w in (("cf", 48), ("ulf", 8), ("i32", 10), ("llf", 16), ("cm", 20), ("oc0", 160), ("dlf", 320), ("yc", 224), ("d0", 224), ("chf", 64), ("m8", 64),
+                 ("k8", 64), ("d8", 64), ("cht", 64), ("chs", 64), ("yo", 224), ("soo", 224), ("yn", 96), ("son", 96), ("acl", 20), ("rc1", 20), ("rc2", 20),
+                 ("cl", 320), ("rkf", 20), ("ot", 160), ("sc", 640), ("rl", 384), ("yb", 320), ("rw1", 128), ("rw2", 128), ("rwb", 128)):
         sb(n, w)
-    sb("chi", 64, I32), sb("chb", 64, I32), sb("rwi", 320, I32)
-    for n, w in (("ul", 8), ("rlst", 14), ("rk16", 20), ("rx", 20), ("fl0", 20), ("fl1", 20), ("fl2", 20), ("fl3", 20)):
+    for n, w in (("bm16", 320), ("dr", 224), ("dlb", 256), ("sd", 320), ("ob", 352), ("tr", 672), ("dcs", 320), ("tf", 1024), ("tl", 1024), ("tab", 64),
+                 ("xo", 272), ("xn", 144), ("ppo", 32), ("ppn", 32), ("too", 32), ("ton", 32), ("opf", 128), ("pfn", 128), ("xg", 16), ("xl", 16),
+                 ("zo", 256), ("zn", 128), ("wo", 256), ("wn", 128), ("rf", 384), ("rt", 384), ("rr", 128), ("mk", 1024), ("rwt", 128)):
+        sb(n, w, BF + "*")
+    for n, w in (("ul", 8), ("otl", 10), ("rll", 8), ("ptl", 1), ("ll", 16), ("hl", 1), ("p4", 2), ("lt", 8), ("ixo", 1), ("ixn", 1), ("lio", 32), ("lin", 32),
+                 ("lpo", 32), ("lpn", 32), ("lx", 1), ("fl", 24), ("rk", 20), ("il", 80)):
         sb(n, w, U16)
-    for p, n in NP.items():
-        S, nc, st = n // 16, n // 32, ST[p]
-        for k, w in (("id", 16 * nc), ("xw", 256 * nc), ("tw", 16 * nc), ("tv", nc), ("lf", 16 * st), ("ac", 16 * st), ("ta", 16 * S + 16), ("cb", nc),
-                     ("f1f", S), ("lr", n), ("lw", n), ("zz", 224 if p == "o" else 192), ("ab", n), ("am", n), ("sx", n), ("so", n), ("sg", n)):
-            sb(k + p, w)
-        for k, w in (("ix", st), ("li", 16 * st), ("tl", 2 * nc), ("f1", S), ("ll", S)):
-            sb(k + p, w, U16)
     return d
 
 
 def _pack(d):
     place, at, rest = {}, {}, {}
+    hosts = {F32: "kf", U16: "ku", I32: "ki", BF + "*": "kb"}
     for name, (where, shape, t) in d.items():
-        host = {F32: "kf", U16: "ku", I32: "ki"}.get(t)
-        if where != "sbuf" or host is None or name in ("chi", "ow", "yb", "rwb"):
+        host = hosts.get(t)
+        if where != "sbuf" or host is None or name in ("chi", "yb", "rwb"):
             rest[name] = (where, shape, t)
             continue
         place[name] = (host, at.get(host, 0))
         at[host] = at.get(host, 0) + (shape[1] + 15) // 16 * 16
-    for host, t in (("kf", F32), ("ku", U16), ("ki", I32)):
-        rest[host] = ("sbuf", [128, at[host]], t)
+    for t, host in hosts.items():
+        rest[host] = ("sbuf", [128, at[host]], t.strip("*"))
     return rest, place
 
 
 BUFS = _scratch()
 SCRATCH, PLACE = _pack(BUFS)
-SEMAPHORES = (["cv", "ct", "cs", "cg", "dx", "du", "dv", "dw", "dc", "zf", "out", "ls"]
-              + [k + "%d" % r for k in ("fo", "fn", "od") for r in range(3)] + ["rc%d" % r for r in range(1, 4)])
+SEMAPHORES = (["cv", "ct", "cs", "cg", "dx", "du", "dv", "dw", "dc", "z1", "z2", "z3", "z4", "z5", "zw", "out", "ls"]
+              + ["sw%d" % r for r in range(3)] + ["rc%d" % r for r in range(1, 4)])
 
 
 def _make(g, T):
@@ -83,17 +78,19 @@ def _make(g, T):
     total, known, recs, jobs = {}, {q: {} for q in queues}, {}, []
 
     def view(a):
-        n, lo, hi, st = a
-        return T[n][:, lo:hi] if st == 1 else T[n][:, lo:hi:st]
+        n, lo, hi, st, p0, p1 = a
+        p = slice(None) if (p0, p1) == (0, 128) else slice(p0, p1)
+        return T[n][p, lo:hi] if st == 1 else T[n][p, lo:hi:st]
 
     def span(a):
-        return (a[0], 0, 512, 1, True) if a[0][:2] == "ps" else (a[0], a[1], a[2], a[3], False)
+        return (a[0], 0, 512, 1, 0, 128) if a[0][:2] == "ps" else a
 
-    def meet(lo, hi, st, x):
-        return x[0] < hi and lo < x[1] and not (st == x[2] and st > 1 and (lo - x[0]) % st)
+    def meet(a, x):
+        return (x[1] < a[2] and a[1] < x[2] and x[4] < a[5] and a[4] < x[5]
+                and not (a[3] > 1 and x[3] > 1 and (a[1] - x[1]) % min(a[3], x[3]) and max(a[3], x[3]) % min(a[3], x[3]) == 0))
 
-    def cover(lo, hi, st, x):
-        return lo <= x[0] and x[1] <= hi and (st == 1 or (st == x[2] and (lo - x[0]) % st == 0))
+    def cover(a, x):
+        return a[1] <= x[1] and x[2] <= a[2] and a[4] <= x[4] and x[5] <= a[5] and (a[3] == 1 or (x[3] % a[3] == 0 and (a[1] - x[1]) % a[3] == 0))
 
     def wait(q, sem, val, clk):
         k = known[q]
@@ -109,16 +106,16 @@ def _make(g, T):
         deps = []
         for lst, isw in ((reads, False), (writes, True)):
             for a in lst:
-                n, lo, hi, st, ps = span(a)
-                for x in recs.get(n, []):
-                    rw, rq, rsem = x[3], x[4], x[5]
-                    if not meet(lo, hi, st, x) or not (isw or rw or (ps and rq != q)):
+                a = span(a)
+                ps = a[0][:2] == "ps"
+                for x, rw, rq, rsem, val, clk in recs.get(a[0], []):
+                    if not meet(a, x) or not (isw or rw or (ps and rq != q)):
                         continue
                     if rq == q == "t" and rw and isw:
                         continue
                     if rsem == sem and not self_ok:
                         continue
-                    deps.append((rsem, x[6], x[7]))
+                    deps.append((rsem, val, clk))
         deps.sort(key=lambda d: -sum(d[2].values()))
         for s, v, c in deps:
             wait(q, s, v if s in comp.values() else total[s], c)
@@ -127,13 +124,13 @@ def _make(g, T):
         clk = dict(known[q])
         for lst, isw in ((reads, False), (writes, True)):
             for a in lst:
-                n, lo, hi, st, ps = span(a)
-                old = recs.get(n, [])
+                a = span(a)
+                old = recs.get(a[0], [])
                 if isw:
-                    old = [x for x in old if not cover(lo, hi, st, x) or (x[5] == sem and sem not in comp.values())]
+                    old = [x for x in old if not cover(a, x[0]) or (x[3] == sem and sem not in comp.values())]
                 else:
-                    old = [x for x in old if not (not x[3] and x[4] == q and x[5] == sem and cover(lo, hi, st, x))]
-                recs[n] = old + [(lo, hi, st, isw, q, sem, val, clk)]
+                    old = [x for x in old if not (not x[1] and x[2] == q and x[3] == sem and cover(a, x[0]))]
+                recs[a[0]] = old + [(a, isw, q, sem, val, clk)]
 
     def put(q, reads, writes, fn):
         sem = comp[q]
@@ -148,14 +145,14 @@ def _make(g, T):
         queues[q].dma_start(out, in_).then_inc(T.sem[sem], 16)
         note(q, reads, writes, sem, total[sem])
 
-    def op(q, reads, writes, fn, cost=60.0):
-        jobs.append(dict(q=q, r=reads, w=writes, fn=fn, cost=cost, lat=0.0, sem=None))
+    def op(cost, reads, writes, fn):
+        jobs.append(dict(c=cost, r=reads, w=writes, fn=fn, lat=0.0, sem=None))
 
     def dma(q, sem, reads, writes, out, in_, lat=2000.0):
-        jobs.append(dict(q=q, r=reads, w=writes, fn=(out, in_), cost=60.0, lat=lat, sem=sem))
+        jobs.append(dict(c={q: 60.0}, r=reads, w=writes, fn=(out, in_), lat=lat, sem=sem))
 
     def raw(q, reads, writes, fn, cost, lat):
-        jobs.append(dict(q=q, r=reads, w=writes, fn=fn, cost=cost, lat=lat, sem="raw"))
+        jobs.append(dict(c={q: cost}, r=reads, w=writes, fn=fn, lat=lat, sem="raw"))
 
     def run():
         table, groups, n = {}, {}, len(jobs)
@@ -163,16 +160,15 @@ def _make(g, T):
             pre = set()
             grp = j["sem"] if j["sem"] not in (None, "raw") else None
             acc = [(span(a), False) for a in j["r"]] + [(span(a), True) for a in j["w"]]
-            for (nm, lo, hi, st, ps), isw in acc:
-                for x in table.get(nm, []):
-                    k = x[4]
-                    if k != i and meet(lo, hi, st, x) and (x[3] or isw or ps) and (grp is None or jobs[k]["sem"] != grp):
+            for a, isw in acc:
+                for x, xw, k in table.get(a[0], []):
+                    if k != i and meet(a, x) and (xw or isw or a[0][:2] == "ps") and (grp is None or jobs[k]["sem"] != grp):
                         pre.add(k)
-            for (nm, lo, hi, st, ps), isw in acc:
-                old = table.get(nm, [])
+            for a, isw in acc:
+                old = table.get(a[0], [])
                 if isw and grp is None:
-                    old = [x for x in old if not cover(lo, hi, st, x)]
-                table[nm] = old + [(lo, hi, st, isw, i)]
+                    old = [x for x in old if not cover(a, x[0])]
+                table[a[0]] = old + [(a, isw, i)]
             for k in list(pre):
                 if jobs[k]["sem"] not in (None, "raw"):
                     pre.update(groups[jobs[k]["sem"]])
@@ -186,24 +182,32 @@ def _make(g, T):
                 after[k].append(i)
         way = [0.0] * n
         for i in range(n - 1, -1, -1):
-            way[i] = jobs[i]["cost"] + jobs[i]["lat"] + max([way[k] + 100.0 for k in after[i]] or [0.0])
+            way[i] = min(jobs[i]["c"].values()) + jobs[i]["lat"] + max([way[k] + 100.0 for k in after[i]] or [0.0])
         free = {q: 0.0 for q in queues}
         fin, qof, left = {}, {}, [len(j["pre"]) for j in jobs]
         ready = [i for i in range(n) if not left[i]]
+
+        def start(i, q):
+            t = 0.0
+            for k in jobs[i]["pre"]:
+                t = max(t, fin[k] + (SELF if qof[k] == q else HOP))
+            return t
         while ready:
             best = None
             for i in ready:
-                for q in (("v", "s") if jobs[i]["q"] == "x" else (jobs[i]["q"],)):
-                    t = 0.0
-                    for k in jobs[i]["pre"]:
-                        t = max(t, fin[k] + (80.0 if qof[k] == q else 150.0))
-                    key = (max(free[q], t - SLACK), -way[i], max(free[q], t))
+                c = jobs[i]["c"]
+                ends = {q: max(free[q], start(i, q)) + c[q] for q in c}
+                for q in c:
+                    if ends[q] > min(ends.values()) + WORSE * c[q]:
+                        continue
+                    t = start(i, q)
+                    key = (max(free[q], t - SLACK), -way[i], ends[q])
                     if best is None or key < best[0]:
                         best = (key, i, q)
             key, i, q = best
             j = jobs[i]
             ready.remove(i)
-            free[q] = key[2] + j["cost"]
+            free[q] = key[2]
             fin[i] = free[q] + j["lat"]
             qof[i] = q
             if j["sem"] is None:
@@ -220,6 +224,10 @@ def _make(g, T):
     return dict(view=view, wait=wait, need=need, op=op, dma=dma, raw=raw, run=run, total=total)
 
 
+WORSE = 0.5
+PIN = {"chain": "s", "count": "s", "shift": "vs", "lay": "vs", "win": "vs", "pick": "vs", "mask": "vs", "rows": "vs"}
+
+
 def rank_program(g, core, T, topo):
     rank = T.rank_of(core)
     if rank is None:
@@ -228,21 +236,21 @@ def rank_program(g, core, T, topo):
     view, op, dma, raw = K["view"], K["op"], K["dma"], K["raw"]
     A, ACT = AluOpType, ActivationFunctionType
 
-    def B(n, lo=0, hi=None, st=1):
+    def B(n, lo=0, hi=None, st=1, p=(0, 128)):
         h, at = PLACE.get(n, (n, 0))
-        return (h, at + lo, at + (BUFS[n][1][1] if hi is None else hi), st)
+        return (h, at + lo, at + (BUFS[n][1][1] if hi is None else hi), st, p[0], p[1])
 
     def cf(j):
         return B("cf", j, j + 1)
 
     def ps(b, lo, hi):
-        return ("ps%d" % b, lo, hi, 1)
+        return ("ps%d" % b, lo, hi, 1, 0, 128)
 
     def width(a):
         return (a[2] - a[1] + a[3] - 1) // a[3]
 
-    def small(a):
-        return SCRATCH[a[0]][2] in (BF, U16)
+    def kind(a):
+        return SCRATCH[a[1][0] if a[0] == "@" else a[0]][2]
 
     def vc(out, ins, two=False):
         n = width(out)
@@ -250,10 +258,13 @@ def rank_program(g, core, T, topo):
             return 50 + 1.5 * CY * n
         if two and not any(a[0][:2] == "ps" for a in ins):
             return max(64, 2 * n) * CY
-        return max(64, n * (0.5 if small(out) and all(small(a) for a in ins) else 1.0)) * CY
+        return max(64, n * (0.5 if all(kind(a) in (BF, U16) for a in [out] + ins) else 1.0)) * CY
 
-    def acost(out, ins):
-        return (65 + 1.5 * CY * width(out)) if any(a[0] == "@" for a in ins) else 50 + CY * width(out)
+    def ac(out, ins):
+        return (65 + 1.5 * CY * width(out)) if any(a[0] == "@" for a in ins) else 60 + CY * width(out)
+
+    def costs(qs, out, ins):
+        return {q: vc(out, ins) if q == "v" else ac(out, ins) for q in qs}
 
     def sc(x):
         return (view(x), [x]) if isinstance(x, tuple) else (x, [])
@@ -263,283 +274,251 @@ def rank_program(g, core, T, topo):
             return view(a[1]).indirect(view(a[2])), [a[1], a[2]]
         return view(a), [a]
 
-    def ts(out, in0, s1, op0, s2=None, op1=None):
+    def ts(out, in0, s1, op0, s2=None, op1=None, qs="vs"):
         iv, ir = src(in0)
         (x1, r1), (x2, r2) = sc(s1), sc(s2)
 
-        def vec(e):
-            if op1 is None:
-                return e.tensor_scalar(view(out), iv, x1, None, op0)
-            return e.tensor_scalar(view(out), iv, x1, x2, op0, op1)
-
-        def either(e):
+        def fn(e):
             if e is g.vector:
-                return vec(e)
+                if op1 is None:
+                    return e.tensor_scalar(view(out), iv, x1, None, op0)
+                return e.tensor_scalar(view(out), iv, x1, x2, op0, op1)
             m, a = (x1, 0.0 if op1 is None else x2) if op0 == A.mult else (1.0, x1)
             return e.activation(view(out), iv, ACT.Identity, bias=a, scale=m)
-        plain = SCRATCH[out[0]][2] == F32 and SCRATCH[in0[0]][2] == F32 and (op0 == A.mult and op1 in (None, A.add) or op0 == A.add and op1 is None)
-        if plain:
-            op("x", ir + r1 + r2, [out], either, 10 + vc(out, [in0]))
-        else:
-            op("v", ir + r1 + r2, [out], vec, vc(out, [in0]))
+        plain = kind(out) in (F32, BF) and kind(in0) in (F32, BF) and (op0 == A.mult and op1 in (None, A.add) or op0 == A.add and op1 is None)
+        op(costs(qs if plain else "v", out, [in0]), ir + r1 + r2, [out], fn)
 
     def tt(out, in0, in1, o):
         iv, ir = src(in0)
-        op("v", ir + [in1], [out], lambda e: e.tensor_tensor(view(out), iv, view(in1), o), vc(out, [in0, in1], True))
+        op({"v": vc(out, [in0, in1], True)}, ir + [in1], [out], lambda e: e.tensor_tensor(view(out), iv, view(in1), o))
 
-    def cp(out, in_, q="v"):
+    def cp(out, in_, qs="vs"):
         iv, ir = src(in_)
 
         def fn(e):
             if e is g.vector:
                 return e.tensor_copy(view(out), iv)
             return e.activation(view(out), iv, ACT.Copy)
-        op(q, ir, [out], fn, vc(out, [in_]) if q == "v" else acost(out, [in_]))
-
-    def lay(out, in_, col):
-        def fn(e):
-            if e is g.vector:
-                return e.tensor_scalar(view(out), view(in_), view(col), None, A.mult)
-            return e.activation(view(out), view(in_), ACT.Copy, scale=view(col))
-        op("x", [in_, col], [out], fn, 90.0)
+        op(costs(qs if kind(out) in (F32, BF) and kind(in_) in (F32, BF) else "v", out, [in_]), ir, [out], fn)
 
     def scan(out, d0, d1, o0, o1):
-        op("v", [d0, d1], [out], lambda e: e.tensor_tensor_scan(view(out), view(d0), view(d1), 0.0, o0, o1), CY * width(out))
+        op({"v": vc(out, [d0, d1])}, [d0, d1], [out], lambda e: e.tensor_tensor_scan(view(out), view(d0), view(d1), 0.0, o0, o1))
 
-    def latch(out, d1):
-        scan(out, B("dl", 0, width(d1)), d1, A.add, A.max)
+    def latch(out, d1, d="dlb"):
+        scan(out, B(d, 0, width(d1)), d1, A.add, A.max)
+
+    def turn(out, in_):
+        op({"v": vc(out, [in_])}, [in_], [out], lambda e: e.transpose(view(out), view(in_)))
+
+    def share(n, w):
+        for a, b in (((0, 64), (64, 128)), ((64, 128), (0, 64))):
+            cp(B(n, 8, w, 16, a), B(n, 0, w, 16, b), PIN["shift"])
+        for k in range(4):
+            k1 = (k + 1) % 4
+            cp(B(n, 4, w, 8, (32 * k, 32 * k + 32)), B(n, 0, w, 8, (32 * k1, 32 * k1 + 32)), PIN["shift"])
 
     def fill(out, x):
-        op("v", [], [out], lambda e: e.memset(view(out), x), vc(out, []))
+        op({"v": vc(out, [])}, [], [out], lambda e: e.memset(view(out), x))
 
     def iota(out, pat, base=0, cm=0):
-        if SCRATCH[out[0]][2] == I32:
-            op("g", [], [out], lambda e: e.iota(view(out), pat, base, cm), 150.0)
+        if kind(out) == I32:
+            op({"g": 140.0}, [], [out], lambda e: e.iota(view(out), pat, base, cm))
         else:
-            op("g", [], [out], lambda e: e.iota(view(out), pat, base, cm, allow_small_or_imprecise_dtypes=True), 130 + 2 * CY * width(out))
+            op({"g": 130 + 2 * CY * width(out)}, [], [out], lambda e: e.iota(view(out), pat, base, cm, allow_small_or_imprecise_dtypes=True))
+
+    def ones_where(out, base):
+        n = width(out)
+        op({"g": 170 + 2 * CY * n}, [B("one", 0, n)], [out], lambda e: e.affine_select(view(out), view(B("one", 0, n)), [[-1, n]], A.is_equal, 0.0, base, 1))
 
     def quant(name, lo, hi, tile, tlo):
-        t = (tile, tlo, tlo + 4 * (hi - lo), 1)
-        c, s = (name + "c", lo, hi, 1), (name + "s", lo, hi, 1)
-        op("v", [t], [c, s], lambda e: e.quantize_mx(view(c), view(s), view(t)), 12 + 0.88 * (hi - lo))
+        t, c, s = B(tile, tlo, tlo + 4 * (hi - lo)), B(name + "c", lo, hi), B(name + "s", lo, hi)
+        op({"v": 12 + 0.88 * (hi - lo)}, [t], [c, s], lambda e: e.quantize_mx(view(c), view(s), view(t)))
 
     def mm(bank, n, w, wlo, x, xlo, start=True, stop=True):
-        lc, ls = (w + "c", wlo, wlo + 128, 1), (w + "s", wlo, wlo + 128, 1)
-        rc, rs = (x + "c", xlo, xlo + n, 1), (x + "s", xlo, xlo + n, 1)
+        lc, ls, rc, rs = B(w + "c", wlo, wlo + 128), B(w + "s", wlo, wlo + 128), B(x + "c", xlo, xlo + n), B(x + "s", xlo, xlo + n)
         o = ps(bank, 0, n)
-        op("t", [lc, ls, rc, rs], [o], lambda e: e.matmul_mx(view(o), view(lc), view(ls), view(rc), view(rs), start, stop), 0.6 * (n + 16))
+        op({"t": 0.6 * (n + 16)}, [lc, ls, rc, rs], [o], lambda e: e.matmul_mx(view(o), view(lc), view(ls), view(rc), view(rs), start, stop))
 
-    dma("y", "dx", [], [B("xb")], view(B("xb")), T.x[:, :])
-    dma("s", "du", [], [B("ub")], view(B("ub")), T.u[:, :])
-    dma("y", "dc", [], [B("chi")], T.chi[0:1, 0:64], T.ch[:, :])
+    def zeros(q, sem, n, lo, hi):
+        dma(q, sem, [B("zb", 0, hi - lo)], [B(n, lo, hi)], view(B(n, lo, hi)), view(B("zb", 0, hi - lo)))
+
+    def zero_codes(q, sem, n, lo, hi):
+        dma(q, sem, [B("zqc", 0, hi - lo)], [B(n + "c", lo, hi)], view(B(n + "c", lo, hi)).bitcast(dt.uint8), view(B("zqc", 0, hi - lo)).bitcast(dt.uint8))
+        dma(q, sem, [B("zqs", 0, hi - lo)], [B(n + "s", lo, hi)], view(B(n + "s", lo, hi)), view(B("zqs", 0, hi - lo)))
+
+    dma("y", "dx", [], [B("xb")], view(B("xb")), T.x[:, :], 3800.0)
+    dma("s", "du", [], [B("ub")], view(B("ub")), T.u[:, :], 2600.0)
+    dma("y", "dc", [], [B("chi")], T.chi[0:1, 0:64], T.ch[:, :], 2200.0)
+    fill(B("zb"), 0.0)
+    quant("zq", 0, 192, "zb", 0)
+    for lo, hi in ((0, 96), (320, 480), (640, 832), (1280, 1344)):
+        zero_codes("y", "z4", "gq", lo, hi)
+    for lo in range(0, 2048, 768):
+        cp(B("lb", lo, min(lo + 768, 2048)), B("zb", 0, min(768, 2048 - lo)), "s")
+    for a in (B("go", 0, 192), B("go", 896, 1088), B("go", 1536, 1856), B("gn", 0, 192), B("gn", 384, 1152, 4), B("gn", 1280, 1408), B("gn", 1283, 2240, 4),
+              B("ta", 384, 512), B("bt")):
+        fill(a, 0.0)
+    for r in range(1, ROUNDS + 1):
+        zero_codes("y", "z5", "ld%d" % r, 96, 128)
+    for h in range(8):
+        o = B("win", 2560 * (h % 2), 2560 * (h % 2) + 1280, 1, (16 * h, 16 * h + 16))
+        dma("y", "zw", [B("zqc")], [o], view(o), T.x[16 * h:16 * h + 16, :])
     dma("y", "dv", [], [B("vb")], view(B("vb")), T.v[:, :])
     dma("y", "dw", [], [B("wqc")], T.wqc[:, 0:512].bitcast(dt.uint8), T.wc[:, :])
     dma("y", "dw", [], [B("wqs")], view(B("wqs")), T.ws[:, :])
 
     iota(B("pi"), [[1, 1]], 0, 1)
     iota(B("ulf"), [[16, 8]])
-    iota(B("m16"), [[0, 20], [1, 16]])
-    iota(B("nn"), [[1, 128]])
-    fill(B("eb"), 0.0)
-    fill(B("ones"), 1.0)
-    op("g", [B("ones")], [B("eye")], lambda e: e.affine_select(view(B("eye")), view(B("ones")), [[-1, 128]], A.is_equal, 0.0, 0, 1), 400.0)
+    iota(B("bm16"), [[0, 20], [1, 16]])
+    fill(B("one"), 1.0)
     cp(B("ul"), B("ulf"))
     quant("uq", 0, 128, "ub", 0)
-    quant("qt0", 0, 320, "xb", 0)
-    op("v", [B("uqc"), B("ul")], [B("urc")], lambda e: e.tensor_copy(T.urc[:, 0:128].bitcast(dt.uint32), T.uqc[:, 0:128].bitcast(dt.uint32).indirect(view(B("ul")))), 210.0)
-    op("v", [B("uqs"), B("ul")], [B("urs")], lambda e: e.tensor_copy(T.urs[:, 0:128], T.uqs[:, 0:128].indirect(view(B("ul")))), 210.0)
-    for b in range(4):
-        cp(B("eb", 512 * b + b, 512 * (b + 1), 4), B("eye"), "x")
-    quant("eq", 0, 512, "eb", 0)
-    ts(B("gi"), B("pi"), 4, A.arith_shift_right)
-    ts(B("ii"), B("pi"), 15, A.bitwise_and)
-    ts(B("e1"), B("ii"), 1, A.bitwise_and)
-    ts(B("e2"), B("ii"), 3, A.bitwise_and)
-    ts(B("e3"), B("ii"), 1, A.arith_shift_right)
-    ts(B("e4"), B("ii"), 2, A.arith_shift_right)
-    ts(B("i7i"), B("ii"), 7, A.bitwise_and)
-    G_, I_, E1, E2, E3, E4, I7, CORR, NCORR, H8, H88 = (cf(j) for j in range(11))
-    for j, n in enumerate(("gi", "ii", "e1", "e2", "e3", "e4", "i7i")):
-        cp(cf(j), B(n))
-    ts(CORR, I_, -STEP, A.mult, 15.0 * STEP, A.add)
-    ts(NCORR, CORR, -1.0, A.mult)
-    for b in range(4):
-        ts(cf(40 + b), NCORR, float(b), A.add)
-    ts(H8, I_, 8.0, A.is_ge)
-    ts(H88, H8, 8.0, A.mult)
-    ts(B("mk"), B("m16", 0, 224), I_, A.is_equal)
-    ts(B("ml"), B("m16", 0, 96), I_, A.is_lt)
-    ts(B("mg"), B("m16", 0, 224), I_, A.is_gt)
-    ts(B("dr"), B("m16"), 0.0, A.is_gt)
-    t0, t1, t2, t3, t4, t5, RN, RA, RB, FN, FA = (cf(j) for j in range(11, 22))
-    ts(t0, G_, 3.0, A.is_ge)
-    ts(FN, t0, -7.0, A.mult, 8.0, A.add)
-    ts(t0, t0, -3.0, A.mult, G_, A.add)
-    ts(t1, E2, 4.0, A.mult, t0, A.add)
-    ts(t2, G_, 6.0, A.is_ge, 100.0, A.mult)
-    tt(RN, t1, t2, A.add)
-    ts(t3, G_, 7.0, A.is_ge)
-    ts(FA, t3, -7.0, A.mult, 8.0, A.add)
-    ts(t3, t3, -7.0, A.mult, G_, A.add)
-    ts(RA, E1, 8.0, A.mult, t3, A.add)
-    ts(t4, E1, 8.0, A.mult, G_, A.add)
-    ts(t5, G_, 2.0, A.is_lt, 100.0, A.mult)
-    ts(t4, t4, -1.0, A.add)
-    tt(RB, t4, t5, A.add)
-    for n, r in (("mao", RA), ("mb", RB), ("man", RN)):
-        ts(B(n), B("m16", 0, 128), r, A.is_equal)
-    fill(B("mvb"), 0.0)
-    fill(B("sto", 3, 1024, 4), 0.0)
-    fill(B("stn", 3, 512, 4), 0.0)
-    for t, w in enumerate((4.0, 2.0, 1.0)):
-        ts(cf(22 + t), FN, w, A.mult)
-        ts(cf(25 + t), FA, w, A.mult)
-        ts(B("mvb", t, 32, 4), B("nn", 0, 8), E3, A.is_equal, cf(25 + t), A.mult)
-        ts(B("mvb", 512 + t, 544, 4), B("nn", 0, 8), E4, A.is_equal, cf(22 + t), A.mult)
-        ts(B("mvb", 1024 + t, 1056, 4), B("nn", 0, 8), E3, A.is_equal, w, A.mult)
-    quant("mv", 0, 384, "mvb", 0)
-    ts(B("dl"), B("m16"), I_, A.is_gt, LOW + STEP, A.mult)
-    ts(B("dl"), B("dl"), -LOW, A.add)
+    quant("qx0", 0, 320, "xb", 0)
+    op({"v": 210.0}, [B("uqc"), B("ul")], [B("urc")], lambda e: e.tensor_copy(T.urc[:, 0:128].bitcast(dt.uint32), T.uqc[:, 0:128].bitcast(dt.uint32).indirect(view(B("ul")))))
+    op({"s": 225.0}, [B("uqs"), B("ul")], [B("urs")], lambda e: e.activation(T.urs[:, 0:128], T.uqs[:, 0:128].indirect(view(B("ul"))), ACT.Copy))
+    for j, (s, m) in enumerate(((5, 3), (4, 1), (3, 1), (2, 1), (0, 3), (0, 15), (0, 7), (1, 63), (0, 1), (4, 7), (1, 3))):
+        ts(B("bi", j, j + 1), B("pi"), s, A.arith_shift_right, m, A.bitwise_and)
+    cp(B("cf", 0, 11), B("bi"))
+    KQ, HB, MI, S2, K0, I_, V_, PH, O_, G_, K1 = (cf(j) for j in range(11))
+    NB, HP, C8, CF_, N3, F1, FO, W8, VL, FN, FW = (cf(j) for j in range(11, 22))
+    t = [cf(j) for j in range(22, 40)]
+    ts(B("yc"), B("bm16", 0, 224), I_, A.subtract, -1e28, A.mult)
+    ts(B("d0"), B("bm16", 0, 224), I_, A.is_le, -9e29, A.mult)
+    ts(B("dr"), B("bm16", 0, 224), 0.0, A.is_gt)
+    ts(B("dlb"), B("bm16", 0, 256), I_, A.is_gt, LOW8 + STEP8, A.mult)
+    ts(B("dlb"), B("dlb"), -LOW8, A.add)
+    ts(B("dlf"), B("bm16"), I_, A.is_gt, LOW + STEP, A.mult)
+    ts(B("dlf"), B("dlf"), -LOW, A.add)
+    ts(NB, HB, -1.0, A.mult, 1.0, A.add)
+    ts(HP, HB, 4.0, A.mult, KQ, A.add)
+    ts(C8, I_, STEP8, A.mult, -15.0 * STEP8, A.add)
+    ts(CF_, I_, STEP + 1.0, A.mult, -15.0 * STEP, A.add)
+    for k, s, o, j in ((K0, S2, N3, 0), (K1, MI, t[8], 3)):
+        ts(t[j], k, KQ, A.subtract, 4.0, A.mult)
+        ts(t[j + 1], k, KQ, A.is_lt, 16.0, A.mult)
+        ts(t[j + 2], s, 16.0, A.mult, t[j], A.add)
+        ts(o, t[j + 2], t[j + 1], A.add)
+    ts(t[9], O_, 128.0, A.mult, 128.0, A.add)
+    ts(F1, t[9], t[8], A.add)
+    ts(t[10], MI, HB, A.not_equal, 320.0, A.mult)
+    ts(t[11], MI, HB, A.is_gt, 32.0, A.mult)
+    ts(FO, N3, t[10], A.add, t[11], A.add)
+    iota(B("i32"), [[32, 10]])
+    ts(B("otl"), B("i32"), FO, A.add)
+    ts(B("rll", 0, 8, 2), B("i32", 0, 4), N3, A.add)
+    ts(B("rll", 1, 8, 2), B("i32", 0, 4), F1, A.add)
+    cp(B("ptl"), N3)
+    iota(B("llf"), [[128, 2], [1, 8]])
+    ts(t[12], I_, 8.0, A.mult)
+    ts(B("ll"), B("llf"), t[12], A.add)
+    ts(B("hl"), HP, 16.0, A.mult, I_, A.add)
+    ts(t[13], V_, 8.0, A.add)
+    ts(B("p4"), B("i32", 0, 2), 0.0, A.mult, t[13], A.add)
+    ts(FN, HP, 16.0, A.mult, C8, A.add)
+    ts(FW, C8, 112.0, A.add)
+    iota(B("cm"), [[16, 20]])
+    ts(B("cm"), B("cm"), CF_, A.add)
+    iota(B("oc0"), [[0, 20], [320, 8]], 1440)
+    ts(t[14], HB, -1280.0, A.mult)
+    ts(B("oc0"), B("oc0"), t[14], A.add)
+    iota(B("sd"), [[1, 320]], -160)
+    fill(B("ob"), 0.0)
+    fill(B("mk", 0, 1024, 8), BIG)
+    fill(B("acl"), 0.0)
+    for n in ("xo", "xn", "opf"):
+        iota(B(n, 0, 16), [[0, 2], [1, 8]])
+    iota(B("opf", 112, 128), [[0, 2], [1, 8]])
+    iota(B("pfn", 0, 16), [[0, 2], [1, 4], [4, 2]])
+    iota(B("ico", 0, 128), [[16, 4], [16, 2], [1, 16]])
+    iota(B("ico", 128, 256), [[8, 4], [32, 2], [1, 16]])
+    ts(W8, O_, -7.0, A.mult, 8.0, A.add)
+    fill(B("cab", 3, 1024, 4), 0.0)
+    for j, w in enumerate((4.0, 2.0, 1.0)):
+        ts(t[15 + j], W8, w, A.mult)
+        ts(B("cab", j, 1024, 4), B("ico"), PH, A.is_equal, t[15 + j], A.mult)
+    quant("ca", 0, 256, "cab", 0)
     iota(B("m64"), [[1, 8], [0, 64]])
-    ts(B("ccb", 0, 512), B("m64"), G_, A.is_equal)
-    ts(B("ccb", 512, 1024), B("m64"), G_, A.is_equal, -1.0, A.mult)
-    quant("cc", 0, 256, "ccb", 0)
-    fill(B("zb"), 0.0)
-    for q in range(4):
-        fill(B("go", 896 * q + 4 * min(64 * q, 96), 896 * q + 4 * min(64 * q + 64, 224)), 0.0)
-        if q:
-            quant("gq", 224 * q, 224 * q + 128, "zb", 0)
-    for t in (2, 3):
-        fill(B("gn", 1280 + t, 2560, 4), 0.0)
-    fill(B("aft"), 0.0)
-    iota(B("cs"), [[16, 14]], -304)
-    ts(B("cs"), B("cs"), CORR, A.add)
-    op("g", [B("chi")], [B("chb")], lambda e: e.partition_broadcast(view(B("chb")), T.chi[0:1, 0:64], 128), 350.0)
+    ts(B("ccb"), B("m64"), G_, A.is_equal, -1.0, A.mult)
+    quant("cc", 0, 128, "ccb", 0)
+    op({"g": 350.0}, [B("chi")], [B("chb")], lambda e: e.partition_broadcast(view(B("chb")), T.chi[0:1, 0:64], 128))
     iota(B("m8"), [[0, 8], [1, 8]])
     cp(B("chf"), B("chb"))
-    ts(B("k8"), B("m8"), I7, A.is_equal)
+    ts(B("k8"), B("m8"), V_, A.is_equal)
     ts(B("d8"), B("m8"), 0.0, A.is_gt)
     tt(B("cht"), B("chf"), B("k8"), A.mult)
     scan(B("chs"), B("d8"), B("cht"), A.mult, A.add)
-    CHV = B("chs", 7, 64, 8)
-    ts(B("chh"), CHV, H8, A.mult)
-    tt(B("clo"), CHV, B("chh"), A.subtract)
+    ts(t[6], MI, -1.0, A.mult, 1.0, A.add)
+    ts(VL, V_, t[6], A.mult)
+    ts(B("lt"), B("chs", 7, 64, 8), MI, A.mult, VL, A.add)
     for a in range(8):
-        ts(B("t1", 8 * a, 8 * a + 8), B("chh"), B("clo", a, a + 1), A.add)
-    iota(B("tao", 0, 16), [[0, 2], [1, 8]])
-    for p in NP:
-        nc, j = NP[p] // 32, 28 + 3 * "on".index(p)
-        iota(B("id" + p), [[16, nc], [16 * nc + 8, 2], [1, 8]])
-        iota(B("id" + p, 8, 16), [[1, 8]], 16 * nc)
-        iota(B("ac" + p), [[0, 16], [16, ST[p]]])
-        ts(B("ac" + p), B("ac" + p), H88, A.add)
-        iota(B("f1f" + p), [[8, 2], [16, nc]])
-        ts(cf(j), I_, 16.0 * nc, A.mult, G_, A.add)
-        ts(B("f1" + p), B("f1f" + p), cf(j), A.add)
-        iota(B("cb" + p), [[16, nc]])
-        ts(cf(j + 1), H8, 16.0 * nc + 8, A.mult, CORR, A.add)
-        ts(cf(j + 2), H8, 16.0 * nc, A.mult, CORR, A.add)
-        ts(B("cb" + p, 1, nc), B("cb" + p, 1, nc), cf(j + 1), A.add)
-        ts(B("cb" + p, 0, 1), B("cb" + p, 0, 1), cf(j + 2), A.add)
-    TI = B("tan", 0, 16)
-    iota(TI, [[0, 2], [1, 8]])
-    ts(TI, TI, G_, A.subtract)
-    ts(B("rxf", 0, 16), TI, 0.0, A.is_lt, 8.0, A.mult)
-    tt(TI, TI, B("rxf", 0, 16), A.add)
-    ts(TI, TI, 20.0, A.mult)
-    iota(B("sd"), [[4, 320]])
-    ts(B("sd"), B("sd"), NCORR, A.add)
-    iota(B("cn"), [[-1, 20]])
-    ts(B("cn"), B("cn"), CORR, A.add)
-    fill(B("xnb", 384, 512), 0.0)
-    quant("zq", 0, 128, "zb", 0)
-    for r in range(1, ROUNDS + 1):
-        dma("y", "zf", [B("zqc", 0, 32)], [B("ld%dc" % r, 96, 128)], T["ld%dc" % r][:, 96:128].bitcast(dt.uint8), T.zqc[:, 0:32].bitcast(dt.uint8))
-        dma("y", "zf", [B("zqs", 0, 32)], [B("ld%ds" % r, 96, 128)], T["ld%ds" % r][:, 96:128], T.zqs[:, 0:32])
+        cp(B("tf", 128 * a, 128 * a + 128), ("@", B("chf", 8 * a, 8 * a + 8), B("lt")))
+    for a in range(4):
+        latch(B("tl", 256 * a, 256 * a + 256), B("tf", 256 * a, 256 * a + 256))
+    ts(t[7], C8, 8.0, A.add)
+    ts(B("tab"), B("tl", 15, 1024, 16), t[7], A.add)
+    ts(cf(41), HB, 16.0, A.mult, I_, A.add)
+    iota(B("i32b"), [[1, 32]])
+    ts(B("eye"), B("i32b"), cf(41), A.is_equal)
+    for k in range(4):
+        for e in range(4):
+            q = (32 * k, 32 * k + 32)
+            cp(B("lb", 512 * k + 129 * e, 512 * k + 128 * e + 128, 4, q), B("eye", p=q), "s")
+    quant("lq", 0, 512, "lb", 0)
+    for b in range(4):
+        o = B("eb", 512 * b, 512 * b + 512)
+        op({"g": 1020.0}, [B("one")], [o], lambda e, o=o, b=b: e.affine_select(view(o), view(B("one")), [[-4, 128], [-1, 4]], A.is_equal, 0.0, b, 4))
+    quant("eq", 0, 512, "eb", 0)
     quant("vq", 0, 128, "vb", 0)
 
-    def products(p, x, xlo):
-        n = 224 if p == "o" else 128
-        mm(0, n, "ur", 0, x, xlo)
-        mm(1, n, "ur", 0, x, xlo)
-        mm(2, 128, x, xlo, "uq", 0)
+    def calls(p, x):
+        bq, at = "bq" + p, 0 if p == "o" else 8
+        for j, lo in enumerate((96, 192) if p == "o" else (0,)):
+            mm(1 + j, 128, x, lo, "uq", 0)
+            ts(B("bt", at + 4 * j, at + 4 * j + 3), ps(1 + j, 1, 4), 0.0, A.is_gt)
+        quant(bq, 0, 128, "bt", at)
+        mm(1, 128, "ca", 0 if p == "o" else 128, bq, 0)
         if p == "o":
-            mm(7, 128, x, xlo + 96, "uq", 0)
-
-    def calls(p):
-        s = "st" + p
-        for b, m, o in [(2, "ma" + p, 0)] + ([(7, "mb", 512)] if p == "o" else []):
-            bits = "bt%d" % (o // 512)
-            ts(B(bits), ps(b, 1, 4), 0.0, A.is_gt)
-            for t in range(3):
-                lay(B(s, o + t, o + 512, 4), B(m), B(bits, t, t + 1))
-        if p == "o":
-            quant("sqo", 0, 256, s, 0)
-            mm(2, 128, "sqo", 0, "mv", 0, True, False)
-            mm(2, 128, "sqo", 128, "mv", 256, False, True)
+            ts(cf(40), ps(1, 1, 2), HB, A.mult, qs="v")
+            ts(B("ixo"), ps(1, 0, 1), NB, A.mult, cf(40), A.add)
         else:
-            quant("sqn", 0, 128, s, 0)
-            mm(2, 128, "sqn", 0, "mv", 128)
-        cp(B("ix" + p), ps(2, 0, ST[p]))
-        tt(B("lf" + p), ("@", B("t1"), B("ix" + p)), B("ac" + p), A.add)
-        cp(B("li" + p), B("lf" + p))
+            cp(B("ixn"), ps(1, 0, 1))
+        cp(B("li" + p, 0, 32, 2), ("@", B("tab"), B("ix" + p)))
 
     def pieces(p):
-        nc, st, n = NP[p] // 32, ST[p], NP[p]
-        w = 16 * nc
-        for e in range(16):
-            b = B("id" + p) if e == 0 else B("xw" + p, w * e - w, w * e)
-            cp(B("xw" + p, w * e, w * e + w), ("@", b, B("li" + p, st * e, st * e + nc)), CHAIN[p])
-        latch(B("tw" + p), B("xw" + p, 15 * w, 16 * w))
-        tt(B("tv" + p), B("tw" + p, 15, w, 16), B("cb" + p), A.subtract)
-        cp(B("tl" + p, 0, 2 * nc, 2), B("tv" + p))
-        for s in range(2 * nc):
-            b, j = 16 * s + (8 if s > nc else 0), 2 * (s % nc)
-            cp(B("ta" + p, 16 * s + 16, 16 * s + 32), ("@", B("ta" + p, b, b + 8), B("tl" + p, j, j + 1)), CHAIN[p])
-        cp(B("lr" + p), ("@", B("xw" + p), B("f1" + p)), "x")
-        latch(B("lw" + p), B("lr" + p))
-        ts(B("ll" + p), B("lw" + p, 15, n, 16), CORR, A.subtract)
+        x, n, pf = "x" + p, 16 if p == "o" else 8, "opf" if p == "o" else "pfn"
+        for e in range(n):
+            cp(B(x, 16 * e + 16, 16 * e + 32), ("@", B(x, 16 * e, 16 * e + 16), B("li" + p, 2 * e, 2 * e + 1)), PIN["chain"])
+        cp(B("pp" + p), ("@", B(x, 16 * n, 16 * n + 16), B("p4")), PIN["chain"])
+        turn(B("to" + p), B("pp" + p))
+        share("to" + p, 32)
+        cp(B("lp" + p, 0, 32, 2), ("@", B("to" + p), B("ptl")))
+        for e in range(6):
+            cp(B(pf, 16 * e + 16, 16 * e + 32), ("@", B(pf, 16 * e, 16 * e + 16), B("lp" + p, 2 * e, 2 * e + 1)), PIN["chain"])
+        cp(B("z" + p), ("@", B(x, 16, 16 * n + 16), B("ll", 0, n)), PIN["rows"])
+        latch(B("w" + p), B("z" + p))
+        if p == "o":
+            ts(B("fl", 8, 24), B("wo", 15, 256, 16), FW, A.add)
+            cp(B("xg"), ("@", B("opf"), B("hl")), PIN["rows"])
+            latch(B("xl"), B("xg"))
+            ts(B("lx"), B("xl", 15, 16), C8, A.add)
+        else:
+            ts(B("fl", 0, 8), B("wn", 15, 128, 16), FN, A.add)
 
-    def rows_own():
-        pieces("o")
-        cp(B("rr"), ("@", B("tao"), B("llo")), "x")
-        latch(B("rv"), B("rr"))
-        ts(B("rlst"), B("rv", 15, 224, 16), CORR, A.subtract)
+    def rows():
+        cp(B("pfn", 112, 128), ("@", B("pfn", 96, 112), B("lx")), PIN["chain"])
+        cp(B("rf", 0, 128), ("@", B("pfn"), B("fl", 0, 8)), PIN["rows"])
+        cp(B("rf", 128, 384), ("@", B("pfn"), B("fl", 8, 24)), PIN["rows"])
+        turn(B("rt"), B("rf"))
+        share("rt", 384)
+        cp(B("rr"), ("@", B("rt"), B("rll")), PIN["rows"])
+        for e in range(1, 8):
+            o, i = B("mk", e, 1024, 8), B("rr")
 
-    def rows_new():
-        pieces("n")
-        cp(B("row", 0, 96), ("@", B("tan"), B("lln")), "x")
-        cp(B("row", 96, 320), ("@", B("tan", 104, 112), B("rlst")), "x")
-        latch(B("rol"), B("row"))
-        tt(B("rxf"), B("rol", 15, 320, 16), B("cn"), A.subtract)
-        cp(B("rx"), B("rxf"))
-        ts(B("ro4"), B("row"), 64.0, A.mult)
-
-    def scores(p):
-        n = NP[p]
-        tt(B("sx" + p), ps(0, 0, n), B("mk", 0, n), A.mult)
-        scan(B("so" + p), B("dr", 0, n), B("sx" + p), A.mult, A.add)
-        ab, z = B("ab" + p), "zz" + p
-        op("s", [ps(1, 0, n)], [ab], lambda e: e.activation(view(ab), view(ps(1, 0, n)), ACT.Abs, bias=2.0 ** -120, scale=0.6 * 2.0 ** -23), acost(ab, []))
-        cp(B(z, 0, n), ps(1, 0, n), "s")
-        if p == "n":
-            tt(B(z, 96, 192), ps(0, 0, n), ab, A.add)
-        tt(B("am" + p), ab, B("ml" if p == "n" else "mg", 0, n), A.mult)
-        tt(B("sg" + p), ps(0, 0, n), B("am" + p), A.add if p == "n" else A.subtract)
-
-    def parts_out(p, x, xlo):
-        c0, n = (96, 224) if p == "o" else (0, 96)
-        for b in range(4):
-            mm(4 + b, max(n, 128), "eq", 128 * b, x, xlo)
-        for b in range(4):
-            cp(B("win", 4 * c0 + b, 4 * (c0 + n), 4), ps(4 + b, 0, n), "x")
-
-    def turn(p, r):
-        lo, hi = (384, 1280) if p == "o" else (0, 384)
-        for s in range(1, 8):
-            o = 1280 * s
-            for d0, d1, s0 in ((0, 128 - 16 * s, 16 * s), (128 - 16 * s, 128, 0)):
-                dma("y", "f%s%d" % (p, r), [("win", lo, hi, 1)], [("win", o + lo, o + hi, 1)], T.win[d0:d1, o + lo:o + hi], T.win[s0:s0 + d1 - d0, lo:hi], 14000.0 if p == "o" else 9000.0)
+            def fn(q, o=o, i=i, e=e):
+                if q is g.vector:
+                    return q.tensor_scalar(view(o), view(i), float(e), BIG, A.is_ge, A.mult)
+                return q.activation(view(o), view(i), ACT.Relu, bias=BIG * (0.5 - e), scale=BIG)
+            op(costs(PIN["mask"], o, [i]), [i], [o], fn)
 
     turns = []
 
@@ -552,78 +531,95 @@ def rank_program(g, core, T, topo):
             if e is g.vector:
                 return e.tensor_reduce(view(acc), view(i), AxisListType.X, A.add)
             return e.activation(view(j), view(i), ACT.Copy, accum_out=view(acc))
-        op("x", [i], [j, acc], fn, 20 + acost(j, []))
+        c = {"s": 20 + ac(j, []), "v": max(64, width(i)) * CY}
+        op({q: c[q] for q in PIN["count"]}, [i], [j, acc], fn)
 
-    def compare_own():
-        for k in range(14):
-            own = B("soo", 16 * k + 15, 16 * k + 16)
-            o = 896 * (k // 4) + k % 4
-            for z, lo, hi, f in (("sgo", 16 * k, 16 * k + 16, A.is_lt), ("zzo", 16 * k + 16, 224, A.is_le)):
-                if lo < hi:
-                    ts(B("go", o + 4 * lo, o - k % 4 + 4 * hi, 4), B(z, lo, hi), own, f)
-            if k < 13:
-                count(B("go", o + 4 * (16 * k + 16), o - k % 4 + 896, 4), B("aft", k, k + 1))
-        for q in range(4):
-            lo = min(64 * q, 96)
-            quant("gq", 224 * q + lo, 224 * q + 224, "go", 896 * q + 4 * lo)
-            mm(3, 224, "cc", 0, "gq", 224 * q, q == 0, False)
+    def slot(tile, q, e, lo, hi):
+        at, c0 = (GO if tile == "go" else GN)[q]
+        return B(tile, at + 4 * (lo - c0) + e, at + 4 * (hi - c0), 4)
 
-    def compare_new():
-        for k in range(6):
-            own = B("son", 16 * k + 15, 16 * k + 16)
-            q, t = divmod(k, 4)
-            o = 1280 * q
-            ts(B("gn", o + t, o + 896, 4), B("zzo"), own, A.is_gt)
-            ts(B("gn", o + 896 + t, o + 1216, 4), B("zzn", 16 * k + 16, 96 + 16 * k), own, A.is_gt)
-            ts(B("gn", o + 1216 + t, o + 1280, 4), B("sgn", 16 * k, 16 * k + 16), own, A.is_gt)
-            count(B("gn", o + t, o + 1280, 4), B("acl", k, k + 1))
-        for q in range(2):
-            quant("gw", 224 * q, 224 * q + 224, "gn", 1280 * q)
-            mm(3, 224, "cc", 128, "gw", 224 * q, False, q == 1)
+    def compare(p, x):
+        bank, c0, n, w = (0, 96, 224, 224) if p == "o" else (2, 0, 96, 320)
+        mm(bank, w, "ur", 0, x, c0)
+        tt(B("y" + p), ps(bank, 0, n), B("yc", 0, n), A.add)
+        scan(B("so" + p), B("d0", 0, n), B("y" + p), A.add, A.max)
+        d = slot("g" + p, 0, 0, c0, c0 + n)
+        tt(d, ps(bank, 0, n), B("so" + p), A.is_gt)
+        scan(B("dcs", c0, c0 + n), B("dr", 0, n), d, A.mult, A.add)
+        for k in range(13 if p == "o" else 6):
+            lo = c0 + 16 * k + 16
+            if p == "o" and k > 10:
+                o = slot("gn", k - 11, 3 * (k - 11), lo, 320)
+            else:
+                o = slot("g" + p, (k + 1) // 4, (k + 1) % 4, lo, 320)
+            ts(o, ps(bank, lo - c0, w), B("so" + p, 16 * k + 15, 16 * k + 16), A.is_gt)
+            count(o, B("acl", c0 // 16 + k, c0 // 16 + k + 1))
+        for q, (at, lo) in enumerate(GO if p == "o" else GN):
+            j = 320 * (q if p == "o" else 3 + q)
+            quant("gq", j + lo, j + 320, "g" + p, at)
+            mm(3, 320, "cc", 0, "gq", j, p == "o" and q == 0, p == "n" and q == 1)
+
+    def window(p, x):
+        c0, n = (96, 224) if p == "o" else (0, 96)
+        for k in range(4):
+            mm(4 + k, max(n, 128), "lq", 128 * k, x, c0)
+        for k in range(4):
+            cp(B("win", 1280 + 320 * k + c0, 1280 + 320 * k + c0 + n), ps(4 + k, 0, n), PIN["win"])
+
+    def swap(r):
+        for k in range(4):
+            for b in range(2):
+                d, s = 32 * k + 16 * b, 32 * k + 16 - 16 * b
+                o, i = B("win", 2560 - 2560 * b, 3840 - 2560 * b, 1, (d, d + 16)), B("win", 1280, 2560, 1, (s, s + 16))
+                dma("y", "sw%d" % r, [i], [o], view(o), view(i), 3500.0)
 
     def early(r):
-        x = "qt%d" % r
-        products("o", x, 96)
-        calls("o")
-        scores("o")
-        parts_out("o", x, 96)
-        turn("o", r)
-        compare_own()
-        rows_own()
+        x = "qx%d" % r
+        calls("o", x)
+        compare("o", x)
+        window("o", x)
+        pieces("o")
 
-    def late(r, x):
-        products("n", x, 0)
-        calls("n")
-        scores("n")
-        parts_out("n", x, 0)
-        turn("n", r)
-        compare_new()
-        cp(B("rk16", 0, 6), B("acl"))
-        tt(B("rkc"), B("aft"), B("cs"), A.add)
-        latch(B("cl"), ps(3, 0, 224))
-        tt(B("rko"), B("cl", 15, 224, 16), B("rkc"), A.subtract)
-        cp(B("rk16", 6, 20), B("rko"))
-        op("v", [B("rk16"), B("sd")], [B("ob")], lambda e: e.tensor_copy(view(B("ob")).indirect(view(B("rk16"))), view(B("sd"))), 50 + 3.3 * CY * 320)
-        latch(B("ol"), B("ob"))
-        cp(B("ow", 0, 20), B("ol", 15, 320, 16))
-        for s in range(1, 8):
-            for d0, d1, s0 in ((0, 128 - 16 * s, 16 * s), (128 - 16 * s, 128, 0)):
-                dma("y" if s % 2 else "s", "od%d" % r, [B("ow", 0, 20)], [B("ow", 20 * s, 20 * s + 20)], T.ow[d0:d1, 20 * s:20 * s + 20], T.ow[s0:s0 + d1 - d0, 0:20], 3500.0)
-        rows_new()
-        tt(B("os1"), ("@", B("ow"), B("rx")), B("ro4"), A.add)
-        latch(B("os2"), B("os1"))
-        for b in range(4):
-            ts(B("fl%d" % b), B("os2", 15, 320, 16), cf(40 + b), A.add)
-        t = "qt%d" % (r + 1)
-        for (l0, l1) in ((0, 8), (8, 20)):
-            for b in range(4):
-                cp(B("tb", 64 * l0 + b, 64 * l1, 4), ("@", B("win"), B("fl%d" % b, l0, l1)), "x")
-            quant(t, 16 * l0, 16 * l1, "tb", 64 * l0)
-            if l0 == 0:
+    def late(r):
+        x = "qx%d" % r
+        calls("n", x)
+        compare("n", x)
+        window("n", x)
+        swap(r)
+        pieces("n")
+        rows()
+        tt(B("rc1"), B("dcs", 15, 320, 16), B("cm"), A.add)
+        tt(B("rc2"), B("rc1"), B("acl"), A.add)
+        latch(B("cl"), ps(3, 0, 320), "dlf")
+        tt(B("rkf"), B("cl", 15, 320, 16), B("rc2"), A.add)
+        cp(B("rk"), B("rkf"))
+        w = B("ob", 16, 336)
+        op({"v": 50 + 3.3 * CY * 320}, [B("rk"), B("sd")], [w], lambda e: e.tensor_copy(view(w).indirect(view(B("rk"))), view(B("sd"))))
+        turn(B("tr", 0, 320), w)
+        turn(B("tr", 320, 672), B("ob"))
+        share("tr", 672)
+        for lo, hi in ((0, 4), (4, 10)):
+            tt(B("ot", 16 * lo, 16 * hi), ("@", B("tr"), B("otl", lo, hi)), B("oc0", 16 * lo, 16 * hi), A.add)
+        for p, m0, n, at, l0 in (("n", 0, 6, 0, 0), ("o", 6, 14, 128, 24)):
+            for G in range(4):
+                o = 8 * (l0 + n * G)
+                scan(B("sc", o, o + 8 * n), B("mk", 256 * G + at, 256 * G + at + 8 * n), B("ot", 8 * m0, 8 * (m0 + n)), A.add, A.min)
+            cp(B("il", l0, l0 + 4 * n), B("sc", 8 * l0 + 7, 8 * (l0 + 4 * n), 8))
+            step = 12 if p == "n" else 14
+            for l in range(l0, l0 + 4 * n, step):
+                cp(B("st", 16 * l, 16 * (l + step)), ("@", B("win"), B("il", l, l + step)), PIN["pick"])
+            for G in range(4):
+                for e in range(4):
+                    o = B("ta" if p == "n" else "tb", 64 * m0 + e, 64 * (m0 + n), 4, (32 * G, 32 * G + 32))
+                    cp(o, B("st", 16 * (l0 + n * G), 16 * (l0 + n * G + n), 1, (32 * e, 32 * e + 32)), PIN["lay"])
+            if p == "n":
+                quant("qs%d" % (r + 1), 0, 128, "ta", 0)
                 send(r + 1)
+            else:
+                quant("qx%d" % (r + 1), 96, 320, "tb", 384)
 
     def send(r):
-        t = "qt%d" % r
+        t = "qs%d" % r
         dst = T.cores[(rank + r) % len(T.cores)]
         rid, pid = topo.addr(dst)[:2]
         m = topo.mask(core, dst)
@@ -636,47 +632,52 @@ def rank_program(g, core, T, topo):
                     o, i = o.bitcast(dt.uint8), i.bitcast(dt.uint8)
                 g.remote_dma(o, i, T.sem["rc%d" % r], T.sem["ls"], pid, rid, m)
                 K["total"]["ls"] = K["total"].get("ls", 0) + len(topo.engines(core, dst))
-        raw("g", [B(t + "c", 0, 96), B(t + "s", 0, 96)], [("sent%d" % r, 0, 1, 1)], fn, 600.0, 2000.0)
+        raw("g", [B(t + "c", 0, 96), B(t + "s", 0, 96)], [("sent%d" % r, 0, 1, 1, 0, 128)], fn, 600.0, 2000.0)
 
     def arrive(r):
         frm = T.cores[(rank - r) % len(T.cores)]
         n = 2 * len(topo.engines(frm, core))
-        raw("t", [("sent%d" % r, 0, 1, 1)], [B("ld%dc" % r, 0, 96), B("ld%ds" % r, 0, 96)], lambda: K["wait"]("t", "rc%d" % r, n, {}), 1.0, 0.0)
+        raw("t", [("sent%d" % r, 0, 1, 1, 0, 128)], [B("ld%dc" % r, 0, 96), B("ld%ds" % r, 0, 96)], lambda: K["wait"]("t", "rc%d" % r, n, {}), 1.0, 0.0)
         for b in range(4):
-            a = (0, 1, 2, 0)[b]
+            a = 1 + b % 2
             mm(4 + b, 128, "wq", 128 * b, "ld%d" % r, 0)
             mm(a, 128, "eq", 128 * b, "ld%d" % r, 0)
             o, i = B("rl", 96 * b, 96 * b + 96), ps(4 + b, 0, 96)
-            op("s", [i], [o], lambda e, o=o, i=i: e.activation(view(o), view(i), ACT.Relu, scale=0.03125), acost(o, []))
-            tt(B("xnb", b, 384, 4), o, ps(a, 0, 96), A.add)
-        quant("xn%d" % r, 0, 128, "xnb", 0)
+
+            def fn(e, o=o, i=i):
+                if e is g.vector:
+                    return e.tensor_scalar(view(o), view(i), 0.0, 0.03125, A.max, A.mult)
+                return e.activation(view(o), view(i), ACT.Relu, scale=0.03125)
+            op(costs("s", o, [i]), [i], [o], fn)
+            tt(B("tb", b, 384, 4), o, ps(a, 0, 96), A.add)
+        quant("qx%d" % r, 0, 128, "tb", 0)
+
+    def store(lo, hi, bank):
+        x = "qx%d" % ROUNDS
+        mm(bank, hi - lo, "vq", 0, x, lo)
+        cp(B("yb", lo, hi), ps(bank, 0, hi - lo))
+        dma("s" if lo == 0 else "y", "out", [B(x + "c", lo, hi)], [], T.oc[:, 4 * lo:4 * hi], view(B(x + "c", lo, hi)).bitcast(dt.uint8))
+        for k in range(4):
+            dma("y", "out", [B(x + "s", lo, hi)], [], T.osc[4 * k:4 * k + 4, lo:hi], T[x + "s"][32 * k:32 * k + 4, lo:hi])
+        dma("y", "out", [B("yb", lo, hi)], [], T.y[:, lo:hi], T.yb[:, lo:hi])
 
     early(0)
-    late(0, "qt0")
+    late(0)
     for r in (1, 2):
         early(r)
         arrive(r)
-        late(r, "xn%d" % r)
-    x = "qt3"
-    mm(3, 224, "vq", 0, x, 96)
-    cp(B("yb", 96, 320), ps(3, 0, 224), "s")
-    ts(B("rwa"), B("row"), 0.05, A.mult, G_, A.add)
-    cp(B("rwi"), B("rwa"))
-    ts(B("rwa"), B("rwi"), 7.5, A.is_ge, -8.0, A.mult)
-    tt(B("rwb"), B("rwa"), B("rwi"), A.add)
-    dma("y", "out", [B(x + "c", 96, 320)], [], T.oc[:, 384:1280], T[x + "c"][:, 96:320].bitcast(dt.uint8))
-    for k in range(4):
-        dma("y", "out", [B(x + "s", 96, 320)], [], T.osc[4 * k:4 * k + 4, 96:320], T[x + "s"][32 * k:32 * k + 4, 96:320])
-    dma("y", "out", [B("yb", 96, 320)], [], T.y[:, 96:320], T.yb[:, 96:320])
-    dma("s", "out", [B("rwb")], [], T.rw[:, :], T.rwb[0:128:16, :])
+        late(r)
+    q0 = (0, 32)
+    turn(B("rwt", p=q0), B("rr", p=q0))
+    ts(B("rw1", p=q0), B("rwt", p=q0), 4.0, A.is_ge, -7.0, A.mult)
+    ts(B("rw2", p=q0), B("rwt", p=q0), 2.0, A.mult)
+    tt(B("rwb", p=q0), B("rw1", p=q0), B("rw2", p=q0), A.add)
+    for h in range(8):
+        dma("y", "out", [B("rwb")], [], T.rw[h, 0:96], T.rwb[0:6, 16 * h:16 * h + 16])
+        dma("y", "out", [B("rwb")], [], T.rw[h, 96:320], T.rwb[16:30, 16 * h:16 * h + 16])
+    store(128, 320, 0)
     arrive(3)
-    x = "xn3"
-    mm(3, 128, "vq", 0, x, 0)
-    cp(B("yb", 0, 96), ps(3, 0, 96), "s")
-    dma("s", "out", [B(x + "c", 0, 96)], [], T.oc[:, 0:384], T[x + "c"][:, 0:96].bitcast(dt.uint8))
-    for k in range(4):
-        dma("s" if k % 2 else "y", "out", [B(x + "s", 0, 96)], [], T.osc[4 * k:4 * k + 4, 0:96], T[x + "s"][32 * k:32 * k + 4, 0:96])
-    dma("y", "out", [B("yb", 0, 96)], [], T.y[:, 0:96], T.yb[:, 0:96])
+    store(0, 128, 1)
     K["run"]()
     for sem, n in sorted(K["total"].items()):
         K["wait"]("g", sem, n, {})

@@ -2,7 +2,7 @@ from concourse.mybir import dt, AluOpType, AxisListType, ActivationFunctionType
 
 CY = 0.83
 SLACK = 60.0
-HOP, SELF = 130.0, 80.0
+HOP, SELF = 200.0, 200.0
 ROUNDS = 3
 STEP, LOW = 512.0, 16384.0
 STEP8, LOW8 = 8.0, 256.0
@@ -187,11 +187,12 @@ def _make(g, T):
         fin, qof, left = {}, {}, [len(j["pre"]) for j in jobs]
         ready = [i for i in range(n) if not left[i]]
 
+        known_start = {}
+
         def start(i, q):
-            t = 0.0
-            for k in jobs[i]["pre"]:
-                t = max(t, fin[k] + (SELF if qof[k] == q else HOP))
-            return t
+            if (i, q) not in known_start:
+                known_start[i, q] = max([fin[k] + (SELF if qof[k] == q else HOP) for k in jobs[i]["pre"]] or [0.0])
+            return known_start[i, q]
         while ready:
             best = None
             for i in ready:
@@ -225,7 +226,7 @@ def _make(g, T):
 
 
 WORSE = 0.5
-PIN = {"chain": "s", "count": "s", "shift": "vs", "lay": "vs", "win": "vs", "pick": "vs", "mask": "vs", "rows": "vs"}
+PIN = {"chain": "vs", "count": "vs", "shift": "vs", "lay": "vs", "win": "vs", "pick": "vs", "mask": "vs", "rows": "vs"}
 
 
 def rank_program(g, core, T, topo):

@@ -1,16 +1,19 @@
+import numpy as np
 from concourse.mybir import dt, AluOpType, AxisListType, ActivationFunctionType
 
 CY = 0.83
-SLACK = 60.0
-HOP, SELF = 200.0, 200.0
+SLACK, HOP, WORSE, TRIES = 60.0, 200.0, 0.5, 600
 ROUNDS = 3
-STEP, LOW = 512.0, 16384.0
+STEP, LOW = 4096.0, 131072.0
 STEP8, LOW8 = 8.0, 256.0
-BIG = 16384.0
+BIG, KEY = 65536.0, 4096
+FIELDS = ((5, 3), (4, 1), (3, 1), (2, 1), (0, 3), (0, 15), (0, 7), (1, 63), (0, 1), (4, 7), (1, 3), (1, 7), (1, 1), (6, 1), (5, 1), (4, 3))
 F32, BF, I32, U16 = "float32", "bfloat16", "int32", "uint16"
 CODE, SC = "float8_e4m3fn_x4", "uint8"
+SIZE = {F32: 4, BF: 2, I32: 4, U16: 2, CODE: 4, SC: 1}
 GO = ((0, 96), (896, 160), (1536, 192))
 GN = ((0, 0), (1280, 64))
+PIN = {"chain": "vs", "count": "vs", "shift": "vs", "lay": "vs", "win": "vs", "pick": "vs", "mask": "vs", "rows": "vs", "relu": "vs"}
 
 
 def _scratch():
@@ -24,11 +27,11 @@ def _scratch():
         sb(name + "s", n, SC)
     for b in range(8):
         d["ps%d" % b] = ("psum", [128, 512], F32)
-    for n, w in (("xb", 1280), ("ub", 512), ("vb", 512), ("eb", 2048), ("lb", 2048), ("zb", 768), ("ccb", 512), ("cab", 1024), ("one", 512),
-                 ("bt", 520), ("eye", 32), ("i32b", 32), ("ta", 512), ("tb", 1280), ("st", 1280), ("win", 3840), ("go", 2048), ("gn", 2304), ("jk", 1280),
-                 ("m64", 512), ("ico", 256)):
+    for n, w in (("xb", 1280), ("ub", 512), ("vb", 512), ("eb", 2048), ("lb", 2048), ("zb", 768), ("ccb", 512), ("cab", 1536), ("one", 512),
+                 ("bt", 528), ("eye", 64), ("i64", 64), ("ta", 512), ("tb", 1280), ("st", 1280), ("win", 5120), ("go", 2048), ("gn", 2304), ("jk", 1280),
+                 ("m64", 512), ("ico", 384), ("mkn", 512), ("mko", 512)):
         sb(n, w, BF)
-    for n, w in (("uq", 128), ("ur", 128), ("vq", 128), ("eq", 512), ("lq", 512), ("zq", 192), ("wq", 512), ("cc", 128), ("ca", 256), ("bqo", 128),
+    for n, w in (("uq", 128), ("ur", 128), ("vq", 128), ("eq", 512), ("lq", 512), ("zq", 192), ("wq", 512), ("cc", 128), ("ca", 384), ("bqo", 130),
                  ("bqn", 128), ("gq", 1600)):
         mx(n, w)
     for r in range(ROUNDS + 1):
@@ -36,17 +39,19 @@ def _scratch():
         if r:
             mx("ld%d" % r, 128)
             mx("qs%d" % r, 128)
-    sb("pi", 1, I32), sb("bi", 11, I32), sb("chi", 64, I32), sb("chb", 64, I32)
-    for n, w in (("cf", 48), ("ulf", 8), ("i32", 10), ("llf", 16), ("cm", 20), ("oc0", 160), ("dlf", 320), ("yc", 224), ("d0", 224), ("chf", 64), ("m8", 64),
-                 ("k8", 64), ("d8", 64), ("cht", 64), ("chs", 64), ("yo", 224), ("soo", 224), ("yn", 96), ("son", 96), ("acl", 20), ("rc1", 20), ("rc2", 20),
-                 ("cl", 320), ("rkf", 20), ("ot", 160), ("sc", 640), ("rl", 384), ("yb", 320), ("rw1", 128), ("rw2", 128), ("rwb", 128)):
+    sb("pi", 1, I32), sb("bi", len(FIELDS), I32), sb("chi", 64, I32), sb("chb", 64, I32), sb("rwi", 64, I32), sb("rwj", 64, I32)
+    for n, w in (("cf", 80), ("ulf", 8), ("i32", 2), ("llf", 16), ("cm", 20), ("i16", 20), ("bs", 20), ("oc0", 224), ("oc", 320), ("dlf", 320), ("dlo", 320),
+                 ("yc", 224), ("d0", 224), ("chf", 64), ("m8", 64), ("k8", 64), ("d8", 64), ("cht", 64), ("chs", 64), ("yo", 224), ("soo", 224), ("sco", 224),
+                 ("yn", 96), ("son", 96), ("acl", 20), ("rc1", 20), ("rc2", 20), ("cl", 320), ("rkf", 20), ("ot", 320), ("sc", 640), ("rl", 384),
+                 ("yb", 320), ("rw0", 64), ("rw1", 64), ("rw2", 64), ("rw3", 64), ("rwb", 64), ("wa", 320), ("wl", 320), ("h1", 8), ("h2", 8),
+                 ("h3", 8), ("h4", 8), ("h5", 8), ("h6", 8), ("h7", 8), ("h8", 8), ("pfn", 160), ("pfo", 224)):
         sb(n, w)
-    for n, w in (("bm16", 320), ("dr", 224), ("dlb", 256), ("sd", 320), ("ob", 352), ("tr", 672), ("dcs", 320), ("tf", 1024), ("tl", 1024), ("tab", 64),
-                 ("xo", 272), ("xn", 144), ("ppo", 32), ("ppn", 32), ("too", 32), ("ton", 32), ("opf", 128), ("pfn", 128), ("xg", 16), ("xl", 16),
-                 ("zo", 256), ("zn", 128), ("wo", 256), ("wn", 128), ("rf", 384), ("rt", 384), ("rr", 128), ("mk", 1024), ("rwt", 128)):
+    for n, w in (("bm16", 320), ("dr", 224), ("dlb", 256), ("sd", 320), ("ob", 352), ("tr", 672), ("dcs", 320), ("tf", 1024), ("tl", 1024), ("tab", 128),
+                 ("xo", 288), ("xn", 144), ("ppo", 64), ("ppn", 32), ("too", 64), ("ton", 32), ("a2", 320),
+                 ("zo", 256), ("zn", 128), ("rto", 256), ("rtn", 128), ("rro", 32), ("rrn", 32)):
         sb(n, w, BF + "*")
-    for n, w in (("ul", 8), ("otl", 10), ("rll", 8), ("ptl", 1), ("ll", 16), ("hl", 1), ("p4", 2), ("lt", 8), ("ixo", 1), ("ixn", 1), ("lio", 32), ("lin", 32),
-                 ("lpo", 32), ("lpn", 32), ("lx", 1), ("fl", 24), ("rk", 20), ("il", 80)):
+    for n, w in (("ul", 8), ("otl", 20), ("rlo", 2), ("rln", 2), ("pto", 1), ("ptn", 1), ("llo", 16), ("lln", 8), ("p4", 4), ("lt", 8), ("ixo", 1), ("ixn", 1),
+                 ("lio", 16), ("lin", 32), ("lpo", 16), ("lpn", 32), ("l2", 6), ("lf", 16), ("rk", 20), ("il", 80)):
         sb(n, w, U16)
     return d
 
@@ -68,8 +73,65 @@ def _pack(d):
 
 BUFS = _scratch()
 SCRATCH, PLACE = _pack(BUFS)
-SEMAPHORES = (["cv", "ct", "cs", "cg", "dx", "du", "dv", "dw", "dc", "z1", "z2", "z3", "z4", "z5", "zw", "out", "ls"]
-              + ["sw%d" % r for r in range(3)] + ["rc%d" % r for r in range(1, 4)])
+SEMAPHORES = (["cv", "ct", "cs", "cg", "dx", "du", "dv", "dw", "dc", "z1", "z4", "z5", "out", "ls"]
+              + [k + "%d" % r for k in ("so", "sn") for r in range(3)] + ["rc%d" % r for r in range(1, 4)])
+PLANS = {}
+
+
+def _plan(jobs):
+    n = len(jobs)
+    after = [[] for _ in jobs]
+    for i, j in enumerate(jobs):
+        for k in j["pre"]:
+            after[k].append(i)
+    way, both = [0.0] * n, {}
+    for j in jobs:
+        both[j["sem"]] = both.get(j["sem"], 0.0) + j["dur"]
+    for i in range(n - 1, -1, -1):
+        j = jobs[i]
+        way[i] = min(j["c"].values()) + j["lat"] + (j["dur"] if j["sem"] in ("raw", "out") else both[j["sem"]]) + max([way[k] + HOP for k in after[i]] or [0.0])
+
+    def once(prio):
+        free, fin, left = {q: 0.0 for q in "vtsgy"}, [0.0] * n, [len(j["pre"]) for j in jobs]
+        t0, order, engines = [0.0] * n, [], 0.0
+        ready = [i for i in range(n) if not left[i]]
+        while ready:
+            best = None
+            for i in ready:
+                c, t = jobs[i]["c"], t0[i]
+                if len(c) == 1:
+                    qs = c
+                else:
+                    ev, es = max(free["v"], t) + c["v"], max(free["s"], t) + c["s"]
+                    qs = "s" if ev > es + WORSE * c["v"] else "v" if es > ev + WORSE * c["s"] else "vs"
+                for q in qs:
+                    key = (max(free[q], t - SLACK), -prio[i])
+                    if best is None or key < best[0]:
+                        best = (key, i, q)
+            key, i, q = best
+            j = jobs[i]
+            ready.remove(i)
+            free[q] = fin[i] = max(free[q], t0[i]) + j["c"][q]
+            if j["dur"]:
+                engines = fin[i] = max(engines, fin[i] + j["lat"]) + j["dur"]
+            order.append((i, q))
+            for k in after[i]:
+                left[k] -= 1
+                t0[k] = max(t0[k], fin[i] + HOP)
+                if not left[k]:
+                    ready.append(k)
+        return max(fin), order
+    rng = np.random.RandomState(1)
+    best, prio = once(way), way
+    for _ in range(TRIES):
+        lo = rng.randint(n)
+        trial = list(prio)
+        for i in range(lo, min(n, lo + n // 6)):
+            trial[i] += float(rng.normal()) * 300.0
+        got = once(trial)
+        if got[0] <= best[0]:
+            best, prio = got, trial
+    return best
 
 
 def _make(g, T):
@@ -132,37 +194,27 @@ def _make(g, T):
                     old = [x for x in old if not (not x[1] and x[2] == q and x[3] == sem and cover(a, x[0]))]
                 recs[a[0]] = old + [(a, isw, q, sem, val, clk)]
 
-    def put(q, reads, writes, fn):
-        sem = comp[q]
-        need(q, reads, writes, sem, True)
-        total[sem] = total.get(sem, 0) + 1
-        fn(queues[q]).then_inc(T.sem[sem], 1)
-        note(q, reads, writes, sem, total[sem])
-
-    def put_dma(q, sem, reads, writes, out, in_):
-        need(q, reads, writes, sem, False)
-        total[sem] = total.get(sem, 0) + 16
-        queues[q].dma_start(out, in_).then_inc(T.sem[sem], 16)
-        note(q, reads, writes, sem, total[sem])
-
     def op(cost, reads, writes, fn):
-        jobs.append(dict(c=cost, r=reads, w=writes, fn=fn, lat=0.0, sem=None))
+        jobs.append(dict(c=cost, r=reads, w=writes, fn=fn, lat=0.0, dur=0.0, sem=None))
 
-    def dma(q, sem, reads, writes, out, in_, lat=2000.0):
-        jobs.append(dict(c={q: 60.0}, r=reads, w=writes, fn=(out, in_), lat=lat, sem=sem))
+    def dma(q, sem, reads, writes, out, in_):
+        a = (writes or reads)[0]
+        rows, row = a[5] - a[4], (a[2] - a[1]) * SIZE[SCRATCH[a[0]][2]]
+        jobs.append(dict(c={q: 60.0}, r=reads, w=writes, fn=(out, in_), lat=1300.0, dur=-(-rows // 16) * (30 + row / 12.0), sem=sem))
 
-    def raw(q, reads, writes, fn, cost, lat):
-        jobs.append(dict(c={q: cost}, r=reads, w=writes, fn=fn, lat=lat, sem="raw"))
+    def raw(q, reads, writes, fn, cost, lat=0.0, dur=0.0):
+        jobs.append(dict(c={q: cost}, r=reads, w=writes, fn=fn, lat=lat, dur=dur, sem="raw"))
 
     def run():
-        table, groups, n = {}, {}, len(jobs)
+        table, groups = {}, {}
         for i, j in enumerate(jobs):
             pre = set()
             grp = j["sem"] if j["sem"] not in (None, "raw") else None
             acc = [(span(a), False) for a in j["r"]] + [(span(a), True) for a in j["w"]]
             for a, isw in acc:
                 for x, xw, k in table.get(a[0], []):
-                    if k != i and meet(a, x) and (xw or isw or a[0][:2] == "ps") and (grp is None or jobs[k]["sem"] != grp):
+                    bank = a[0][:2] == "ps" and not (len(j["c"]) == 1 and j["c"].keys() == jobs[k]["c"].keys())
+                    if k != i and meet(a, x) and (xw or isw or bank) and (grp is None or jobs[k]["sem"] != grp):
                         pre.add(k)
             for a, isw in acc:
                 old = table.get(a[0], [])
@@ -176,57 +228,23 @@ def _make(g, T):
             j["pre"] = pre
             if grp:
                 groups.setdefault(grp, []).append(i)
-        after = [[] for _ in jobs]
-        for i, j in enumerate(jobs):
-            for k in j["pre"]:
-                after[k].append(i)
-        way = [0.0] * n
-        for i in range(n - 1, -1, -1):
-            way[i] = min(jobs[i]["c"].values()) + jobs[i]["lat"] + max([way[k] + 100.0 for k in after[i]] or [0.0])
-        free = {q: 0.0 for q in queues}
-        fin, qof, left = {}, {}, [len(j["pre"]) for j in jobs]
-        ready = [i for i in range(n) if not left[i]]
-
-        known_start = {}
-
-        def start(i, q):
-            if (i, q) not in known_start:
-                known_start[i, q] = max([fin[k] + (SELF if qof[k] == q else HOP) for k in jobs[i]["pre"]] or [0.0])
-            return known_start[i, q]
-        while ready:
-            best = None
-            for i in ready:
-                c = jobs[i]["c"]
-                ends = {q: max(free[q], start(i, q)) + c[q] for q in c}
-                for q in c:
-                    if ends[q] > min(ends.values()) + WORSE * c[q]:
-                        continue
-                    t = start(i, q)
-                    key = (max(free[q], t - SLACK), -way[i], ends[q])
-                    if best is None or key < best[0]:
-                        best = (key, i, q)
-            key, i, q = best
+        if len(jobs) not in PLANS:
+            PLANS[len(jobs)] = _plan(jobs)
+        for i, q in PLANS[len(jobs)][1]:
             j = jobs[i]
-            ready.remove(i)
-            free[q] = key[2]
-            fin[i] = free[q] + j["lat"]
-            qof[i] = q
-            if j["sem"] is None:
-                put(q, j["r"], j["w"], j["fn"])
-            elif j["sem"] == "raw":
+            if j["sem"] == "raw":
                 j["fn"]()
+                continue
+            sem = j["sem"] or comp[q]
+            need(q, j["r"], j["w"], sem, j["sem"] is None)
+            if j["sem"]:
+                total[sem] = total.get(sem, 0) + 16
+                queues[q].dma_start(*j["fn"]).then_inc(T.sem[sem], 16)
             else:
-                put_dma(q, j["sem"], j["r"], j["w"], j["fn"][0], j["fn"][1])
-            for k in after[i]:
-                left[k] -= 1
-                if not left[k]:
-                    ready.append(k)
-        jobs.clear()
+                total[sem] = total.get(sem, 0) + 1
+                j["fn"](queues[q]).then_inc(T.sem[sem], 1)
+            note(q, j["r"], j["w"], sem, total[sem])
     return dict(view=view, wait=wait, need=need, op=op, dma=dma, raw=raw, run=run, total=total)
-
-
-WORSE = 0.5
-PIN = {"chain": "vs", "count": "vs", "shift": "vs", "lay": "vs", "win": "vs", "pick": "vs", "mask": "vs", "rows": "vs"}
 
 
 def rank_program(g, core, T, topo):
@@ -305,8 +323,8 @@ def rank_program(g, core, T, topo):
     def scan(out, d0, d1, o0, o1):
         op({"v": vc(out, [d0, d1])}, [d0, d1], [out], lambda e: e.tensor_tensor_scan(view(out), view(d0), view(d1), 0.0, o0, o1))
 
-    def latch(out, d1, d="dlb"):
-        scan(out, B(d, 0, width(d1)), d1, A.add, A.max)
+    def latch(out, d1, d):
+        scan(out, d, d1, A.add, A.max)
 
     def turn(out, in_):
         op({"v": vc(out, [in_])}, [in_], [out], lambda e: e.transpose(view(out), view(in_)))
@@ -327,10 +345,6 @@ def rank_program(g, core, T, topo):
         else:
             op({"g": 130 + 2 * CY * width(out)}, [], [out], lambda e: e.iota(view(out), pat, base, cm, allow_small_or_imprecise_dtypes=True))
 
-    def ones_where(out, base):
-        n = width(out)
-        op({"g": 170 + 2 * CY * n}, [B("one", 0, n)], [out], lambda e: e.affine_select(view(out), view(B("one", 0, n)), [[-1, n]], A.is_equal, 0.0, base, 1))
-
     def quant(name, lo, hi, tile, tlo):
         t, c, s = B(tile, tlo, tlo + 4 * (hi - lo)), B(name + "c", lo, hi), B(name + "s", lo, hi)
         op({"v": 12 + 0.88 * (hi - lo)}, [t], [c, s], lambda e: e.quantize_mx(view(c), view(s), view(t)))
@@ -340,16 +354,13 @@ def rank_program(g, core, T, topo):
         o = ps(bank, 0, n)
         op({"t": 0.6 * (n + 16)}, [lc, ls, rc, rs], [o], lambda e: e.matmul_mx(view(o), view(lc), view(ls), view(rc), view(rs), start, stop))
 
-    def zeros(q, sem, n, lo, hi):
-        dma(q, sem, [B("zb", 0, hi - lo)], [B(n, lo, hi)], view(B(n, lo, hi)), view(B("zb", 0, hi - lo)))
-
     def zero_codes(q, sem, n, lo, hi):
         dma(q, sem, [B("zqc", 0, hi - lo)], [B(n + "c", lo, hi)], view(B(n + "c", lo, hi)).bitcast(dt.uint8), view(B("zqc", 0, hi - lo)).bitcast(dt.uint8))
         dma(q, sem, [B("zqs", 0, hi - lo)], [B(n + "s", lo, hi)], view(B(n + "s", lo, hi)), view(B("zqs", 0, hi - lo)))
 
-    dma("y", "dx", [], [B("xb")], view(B("xb")), T.x[:, :], 3800.0)
-    dma("s", "du", [], [B("ub")], view(B("ub")), T.u[:, :], 2600.0)
-    dma("y", "dc", [], [B("chi")], T.chi[0:1, 0:64], T.ch[:, :], 2200.0)
+    dma("y", "dc", [], [B("chi", p=(0, 1))], T.chi[0:1, 0:64], T.ch[:, :])
+    dma("y", "dx", [], [B("xb")], view(B("xb")), T.x[:, :])
+    dma("s", "du", [], [B("ub")], view(B("ub")), T.u[:, :])
     fill(B("zb"), 0.0)
     quant("zq", 0, 192, "zb", 0)
     for lo, hi in ((0, 96), (320, 480), (640, 832), (1280, 1344)):
@@ -359,85 +370,112 @@ def rank_program(g, core, T, topo):
     for a in (B("go", 0, 192), B("go", 896, 1088), B("go", 1536, 1856), B("gn", 0, 192), B("gn", 384, 1152, 4), B("gn", 1280, 1408), B("gn", 1283, 2240, 4),
               B("ta", 384, 512), B("bt")):
         fill(a, 0.0)
+    for n in ("mkn", "mko"):
+        dma("y", "z1", [B("zb", 0, 512)], [B(n)], view(B(n)), view(B("zb", 0, 512)))
     for r in range(1, ROUNDS + 1):
         zero_codes("y", "z5", "ld%d" % r, 96, 128)
-    for h in range(8):
-        o = B("win", 2560 * (h % 2), 2560 * (h % 2) + 1280, 1, (16 * h, 16 * h + 16))
-        dma("y", "zw", [B("zqc")], [o], view(o), T.x[16 * h:16 * h + 16, :])
-    dma("y", "dv", [], [B("vb")], view(B("vb")), T.v[:, :])
     dma("y", "dw", [], [B("wqc")], T.wqc[:, 0:512].bitcast(dt.uint8), T.wc[:, :])
     dma("y", "dw", [], [B("wqs")], view(B("wqs")), T.ws[:, :])
+    dma("y", "dv", [], [B("vb")], view(B("vb")), T.v[:, :])
 
     iota(B("pi"), [[1, 1]], 0, 1)
     iota(B("ulf"), [[16, 8]])
     iota(B("bm16"), [[0, 20], [1, 16]])
-    fill(B("one"), 1.0)
+    ts(B("one"), B("zb", 0, 512), 1.0, A.add, qs="s")
     cp(B("ul"), B("ulf"))
     quant("uq", 0, 128, "ub", 0)
     quant("qx0", 0, 320, "xb", 0)
     op({"v": 210.0}, [B("uqc"), B("ul")], [B("urc")], lambda e: e.tensor_copy(T.urc[:, 0:128].bitcast(dt.uint32), T.uqc[:, 0:128].bitcast(dt.uint32).indirect(view(B("ul")))))
     op({"s": 225.0}, [B("uqs"), B("ul")], [B("urs")], lambda e: e.activation(T.urs[:, 0:128], T.uqs[:, 0:128].indirect(view(B("ul"))), ACT.Copy))
-    for j, (s, m) in enumerate(((5, 3), (4, 1), (3, 1), (2, 1), (0, 3), (0, 15), (0, 7), (1, 63), (0, 1), (4, 7), (1, 3))):
+    for j, (s, m) in enumerate(FIELDS):
         ts(B("bi", j, j + 1), B("pi"), s, A.arith_shift_right, m, A.bitwise_and)
-    cp(B("cf", 0, 11), B("bi"))
-    KQ, HB, MI, S2, K0, I_, V_, PH, O_, G_, K1 = (cf(j) for j in range(11))
-    NB, HP, C8, CF_, N3, F1, FO, W8, VL, FN, FW = (cf(j) for j in range(11, 22))
-    t = [cf(j) for j in range(22, 40)]
+    cp(B("cf", 0, len(FIELDS)), B("bi"))
+    KQ, HB, MI, S2, K0, I_, V_, PH, O_, G_, K1, J1, SA, KH, Q1, GL = (cf(j) for j in range(16))
+    NMI, C8, CF_, CN, CW, N3, W8, VL, A16, O64, M8, RB, KA = (cf(j) for j in range(16, 29))
+    t = [cf(j) for j in range(31, 80)]
     ts(B("yc"), B("bm16", 0, 224), I_, A.subtract, -1e28, A.mult)
     ts(B("d0"), B("bm16", 0, 224), I_, A.is_le, -9e29, A.mult)
     ts(B("dr"), B("bm16", 0, 224), 0.0, A.is_gt)
     ts(B("dlb"), B("bm16", 0, 256), I_, A.is_gt, LOW8 + STEP8, A.mult)
     ts(B("dlb"), B("dlb"), -LOW8, A.add)
-    ts(B("dlf"), B("bm16"), I_, A.is_gt, LOW + STEP, A.mult)
-    ts(B("dlf"), B("dlf"), -LOW, A.add)
-    ts(NB, HB, -1.0, A.mult, 1.0, A.add)
-    ts(HP, HB, 4.0, A.mult, KQ, A.add)
+    ts(B("dlo"), B("bm16"), I_, A.is_gt, LOW + STEP, A.mult)
+    ts(B("dlf"), B("dlo"), -LOW, A.add)
+    ts(B("dlo"), B("dlo"), -LOW, A.add)
+    ts(NMI, MI, -1.0, A.mult, 1.0, A.add)
+    ts(M8, MI, 8.0, A.mult)
     ts(C8, I_, STEP8, A.mult, -15.0 * STEP8, A.add)
-    ts(CF_, I_, STEP + 1.0, A.mult, -15.0 * STEP, A.add)
-    for k, s, o, j in ((K0, S2, N3, 0), (K1, MI, t[8], 3)):
+    ts(CN, I_, STEP, A.mult, -15.0 * STEP, A.add)
+    ts(CF_, CN, I_, A.add)
+    ts(CW, CN, M8, A.add)
+    ts(KA, O_, 2.0, A.mult, MI, A.add)
+    for k, s, o, j in ((K0, S2, N3, 0), (K1, MI, t[9], 3), (KA, SA, t[10], 6)):
         ts(t[j], k, KQ, A.subtract, 4.0, A.mult)
         ts(t[j + 1], k, KQ, A.is_lt, 16.0, A.mult)
         ts(t[j + 2], s, 16.0, A.mult, t[j], A.add)
         ts(o, t[j + 2], t[j + 1], A.add)
-    ts(t[9], O_, 128.0, A.mult, 128.0, A.add)
-    ts(F1, t[9], t[8], A.add)
-    ts(t[10], MI, HB, A.not_equal, 320.0, A.mult)
-    ts(t[11], MI, HB, A.is_gt, 32.0, A.mult)
-    ts(FO, N3, t[10], A.add, t[11], A.add)
-    iota(B("i32"), [[32, 10]])
-    ts(B("otl"), B("i32"), FO, A.add)
-    ts(B("rll", 0, 8, 2), B("i32", 0, 4), N3, A.add)
-    ts(B("rll", 1, 8, 2), B("i32", 0, 4), F1, A.add)
-    cp(B("ptl"), N3)
-    iota(B("llf"), [[128, 2], [1, 8]])
+    iota(B("i32"), [[64, 2]])
+    ts(t[11], O_, 128.0, A.mult, t[9], A.add)
+    ts(t[27], Q1, 32.0, A.mult)
+    ts(B("rln"), B("i32"), N3, A.add, t[27], A.add)
+    ts(B("rlo"), B("i32"), t[11], A.add, t[27], A.add)
+    cp(B("ptn"), N3)
+    ts(B("pto"), S2, 32.0, A.mult, t[10], A.add)
+    iota(B("llf"), [[16, 2], [1, 8]])
     ts(t[12], I_, 8.0, A.mult)
-    ts(B("ll"), B("llf"), t[12], A.add)
-    ts(B("hl"), HP, 16.0, A.mult, I_, A.add)
-    ts(t[13], V_, 8.0, A.add)
-    ts(B("p4"), B("i32", 0, 2), 0.0, A.mult, t[13], A.add)
-    ts(FN, HP, 16.0, A.mult, C8, A.add)
-    ts(FW, C8, 112.0, A.add)
-    iota(B("cm"), [[16, 20]])
-    ts(B("cm"), B("cm"), CF_, A.add)
-    iota(B("oc0"), [[0, 20], [320, 8]], 1440)
-    ts(t[14], HB, -1280.0, A.mult)
-    ts(B("oc0"), B("oc0"), t[14], A.add)
+    ts(B("lln"), B("llf", 0, 8), t[12], A.add)
+    ts(t[13], O_, 8.0, A.mult)
+    ts(t[14], J1, 32.0, A.mult, t[13], A.add)
+    ts(B("llo"), B("llf"), t[14], A.add)
+    ts(t[18], V_, 8.0, A.add)
+    ts(t[19], V_, 24.0, A.add)
+    ts(B("p4", 0, 2), B("i32"), 0.0, A.mult, t[18], A.add)
+    ts(B("p4", 2, 4), B("i32"), 0.0, A.mult, t[19], A.add)
+    ts(t[20], KH, 16.0, A.mult)
+    ts(A16, HB, 32.0, A.mult, t[20], A.add)
+    ts(O64, O_, 64.0, A.mult)
+    ts(RB, GL, 320.0, A.mult, -159.75, A.add)
+    iota(B("i16"), [[16, 20]])
+    ts(B("cm"), B("i16"), CF_, A.add)
+    ts(t[21], HB, 320.0, A.mult)
+    ts(t[22], HB, -352.0, A.mult, 336.0, A.add)
+    ts(B("bs", 0, 20, 2), B("i16", 0, 20, 2), t[21], A.add)
+    ts(B("bs", 1, 20, 2), B("i16", 1, 20, 2), t[22], A.add)
+    tt(B("dlo", 15, 320, 16), B("dlo", 15, 320, 16), B("bs"), A.add)
+    iota(B("oc0"), [[0, 14], [32767, 2], [KEY, 8]], 160)
+    fill(B("oc", 88, 96), BIG), fill(B("oc", 312, 320), BIG)
     iota(B("sd"), [[1, 320]], -160)
-    fill(B("ob"), 0.0)
-    fill(B("mk", 0, 1024, 8), BIG)
+    fill(B("ob", 0, 16), 0.0), fill(B("ob", 336, 352), 0.0)
+    dma("y", "z1", [B("zb", 0, 320)], [B("ob", 16, 336)], view(B("ob", 16, 336)), view(B("zb", 0, 320)))
+    for n in ("mkn", "mko"):
+        fill(B(n, 0, 512, 16), BIG)
     fill(B("acl"), 0.0)
-    for n in ("xo", "xn", "opf"):
-        iota(B(n, 0, 16), [[0, 2], [1, 8]])
-    iota(B("opf", 112, 128), [[0, 2], [1, 8]])
-    iota(B("pfn", 0, 16), [[0, 2], [1, 4], [4, 2]])
-    iota(B("ico", 0, 128), [[16, 4], [16, 2], [1, 16]])
-    iota(B("ico", 128, 256), [[8, 4], [32, 2], [1, 16]])
+    fill(B("rw0"), 0.0)
+    iota(B("xo", 0, 32), [[0, 4], [1, 8]])
+    iota(B("xn", 0, 16), [[0, 2], [1, 8]])
+    iota(B("a2", 0, 64), [[16, 4], [0, 2], [1, 8]])
+    iota(B("h1"), [[1, 4], [0, 2]])
+    iota(B("h2"), [[0, 4], [16, 2]])
+    ts(B("h3"), B("h1"), KQ, A.subtract, 4.0, A.mult)
+    ts(B("h4"), B("h1"), KQ, A.is_lt, 16.0, A.mult)
+    tt(B("h3"), B("h3"), B("h2"), A.add)
+    tt(B("pfn", 0, 8), B("h3"), B("h4"), A.add)
+    iota(B("h5"), [[0, 2], [1, 4]])
+    iota(B("h6"), [[1, 2], [0, 4]])
+    ts(B("h7"), B("h5"), GL, A.subtract, 320.0, A.mult)
+    ts(B("h8"), B("h5"), GL, A.is_lt, 1280.0, A.mult)
+    ts(B("h6"), B("h6"), 0.5, A.mult)
+    tt(B("h7"), B("h7"), B("h6"), A.add)
+    tt(B("pfn", 8, 16), B("h7"), B("h8"), A.add)
+    for j in range(2):
+        iota(B("ico", j, 128, 2), [[16, 4], [1000, 2], [1, 8]], 8 * j)
+        iota(B("ico", 128 + j, 256, 2), [[16, 4], [-1000, 2], [1, 8]], 1016 + 8 * j)
+    iota(B("ico", 256, 384), [[8, 4], [32, 2], [1, 16]])
     ts(W8, O_, -7.0, A.mult, 8.0, A.add)
-    fill(B("cab", 3, 1024, 4), 0.0)
+    fill(B("cab", 3, 1536, 4), 0.0)
     for j, w in enumerate((4.0, 2.0, 1.0)):
         ts(t[15 + j], W8, w, A.mult)
-        ts(B("cab", j, 1024, 4), B("ico"), PH, A.is_equal, t[15 + j], A.mult)
-    quant("ca", 0, 256, "cab", 0)
+        ts(B("cab", j, 1536, 4), B("ico"), PH, A.is_equal, t[15 + j], A.mult)
+    quant("ca", 0, 384, "cab", 0)
     iota(B("m64"), [[1, 8], [0, 64]])
     ts(B("ccb"), B("m64"), G_, A.is_equal, -1.0, A.mult)
     quant("cc", 0, 128, "ccb", 0)
@@ -448,22 +486,22 @@ def rank_program(g, core, T, topo):
     ts(B("d8"), B("m8"), 0.0, A.is_gt)
     tt(B("cht"), B("chf"), B("k8"), A.mult)
     scan(B("chs"), B("d8"), B("cht"), A.mult, A.add)
-    ts(t[6], MI, -1.0, A.mult, 1.0, A.add)
-    ts(VL, V_, t[6], A.mult)
+    ts(VL, V_, NMI, A.mult)
     ts(B("lt"), B("chs", 7, 64, 8), MI, A.mult, VL, A.add)
     for a in range(8):
         cp(B("tf", 128 * a, 128 * a + 128), ("@", B("chf", 8 * a, 8 * a + 8), B("lt")))
     for a in range(4):
-        latch(B("tl", 256 * a, 256 * a + 256), B("tf", 256 * a, 256 * a + 256))
-    ts(t[7], C8, 8.0, A.add)
-    ts(B("tab"), B("tl", 15, 1024, 16), t[7], A.add)
-    ts(cf(41), HB, 16.0, A.mult, I_, A.add)
-    iota(B("i32b"), [[1, 32]])
-    ts(B("eye"), B("i32b"), cf(41), A.is_equal)
+        latch(B("tl", 256 * a, 256 * a + 256), B("tf", 256 * a, 256 * a + 256), B("dlb"))
+    for j in range(2):
+        ts(t[24 + j], C8, 8.0 + 16 * j, A.add)
+        ts(B("tab", 64 * j, 64 * j + 64), B("tl", 15, 1024, 16), t[24 + j], A.add)
+    ts(t[26], GL, 16.0, A.mult, I_, A.add)
+    iota(B("i64"), [[1, 64]])
+    ts(B("eye"), B("i64"), t[26], A.is_equal)
     for k in range(4):
-        for e in range(4):
-            q = (32 * k, 32 * k + 32)
-            cp(B("lb", 512 * k + 129 * e, 512 * k + 128 * e + 128, 4, q), B("eye", p=q), "s")
+        for e in range(2):
+            q = (64 * (k // 2), 64 * (k // 2) + 64)
+            cp(B("lb", 512 * k + 258 * e + k % 2, 512 * k + 256 * e + 256, 4, q), B("eye", p=q), "s")
     quant("lq", 0, 512, "lb", 0)
     for b in range(4):
         o = B("eb", 512 * b, 512 * b + 512)
@@ -472,54 +510,68 @@ def rank_program(g, core, T, topo):
     quant("vq", 0, 128, "vb", 0)
 
     def calls(p, x):
-        bq, at = "bq" + p, 0 if p == "o" else 8
-        for j, lo in enumerate((96, 192) if p == "o" else (0,)):
-            mm(1 + j, 128, x, lo, "uq", 0)
-            ts(B("bt", at + 4 * j, at + 4 * j + 3), ps(1 + j, 1, 4), 0.0, A.is_gt)
-        quant(bq, 0, 128, "bt", at)
-        mm(1, 128, "ca", 0 if p == "o" else 128, bq, 0)
         if p == "o":
-            ts(cf(40), ps(1, 1, 2), HB, A.mult, qs="v")
-            ts(B("ixo"), ps(1, 0, 1), NB, A.mult, cf(40), A.add)
+            for j, lo in enumerate((96, 192)):
+                mm(2 + j, 128, x, lo, "uq", 0)
+                ts(B("bt", 8 * j, 8 * j + 3), ps(2 + j, 1, 4), 0.0, A.is_gt)
+            quant("bqo", 0, 130, "bt", 0)
+            mm(1, 128, "ca", 0, "bqo", 0, True, False)
+            mm(1, 128, "ca", 128, "bqo", 2, False, True)
+            ts(B("ixo"), ps(1, 0, 1), O64, A.add)
+            cp(B("lio"), ("@", B("tab"), B("ixo")))
         else:
+            mm(1, 128, x, 0, "uq", 0)
+            ts(B("bt", 16, 19), ps(1, 1, 4), 0.0, A.is_gt)
+            quant("bqn", 0, 128, "bt", 16)
+            mm(1, 128, "ca", 256, "bqn", 0)
             cp(B("ixn"), ps(1, 0, 1))
-        cp(B("li" + p, 0, 32, 2), ("@", B("tab"), B("ix" + p)))
+            cp(B("lin", 0, 32, 2), ("@", B("tab"), B("ixn")))
 
     def pieces(p):
-        x, n, pf = "x" + p, 16 if p == "o" else 8, "opf" if p == "o" else "pfn"
-        for e in range(n):
-            cp(B(x, 16 * e + 16, 16 * e + 32), ("@", B(x, 16 * e, 16 * e + 16), B("li" + p, 2 * e, 2 * e + 1)), PIN["chain"])
-        cp(B("pp" + p), ("@", B(x, 16 * n, 16 * n + 16), B("p4")), PIN["chain"])
-        turn(B("to" + p), B("pp" + p))
-        share("to" + p, 32)
-        cp(B("lp" + p, 0, 32, 2), ("@", B("to" + p), B("ptl")))
-        for e in range(6):
-            cp(B(pf, 16 * e + 16, 16 * e + 32), ("@", B(pf, 16 * e, 16 * e + 16), B("lp" + p, 2 * e, 2 * e + 1)), PIN["chain"])
-        cp(B("z" + p), ("@", B(x, 16, 16 * n + 16), B("ll", 0, n)), PIN["rows"])
-        latch(B("w" + p), B("z" + p))
+        x, n = "x" + p, 2 if p == "o" else 1
+        w = 16 * n
+        for e in range(8):
+            cp(B(x, w * e + w, w * e + 2 * w), ("@", B(x, w * e, w * e + w), B("li" + p, 2 * e, 2 * e + n)), PIN["chain"])
+        last = ("@", B(x, 8 * w, 9 * w), B("p4", 0, 2 * n))
         if p == "o":
-            ts(B("fl", 8, 24), B("wo", 15, 256, 16), FW, A.add)
-            cp(B("xg"), ("@", B("opf"), B("hl")), PIN["rows"])
-            latch(B("xl"), B("xg"))
-            ts(B("lx"), B("xl", 15, 16), C8, A.add)
+            ts(B("ppo"), last, A16, A.add, qs=PIN["chain"])
         else:
-            ts(B("fl", 0, 8), B("wn", 15, 128, 16), FN, A.add)
-
-    def rows():
-        cp(B("pfn", 112, 128), ("@", B("pfn", 96, 112), B("lx")), PIN["chain"])
-        cp(B("rf", 0, 128), ("@", B("pfn"), B("fl", 0, 8)), PIN["rows"])
-        cp(B("rf", 128, 384), ("@", B("pfn"), B("fl", 8, 24)), PIN["rows"])
-        turn(B("rt"), B("rf"))
-        share("rt", 384)
-        cp(B("rr"), ("@", B("rt"), B("rll")), PIN["rows"])
+            cp(B("ppn"), last, PIN["chain"])
+        turn(B("to" + p), B("pp" + p))
+        share("to" + p, 2 * w)
+        if p == "o":
+            cp(B("lpo"), ("@", B("too"), B("pto")))
+            for j in range(4):
+                cp(B("a2", 64 * j + 64, 64 * j + 128), ("@", B("a2", 64 * j, 64 * j + 64), B("lpo", 4 * j, 4 * j + 4)), PIN["chain"])
+            latch(B("wa"), B("a2"), B("dlf"))
+            ts(B("l2", 0, 6, 2), B("wa", 271, 304, 16), CW, A.add)
+            for j in range(4):
+                ts(B("lf", j, 16, 4), B("wa", 64 * j + 15, 64 * j + 64, 16), CW, A.add)
+        else:
+            ts(B("lpn", 0, 32, 2), ("@", B("ton"), B("ptn")), M8, A.add)
+            for e in range(6):
+                cp(B("pfn", 16 * e + 16, 16 * e + 32), ("@", B("pfn", 16 * e, 16 * e + 16), B("lpn", 2 * e, 2 * e + 1)), PIN["chain"])
+            for a in range(3):
+                cp(B("pfn", 112 + 16 * a, 128 + 16 * a), ("@", B("pfn", 96, 112 + 16 * a), B("l2", 2 * a, 2 * a + 1)), PIN["chain"])
+            cp(B("pfo"), ("@", B("pfn", 96, 160), B("lf", 0, 14)), PIN["rows"])
+            for pf, lo, hi in (("pfn", 0, 96), ("pfo", 96, 320)):
+                latch(B("wl", lo, hi), B(pf, 0, hi - lo), B("dlo", lo, hi))
+                ts(B("otl", lo // 16, hi // 16), B("wl", lo + 15, hi, 16), CN, A.add, NMI, A.mult)
+                tt(B("oc", lo, hi - 8), B(pf, 8, hi - lo), B("oc0", 0, hi - lo - 8), A.add)
+        cp(B("z" + p), ("@", B(x, w, 9 * w), B("ll" + p)), PIN["rows"])
+        turn(B("rt" + p), B("z" + p))
+        share("rt" + p, 8 * w)
+        i = B("rr" + p)
+        cp(i, ("@", B("rt" + p), B("rl" + p)), PIN["rows"])
         for e in range(1, 8):
-            o, i = B("mk", e, 1024, 8), B("rr")
+            o = B("mk" + p, e, 512, 16)
 
-            def fn(q, o=o, i=i, e=e):
+            def fn(q, o=o, e=e):
                 if q is g.vector:
                     return q.tensor_scalar(view(o), view(i), float(e), BIG, A.is_ge, A.mult)
                 return q.activation(view(o), view(i), ACT.Relu, bias=BIG * (0.5 - e), scale=BIG)
             op(costs(PIN["mask"], o, [i]), [i], [o], fn)
+        ts(B("mk" + p, 8, 512, 16), i, -float(KEY), A.mult, qs=PIN["mask"])
 
     turns = []
 
@@ -539,13 +591,21 @@ def rank_program(g, core, T, topo):
         at, c0 = (GO if tile == "go" else GN)[q]
         return B(tile, at + 4 * (lo - c0) + e, at + 4 * (hi - c0), 4)
 
-    def compare(p, x):
+    def scores(p, x):
         bank, c0, n, w = (0, 96, 224, 224) if p == "o" else (2, 0, 96, 320)
         mm(bank, w, "ur", 0, x, c0)
         tt(B("y" + p), ps(bank, 0, n), B("yc", 0, n), A.add)
+        if p == "o":
+            cp(B("sco"), ps(bank, 0, n), "s")
         scan(B("so" + p), B("d0", 0, n), B("y" + p), A.add, A.max)
+
+    def compare(p):
+        c0, n = (96, 224) if p == "o" else (0, 96)
+
+        def row(lo, hi):
+            return B("sco", lo - c0, hi - c0) if p == "o" else ps(2, lo, hi)
         d = slot("g" + p, 0, 0, c0, c0 + n)
-        tt(d, ps(bank, 0, n), B("so" + p), A.is_gt)
+        tt(d, row(c0, c0 + n), B("so" + p), A.is_gt)
         scan(B("dcs", c0, c0 + n), B("dr", 0, n), d, A.mult, A.add)
         for k in range(13 if p == "o" else 6):
             lo = c0 + 16 * k + 16
@@ -553,45 +613,43 @@ def rank_program(g, core, T, topo):
                 o = slot("gn", k - 11, 3 * (k - 11), lo, 320)
             else:
                 o = slot("g" + p, (k + 1) // 4, (k + 1) % 4, lo, 320)
-            ts(o, ps(bank, lo - c0, w), B("so" + p, 16 * k + 15, 16 * k + 16), A.is_gt)
+            ts(o, row(lo, 320), B("so" + p, 16 * k + 15, 16 * k + 16), A.is_gt)
             count(o, B("acl", c0 // 16 + k, c0 // 16 + k + 1))
         for q, (at, lo) in enumerate(GO if p == "o" else GN):
             j = 320 * (q if p == "o" else 3 + q)
             quant("gq", j + lo, j + 320, "g" + p, at)
             mm(3, 320, "cc", 0, "gq", j, p == "o" and q == 0, p == "n" and q == 1)
 
-    def window(p, x):
+    def window(p, x, r):
         c0, n = (96, 224) if p == "o" else (0, 96)
         for k in range(4):
             mm(4 + k, max(n, 128), "lq", 128 * k, x, c0)
         for k in range(4):
-            cp(B("win", 1280 + 320 * k + c0, 1280 + 320 * k + c0 + n), ps(4 + k, 0, n), PIN["win"])
+            cp(B("win", 4 * c0 + k, 4 * (c0 + n), 4), ps(4 + k, 0, n), PIN["win"])
+        lo, hi = 4 * c0, 4 * (c0 + n)
+        for s in range(1, 4):
+            for h in (0, 64):
+                for d0, d1, s0 in ((0, 64 - 16 * s, 16 * s), (64 - 16 * s, 64, 0)):
+                    o, i = B("win", 1280 * s + lo, 1280 * s + hi, 1, (h + d0, h + d1)), B("win", lo, hi, 1, (h + s0, h + s0 + d1 - d0))
+                    dma("y", "s%s%d" % (p, r), [i], [o], view(o), view(i))
 
-    def swap(r):
-        for k in range(4):
-            for b in range(2):
-                d, s = 32 * k + 16 * b, 32 * k + 16 - 16 * b
-                o, i = B("win", 2560 - 2560 * b, 3840 - 2560 * b, 1, (d, d + 16)), B("win", 1280, 2560, 1, (s, s + 16))
-                dma("y", "sw%d" % r, [i], [o], view(o), view(i), 3500.0)
-
-    def early(r):
+    def one_round(r):
         x = "qx%d" % r
         calls("o", x)
-        compare("o", x)
-        window("o", x)
+        scores("o", x)
         pieces("o")
-
-    def late(r):
-        x = "qx%d" % r
+        if r:
+            arrive(r)
+        compare("o")
+        window("o", x, r)
         calls("n", x)
-        compare("n", x)
-        window("n", x)
-        swap(r)
+        scores("n", x)
+        compare("n")
+        window("n", x, r)
         pieces("n")
-        rows()
         tt(B("rc1"), B("dcs", 15, 320, 16), B("cm"), A.add)
         tt(B("rc2"), B("rc1"), B("acl"), A.add)
-        latch(B("cl"), ps(3, 0, 320), "dlf")
+        latch(B("cl"), ps(3, 0, 320), B("dlf"))
         tt(B("rkf"), B("cl", 15, 320, 16), B("rc2"), A.add)
         cp(B("rk"), B("rkf"))
         w = B("ob", 16, 336)
@@ -599,20 +657,21 @@ def rank_program(g, core, T, topo):
         turn(B("tr", 0, 320), w)
         turn(B("tr", 320, 672), B("ob"))
         share("tr", 672)
-        for lo, hi in ((0, 4), (4, 10)):
-            tt(B("ot", 16 * lo, 16 * hi), ("@", B("tr"), B("otl", lo, hi)), B("oc0", 16 * lo, 16 * hi), A.add)
-        for p, m0, n, at, l0 in (("n", 0, 6, 0, 0), ("o", 6, 14, 128, 24)):
-            for G in range(4):
-                o = 8 * (l0 + n * G)
-                scan(B("sc", o, o + 8 * n), B("mk", 256 * G + at, 256 * G + at + 8 * n), B("ot", 8 * m0, 8 * (m0 + n)), A.add, A.min)
-            cp(B("il", l0, l0 + 4 * n), B("sc", 8 * l0 + 7, 8 * (l0 + 4 * n), 8))
+        for p, m0, n, l0 in (("n", 0, 6, 0), ("o", 6, 14, 24)):
+            ot = B("ot", 16 * m0, 16 * (m0 + n))
+            tt(ot, ("@", B("tr"), B("otl", m0, m0 + n)), B("oc", 16 * m0, 16 * (m0 + n)), A.add)
+            for G in range(2):
+                o = 8 * l0 + 16 * n * G
+                scan(B("sc", o, o + 16 * n), B("mk" + p, 256 * G, 256 * G + 16 * n), ot, A.add, A.min)
+            for e in range(2):
+                ts(B("il", l0 + 2 * n * e, l0 + 2 * n * (e + 1)), B("sc", 8 * l0 + 15, 8 * l0 + 32 * n, 16), 4.0, A.mult, float(e), A.add)
             step = 12 if p == "n" else 14
             for l in range(l0, l0 + 4 * n, step):
                 cp(B("st", 16 * l, 16 * (l + step)), ("@", B("win"), B("il", l, l + step)), PIN["pick"])
-            for G in range(4):
-                for e in range(4):
-                    o = B("ta" if p == "n" else "tb", 64 * m0 + e, 64 * (m0 + n), 4, (32 * G, 32 * G + 32))
-                    cp(o, B("st", 16 * (l0 + n * G), 16 * (l0 + n * G + n), 1, (32 * e, 32 * e + 32)), PIN["lay"])
+            for e in range(4):
+                for G in range(2):
+                    o, l = B("ta" if p == "n" else "tb", 64 * m0 + e, 64 * (m0 + n), 4, (64 * G, 64 * G + 64)), l0 + n * (2 * (e % 2) + G)
+                    cp(o, B("st", 16 * l, 16 * (l + n), 1, (64 * (e // 2), 64 * (e // 2) + 64)), PIN["lay"])
             if p == "n":
                 quant("qs%d" % (r + 1), 0, 128, "ta", 0)
                 send(r + 1)
@@ -633,24 +692,24 @@ def rank_program(g, core, T, topo):
                     o, i = o.bitcast(dt.uint8), i.bitcast(dt.uint8)
                 g.remote_dma(o, i, T.sem["rc%d" % r], T.sem["ls"], pid, rid, m)
                 K["total"]["ls"] = K["total"].get("ls", 0) + len(topo.engines(core, dst))
-        raw("g", [B(t + "c", 0, 96), B(t + "s", 0, 96)], [("sent%d" % r, 0, 1, 1, 0, 128)], fn, 600.0, 2000.0)
+        raw("g", [B(t + "c", 0, 96), B(t + "s", 0, 96)], [("sent%d" % r, 0, 1, 1, 0, 128)], fn, 600.0, 1200.0, 800.0)
 
     def arrive(r):
         frm = T.cores[(rank - r) % len(T.cores)]
         n = 2 * len(topo.engines(frm, core))
-        raw("t", [("sent%d" % r, 0, 1, 1, 0, 128)], [B("ld%dc" % r, 0, 96), B("ld%ds" % r, 0, 96)], lambda: K["wait"]("t", "rc%d" % r, n, {}), 1.0, 0.0)
+        raw("t", [("sent%d" % r, 0, 1, 1, 0, 128)], [B("ld%dc" % r, 0, 96), B("ld%ds" % r, 0, 96)], lambda: K["wait"]("t", "rc%d" % r, n, {}), 1.0)
         for b in range(4):
-            a = 1 + b % 2
             mm(4 + b, 128, "wq", 128 * b, "ld%d" % r, 0)
-            mm(a, 128, "eq", 128 * b, "ld%d" % r, 0)
+            mm((3, 2, 0, 1)[b], 128, "eq", 128 * b, "ld%d" % r, 0)
+        for b in range(4):
             o, i = B("rl", 96 * b, 96 * b + 96), ps(4 + b, 0, 96)
 
             def fn(e, o=o, i=i):
                 if e is g.vector:
                     return e.tensor_scalar(view(o), view(i), 0.0, 0.03125, A.max, A.mult)
                 return e.activation(view(o), view(i), ACT.Relu, scale=0.03125)
-            op(costs("s", o, [i]), [i], [o], fn)
-            tt(B("tb", b, 384, 4), o, ps(a, 0, 96), A.add)
+            op(costs(PIN["relu"], o, [i]), [i], [o], fn)
+            tt(B("tb", b, 384, 4), o, ps((3, 2, 0, 1)[b], 0, 96), A.add)
         quant("qx%d" % r, 0, 128, "tb", 0)
 
     def store(lo, hi, bank):
@@ -659,23 +718,26 @@ def rank_program(g, core, T, topo):
         cp(B("yb", lo, hi), ps(bank, 0, hi - lo))
         dma("s" if lo == 0 else "y", "out", [B(x + "c", lo, hi)], [], T.oc[:, 4 * lo:4 * hi], view(B(x + "c", lo, hi)).bitcast(dt.uint8))
         for k in range(4):
-            dma("y", "out", [B(x + "s", lo, hi)], [], T.osc[4 * k:4 * k + 4, lo:hi], T[x + "s"][32 * k:32 * k + 4, lo:hi])
+            dma("y", "out", [B(x + "s", lo, hi, 1, (32 * k, 32 * k + 4))], [], T.osc[4 * k:4 * k + 4, lo:hi], T[x + "s"][32 * k:32 * k + 4, lo:hi])
         dma("y", "out", [B("yb", lo, hi)], [], T.y[:, lo:hi], T.yb[:, lo:hi])
 
-    early(0)
-    late(0)
-    for r in (1, 2):
-        early(r)
-        arrive(r)
-        late(r)
-    q0 = (0, 32)
-    turn(B("rwt", p=q0), B("rr", p=q0))
-    ts(B("rw1", p=q0), B("rwt", p=q0), 4.0, A.is_ge, -7.0, A.mult)
-    ts(B("rw2", p=q0), B("rwt", p=q0), 2.0, A.mult)
-    tt(B("rwb", p=q0), B("rw1", p=q0), B("rw2", p=q0), A.add)
+    for r in range(ROUNDS):
+        one_round(r)
+    for m0, n, l0 in ((0, 6, 0), (6, 14, 24)):
+        for G in range(2):
+            o = 8 * l0 + 16 * n * G
+            cp(B("rw0", 32 * G + m0, 32 * G + m0 + n), B("sc", o + 15, o + 16 * n, 16))
+    ts(B("rw1"), B("rw0"), RB, A.add, 1.0 / 320, A.mult)
+    ts(B("rw2"), B("rw0"), 2.0, A.mult)
+    for n, f, m in (("rwi", "rw1", 3), ("rwj", "rw2", 1)):
+        cp(B(n), B(f))
+        ts(B(n), B(n), m, A.bitwise_and)
+    ts(B("rw3"), B("rwj"), 4.0, A.mult)
+    tt(B("rw3"), B("rw3"), B("rwi"), A.add)
+    turn(B("rwb"), B("rw3"))
     for h in range(8):
-        dma("y", "out", [B("rwb")], [], T.rw[h, 0:96], T.rwb[0:6, 16 * h:16 * h + 16])
-        dma("y", "out", [B("rwb")], [], T.rw[h, 96:320], T.rwb[16:30, 16 * h:16 * h + 16])
+        q, c = 32 * (h // 2 % 2), 32 * (h // 4) + 16 * (h % 2)
+        dma("y", "out", [B("rwb", c, c + 16, 1, (q, q + 20))], [], T.rw[h, :], T.rwb[q:q + 20, c:c + 16])
     store(128, 320, 0)
     arrive(3)
     store(0, 128, 1)

@@ -2,12 +2,18 @@ import numpy as np
 from concourse.mybir import dt, AluOpType, AxisListType, ActivationFunctionType
 
 CY = 0.83
-SLACK, HOP, WORSE, TRIES = 60.0, 200.0, 0.5, 600
+SLACK, HOP, WORSE, TRIES = 0.0, 200.0, 0.5, 1500
+SPAN, SIGMA, HEAT = 30, 300.0, 100.0
+ALONE = (0, 1)
+MORE = [3000.0, 0.0, 0.0]
+IDLE = 3.0
+SCAN = (9, 10, 11, 12, 13)
+DEAR = {"v": 2.0, "s": 1.0, "g": 1.0}
 ROUNDS = 3
-STEP, LOW = 4096.0, 131072.0
+STEP, LOW = 65536.0, 2097152.0
 STEP8, LOW8 = 8.0, 256.0
-BIG, KEY = 65536.0, 4096
-FIELDS = ((5, 3), (4, 1), (3, 1), (2, 1), (0, 3), (0, 15), (0, 7), (1, 63), (0, 1), (4, 7), (1, 3), (1, 7), (1, 1), (6, 1), (5, 1), (4, 3))
+BIG, KEY, HUGE = 65536.0, 4096, 2.0 ** 92
+FIELDS = ((5, 2), (4, 1), (3, 1), (2, 1), (0, 2), (0, 4), (0, 3), (1, 6), (0, 1), (4, 3), (1, 2), (1, 3), (1, 1), (6, 1), (5, 1), (4, 2))
 F32, BF, I32, U16 = "float32", "bfloat16", "int32", "uint16"
 CODE, SC = "float8_e4m3fn_x4", "uint8"
 SIZE = {F32: 4, BF: 2, I32: 4, U16: 2, CODE: 4, SC: 1}
@@ -28,10 +34,10 @@ def _scratch():
     for b in range(8):
         d["ps%d" % b] = ("psum", [128, 512], F32)
     for n, w in (("xb", 1280), ("ub", 512), ("vb", 512), ("eb", 2048), ("lb", 2048), ("zb", 768), ("ccb", 512), ("cab", 1536), ("one", 512),
-                 ("bt", 528), ("eye", 64), ("i64", 64), ("ta", 512), ("tb", 1280), ("st", 1280), ("win", 5120), ("go", 2048), ("gn", 2304), ("jk", 1280),
-                 ("m64", 512), ("ico", 384), ("mkn", 512), ("mko", 512)):
+                 ("bt", 528), ("li", 512), ("ta", 512), ("tb", 1280), ("st", 1280), ("win", 5120), ("go", 2048), ("gn", 2304), ("jk", 1280),
+                 ("m64", 512), ("ico", 384), ("mk", 1024)):
         sb(n, w, BF)
-    for n, w in (("uq", 128), ("ur", 128), ("vq", 128), ("eq", 512), ("lq", 512), ("zq", 192), ("wq", 512), ("cc", 128), ("ca", 384), ("bqo", 130),
+    for n, w in (("uq", 128), ("ur", 128), ("vq", 128), ("eq", 512), ("lq", 512), ("wq", 512), ("cc", 128), ("ca", 384), ("bqo", 130),
                  ("bqn", 128), ("gq", 1600)):
         mx(n, w)
     for r in range(ROUNDS + 1):
@@ -39,18 +45,18 @@ def _scratch():
         if r:
             mx("ld%d" % r, 128)
             mx("qs%d" % r, 128)
-    sb("pi", 1, I32), sb("bi", len(FIELDS), I32), sb("chi", 64, I32), sb("chb", 64, I32), sb("rwi", 64, I32), sb("rwj", 64, I32)
-    for n, w in (("cf", 80), ("ulf", 8), ("i32", 2), ("llf", 16), ("cm", 20), ("i16", 20), ("bs", 20), ("oc0", 224), ("oc", 320), ("dlf", 320), ("dlo", 320),
+    sb("bi", 7, I32), sb("pi", 1), sb("half", 7), sb("pw", 7), sb("fl", 7), sb("chi", 64, I32), sb("chb", 64, I32), sb("rwi", 64, I32), sb("rwj", 64, I32)
+    for n, w in (("cf", 80), ("ulf", 8), ("i32", 2), ("llf", 16), ("cm", 20), ("i16", 20), ("bs", 20), ("oc0", 240), ("oc", 96), ("dlf", 320), ("dlo", 320),
                  ("yc", 224), ("d0", 224), ("chf", 64), ("m8", 64), ("k8", 64), ("d8", 64), ("cht", 64), ("chs", 64), ("yo", 224), ("soo", 224), ("sco", 224),
                  ("yn", 96), ("son", 96), ("acl", 20), ("rc1", 20), ("rc2", 20), ("cl", 320), ("rkf", 20), ("ot", 320), ("sc", 640), ("rl", 384),
-                 ("yb", 320), ("rw0", 64), ("rw1", 64), ("rw2", 64), ("rw3", 64), ("rwb", 64), ("wa", 320), ("wl", 320), ("h1", 8), ("h2", 8),
-                 ("h3", 8), ("h4", 8), ("h5", 8), ("h6", 8), ("h7", 8), ("h8", 8), ("pfn", 160), ("pfo", 224)):
+                 ("yb", 320), ("rw0", 64), ("rw1", 64), ("rw2", 64), ("rw3", 64), ("rwb", 64), ("wl", 320), ("h1", 8), ("h2", 8),
+                 ("h3", 8), ("h4", 8), ("h5", 8), ("h6", 8), ("h7", 8), ("h8", 8), ("pfn", 160), ("pfo", 232), ("a16", 64), ("rc3", 20)):
         sb(n, w)
-    for n, w in (("bm16", 320), ("dr", 224), ("dlb", 256), ("sd", 320), ("ob", 352), ("tr", 672), ("dcs", 320), ("tf", 1024), ("tl", 1024), ("tab", 128),
-                 ("xo", 288), ("xn", 144), ("ppo", 64), ("ppn", 32), ("too", 64), ("ton", 32), ("a2", 320),
-                 ("zo", 256), ("zn", 128), ("rto", 256), ("rtn", 128), ("rro", 32), ("rrn", 32)):
+    for n, w in (("bm16", 320), ("dr", 224), ("dlb", 320), ("sd", 320), ("ob", 352), ("tr", 672), ("dcs", 320), ("tf", 1024), ("tl", 1024), ("tab", 128),
+                 ("xo", 288), ("xn", 144), ("a2", 320),
+                 ("zo", 320), ("zn", 160), ("rto", 320), ("rtn", 160), ("rr", 64), ("jv", 6080), ("sg", 416), ("wa", 320)):
         sb(n, w, BF + "*")
-    for n, w in (("ul", 8), ("otl", 20), ("rlo", 2), ("rln", 2), ("pto", 1), ("ptn", 1), ("llo", 16), ("lln", 8), ("p4", 4), ("lt", 8), ("ixo", 1), ("ixn", 1),
+    for n, w in (("ul", 8), ("otl", 20), ("rll", 4), ("pto", 1), ("ptn", 1), ("llo", 20), ("lln", 10), ("lt", 8), ("ixo", 1), ("ixn", 1),
                  ("lio", 16), ("lin", 32), ("lpo", 16), ("lpn", 32), ("l2", 6), ("lf", 16), ("rk", 20), ("il", 80)):
         sb(n, w, U16)
     return d
@@ -91,7 +97,7 @@ def _plan(jobs):
         j = jobs[i]
         way[i] = min(j["c"].values()) + j["lat"] + (j["dur"] if j["sem"] in ("raw", "out") else both[j["sem"]]) + max([way[k] + HOP for k in after[i]] or [0.0])
 
-    def once(prio):
+    def once(prio, lean):
         free, fin, left = {q: 0.0 for q in "vtsgy"}, [0.0] * n, [len(j["pre"]) for j in jobs]
         t0, order, engines = [0.0] * n, [], 0.0
         ready = [i for i in range(n) if not left[i]]
@@ -99,16 +105,23 @@ def _plan(jobs):
             best = None
             for i in ready:
                 c, t = jobs[i]["c"], t0[i]
-                if len(c) == 1:
-                    qs = c
+                if len(c) == 1 or lean[i]:
+                    qs = lean[i] or c
                 else:
-                    ev, es = max(free["v"], t) + c["v"], max(free["s"], t) + c["s"]
-                    qs = "s" if ev > es + WORSE * c["v"] else "v" if es > ev + WORSE * c["s"] else "vs"
+                    ends = {q: max(free[q], t) + c[q] * DEAR[q] for q in c}
+                    soonest = min(ends.values())
+                    qs = [q for q in c if ends[q] <= soonest + WORSE * c[q]]
                 for q in qs:
                     key = (max(free[q], t - SLACK), -prio[i])
                     if best is None or key < best[0]:
                         best = (key, i, q)
             key, i, q = best
+            s = max(free[q], t0[i])
+            e = s + jobs[i]["c"][q]
+            for k in ready:
+                if s < t0[k] < e and prio[k] > prio[i] and q in jobs[k]["c"] and lean[k] in ("", q) and (len(jobs[k]["c"]) == 1 or lean[k]):
+                    if max(t0[k] + prio[k], t0[k] + jobs[k]["c"][q] + prio[i]) + IDLE * (t0[k] - s) < max(s + prio[i], e + prio[k]):
+                        i, e = k, t0[k]
             j = jobs[i]
             ready.remove(i)
             free[q] = fin[i] = max(free[q], t0[i]) + j["c"][q]
@@ -117,20 +130,39 @@ def _plan(jobs):
             order.append((i, q))
             for k in after[i]:
                 left[k] -= 1
-                t0[k] = max(t0[k], fin[i] + HOP)
+                t0[k] = max(t0[k], fin[i] + (0.0 if q == "t" and "t" in jobs[k]["c"] else HOP))
                 if not left[k]:
                     ready.append(k)
         return max(fin), order
+    way = [w + j.get("more", 0.0) for w, j in zip(way, jobs)]
     rng = np.random.RandomState(1)
-    best, prio = once(way), way
-    for _ in range(TRIES):
-        lo = rng.randint(n)
-        trial = list(prio)
-        for i in range(lo, min(n, lo + n // 6)):
-            trial[i] += float(rng.normal()) * 300.0
-        got = once(trial)
-        if got[0] <= best[0]:
-            best, prio = got, trial
+    alike = {}
+    for i, j in enumerate(jobs):
+        alike.setdefault(tuple((a[0].rstrip("cs").rstrip("0123") if a[0][0] in "ql" else a[0],) + a[1:] for a in j["w"] + j["r"]), []).append(i)
+    alike = list(alike.values())
+    either = [a for a in alike if len(jobs[a[0]]["c"]) > 1]
+    prio, lean = way, [""] * n
+    best = now = once(prio, lean)
+    for step in range(TRIES):
+        p2, l2 = list(prio), list(lean)
+        one = rng.randint(6)
+        if step % 2:
+            lo = rng.randint(len(alike))
+            for a in alike[lo:lo + rng.randint(1, SPAN)]:
+                d = float(rng.normal()) * SIGMA
+                for i in (a if one > 2 else a[one:one + 1]):
+                    p2[i] += d
+        else:
+            lo = rng.randint(len(either))
+            for a in either[lo:lo + rng.randint(1, 4)]:
+                q = ([""] + list(jobs[a[0]]["c"]))[rng.randint(len(jobs[a[0]]["c"]) + 1)]
+                for i in (a if one > 2 else a[one:one + 1]):
+                    l2[i] = q
+        got = once(p2, l2)
+        if got[0] <= now[0] + HEAT * (1.0 - step / TRIES):
+            now, prio, lean = got, p2, l2
+            if got[0] < best[0]:
+                best = got
     return best
 
 
@@ -205,6 +237,10 @@ def _make(g, T):
     def raw(q, reads, writes, fn, cost, lat=0.0, dur=0.0):
         jobs.append(dict(c={q: cost}, r=reads, w=writes, fn=fn, lat=lat, dur=dur, sem="raw"))
 
+    def sooner(count, ns):
+        for j in jobs[-count:]:
+            j["more"] = ns
+
     def run():
         table, groups = {}, {}
         for i, j in enumerate(jobs):
@@ -244,7 +280,7 @@ def _make(g, T):
                 total[sem] = total.get(sem, 0) + 1
                 j["fn"](queues[q]).then_inc(T.sem[sem], 1)
             note(q, j["r"], j["w"], sem, total[sem])
-    return dict(view=view, wait=wait, need=need, op=op, dma=dma, raw=raw, run=run, total=total)
+    return dict(view=view, wait=wait, need=need, op=op, dma=dma, raw=raw, run=run, total=total, sooner=sooner)
 
 
 def rank_program(g, core, T, topo):
@@ -320,8 +356,8 @@ def rank_program(g, core, T, topo):
             return e.activation(view(out), iv, ACT.Copy)
         op(costs(qs if kind(out) in (F32, BF) and kind(in_) in (F32, BF) else "v", out, [in_]), ir, [out], fn)
 
-    def scan(out, d0, d1, o0, o1):
-        op({"v": vc(out, [d0, d1])}, [d0, d1], [out], lambda e: e.tensor_tensor_scan(view(out), view(d0), view(d1), 0.0, o0, o1))
+    def scan(out, d0, d1, o0, o1, first=0.0):
+        op({"v": vc(out, [d0, d1])}, [d0, d1], [out], lambda e: e.tensor_tensor_scan(view(out), view(d0), view(d1), first, o0, o1))
 
     def latch(out, d1, d):
         scan(out, d, d1, A.add, A.max)
@@ -337,7 +373,12 @@ def rank_program(g, core, T, topo):
             cp(B(n, 4, w, 8, (32 * k, 32 * k + 32)), B(n, 0, w, 8, (32 * k1, 32 * k1 + 32)), PIN["shift"])
 
     def fill(out, x):
-        op({"v": vc(out, [])}, [], [out], lambda e: e.memset(view(out), x))
+        if x != int(x):
+            return op({"v": vc(out, [])}, [], [out], lambda e: e.memset(view(out), x))
+        op({"v": vc(out, []), "g": 130 + 2 * CY * width(out)}, [], [out], lambda e: e.memset(view(out), x) if e is g.vector else same(out, x))
+
+    def same(out, x):
+        return g.iota(view(out), [[0, width(out)]], int(x), 0, allow_small_or_imprecise_dtypes=True)
 
     def iota(out, pat, base=0, cm=0):
         if kind(out) == I32:
@@ -354,31 +395,48 @@ def rank_program(g, core, T, topo):
         o = ps(bank, 0, n)
         op({"t": 0.6 * (n + 16)}, [lc, ls, rc, rs], [o], lambda e: e.matmul_mx(view(o), view(lc), view(ls), view(rc), view(rs), start, stop))
 
-    def zero_codes(q, sem, n, lo, hi):
-        dma(q, sem, [B("zqc", 0, hi - lo)], [B(n + "c", lo, hi)], view(B(n + "c", lo, hi)).bitcast(dt.uint8), view(B("zqc", 0, hi - lo)).bitcast(dt.uint8))
-        dma(q, sem, [B("zqs", 0, hi - lo)], [B(n + "s", lo, hi)], view(B(n + "s", lo, hi)), view(B("zqs", 0, hi - lo)))
+    def bits(a):
+        return view(a).bitcast(dt.uint8) if kind(a) == CODE else view(a)
 
-    dma("y", "dc", [], [B("chi", p=(0, 1))], T.chi[0:1, 0:64], T.ch[:, :])
+    def clear(out):
+        z = B("zb", 0, width(out))
+        op({"v": vc(out, []), "s": ac(out, []), "g": 130 + 2 * CY * width(out)}, [z], [out],
+           lambda e: same(out, 0) if e is g else e.memset(view(out), 0.0) if e is g.vector else e.activation(view(out), view(z), ACT.Copy))
+
+    def act(out, in_, f, bias=0.0, scale=1.0):
+        x, r = sc(bias)
+        op(costs("s", out, [in_]), [in_] + r, [out], lambda e: e.activation(view(out), view(in_), f, bias=x, scale=scale))
+
+    dma("s", "dc", [], [B("chi", p=(0, 1))], T.chi[0:1, 0:64], T.ch[:, :])
     dma("y", "dx", [], [B("xb")], view(B("xb")), T.x[:, :])
-    dma("s", "du", [], [B("ub")], view(B("ub")), T.u[:, :])
+    dma("y", "du", [], [B("ub")], view(B("ub")), T.u[:, :])
     fill(B("zb"), 0.0)
-    quant("zq", 0, 192, "zb", 0)
-    for lo, hi in ((0, 96), (320, 480), (640, 832), (1280, 1344)):
-        zero_codes("y", "z4", "gq", lo, hi)
-    for lo in range(0, 2048, 768):
-        cp(B("lb", lo, min(lo + 768, 2048)), B("zb", 0, min(768, 2048 - lo)), "s")
+    quant("gq", 640, 832, "zb", 0)
+    for lo, hi in ((0, 96), (320, 480), (1280, 1344)):
+        for k in "cs":
+            o, i = B("gq" + k, lo, hi), B("gq" + k, 640, 640 + hi - lo)
+            dma("y", "z4", [i], [o], bits(o), bits(i))
     for a in (B("go", 0, 192), B("go", 896, 1088), B("go", 1536, 1856), B("gn", 0, 192), B("gn", 384, 1152, 4), B("gn", 1280, 1408), B("gn", 1283, 2240, 4),
               B("ta", 384, 512), B("bt")):
-        fill(a, 0.0)
-    for n in ("mkn", "mko"):
-        dma("y", "z1", [B("zb", 0, 512)], [B(n)], view(B(n)), view(B("zb", 0, 512)))
-    for r in range(1, ROUNDS + 1):
-        zero_codes("y", "z5", "ld%d" % r, 96, 128)
-    dma("y", "dw", [], [B("wqc")], T.wqc[:, 0:512].bitcast(dt.uint8), T.wc[:, :])
-    dma("y", "dw", [], [B("wqs")], view(B("wqs")), T.ws[:, :])
-    dma("y", "dv", [], [B("vb")], view(B("vb")), T.v[:, :])
+        clear(a)
+    clear(B("mk", 0, 512)), clear(B("mk", 512, 1024))
+
+    def beside(r, sem, after):
+        for k in "cs":
+            o, i = B("ld%d%s" % (r, k), 96, 128), B("gq" + k, 640, 672)
+            dma("y", sem, [i] + after, [o], bits(o), bits(i))
+    beside(1, "z1", [])
+    dma("y", "dw", [B("gqc", 640, 672)], [B("wqc")], T.wqc[:, 0:512].bitcast(dt.uint8), T.wc[:, :])
+    dma("y", "dw", [B("gqc", 640, 672)], [B("wqs")], view(B("wqs")), T.ws[:, :])
+
+    def later_loads():
+        after = [B("qx1c", 0, 96)]
+        beside(2, "z5", after), beside(3, "z5", after)
+        dma("y", "dv", after, [B("vb")], view(B("vb")), T.v[:, :])
+        quant("vq", 0, 128, "vb", 0)
 
     iota(B("pi"), [[1, 1]], 0, 1)
+    fill(B("half"), 0.5)
     iota(B("ulf"), [[16, 8]])
     iota(B("bm16"), [[0, 20], [1, 16]])
     ts(B("one"), B("zb", 0, 512), 1.0, A.add, qs="s")
@@ -387,26 +445,34 @@ def rank_program(g, core, T, topo):
     quant("qx0", 0, 320, "xb", 0)
     op({"v": 210.0}, [B("uqc"), B("ul")], [B("urc")], lambda e: e.tensor_copy(T.urc[:, 0:128].bitcast(dt.uint32), T.uqc[:, 0:128].bitcast(dt.uint32).indirect(view(B("ul")))))
     op({"s": 225.0}, [B("uqs"), B("ul")], [B("urs")], lambda e: e.activation(T.urs[:, 0:128], T.uqs[:, 0:128].indirect(view(B("ul"))), ACT.Copy))
-    for j, (s, m) in enumerate(FIELDS):
-        ts(B("bi", j, j + 1), B("pi"), s, A.arith_shift_right, m, A.bitwise_and)
-    cp(B("cf", 0, len(FIELDS)), B("bi"))
-    KQ, HB, MI, S2, K0, I_, V_, PH, O_, G_, K1, J1, SA, KH, Q1, GL = (cf(j) for j in range(16))
-    NMI, C8, CF_, CN, CW, N3, W8, VL, A16, O64, M8, RB, KA = (cf(j) for j in range(16, 29))
+    scan(B("pw"), B("half"), B("zb", 0, 7), A.mult, A.add, 2.0)
+    ts(B("pw"), B("pw"), B("pi"), A.mult, -0.49, A.add, qs="v")
+    cp(B("bi"), B("pw"))
+    cp(B("fl"), B("bi"))
+
+    def field(j, s, w):
+        if s + w == 7:
+            return B("fl", s, s + 1)
+        ts(cf(j), B("fl", s + w, s + w + 1), -float(1 << w), A.mult, B("fl", s, s + 1), A.add)
+        return cf(j)
+    KQ, HB, MI, S2, K0, I_, V_, PH, O_, G_, K1, J1, SA, KH, Q1, GL = (field(j, s, w) for j, (s, w) in enumerate(FIELDS))
+    NMI, C8, CF_, CN, CW, N3, W8, VL, A16, O64, M8, RB, KA, CO = (cf(j) for j in range(16, 30))
     t = [cf(j) for j in range(31, 80)]
-    ts(B("yc"), B("bm16", 0, 224), I_, A.subtract, -1e28, A.mult)
-    ts(B("d0"), B("bm16", 0, 224), I_, A.is_le, -9e29, A.mult)
-    ts(B("dr"), B("bm16", 0, 224), 0.0, A.is_gt)
-    ts(B("dlb"), B("bm16", 0, 256), I_, A.is_gt, LOW8 + STEP8, A.mult)
+    ts(t[30], I_, HUGE, A.mult)
+    ts(t[31], I_, 4 * HUGE, A.mult, 2 * HUGE, A.add)
+    act(B("yc"), B("bm16", 0, 224), ACT.Abs, t[30], -HUGE)
+    act(B("d0"), B("bm16", 0, 224), ACT.Relu, t[31], -4 * HUGE)
+    act(B("dr"), B("bm16", 0, 224), ACT.Sign)
+    ts(B("dlb"), B("bm16"), I_, A.is_gt, LOW8 + STEP8, A.mult)
     ts(B("dlb"), B("dlb"), -LOW8, A.add)
-    ts(B("dlo"), B("bm16"), I_, A.is_gt, LOW + STEP, A.mult)
-    ts(B("dlf"), B("dlo"), -LOW, A.add)
-    ts(B("dlo"), B("dlo"), -LOW, A.add)
+    ts(B("dlf"), B("dlb"), STEP / STEP8, A.mult)
+    ts(B("dlo"), B("dlb"), STEP / STEP8, A.mult)
     ts(NMI, MI, -1.0, A.mult, 1.0, A.add)
     ts(M8, MI, 8.0, A.mult)
     ts(C8, I_, STEP8, A.mult, -15.0 * STEP8, A.add)
     ts(CN, I_, STEP, A.mult, -15.0 * STEP, A.add)
     ts(CF_, CN, I_, A.add)
-    ts(CW, CN, M8, A.add)
+    ts(CW, C8, M8, A.add)
     ts(KA, O_, 2.0, A.mult, MI, A.add)
     for k, s, o, j in ((K0, S2, N3, 0), (K1, MI, t[9], 3), (KA, SA, t[10], 6)):
         ts(t[j], k, KQ, A.subtract, 4.0, A.mult)
@@ -414,22 +480,24 @@ def rank_program(g, core, T, topo):
         ts(t[j + 2], s, 16.0, A.mult, t[j], A.add)
         ts(o, t[j + 2], t[j + 1], A.add)
     iota(B("i32"), [[64, 2]])
+    fill(B("ob", 0, 16), 0.0), fill(B("ob", 336, 352), 0.0)
     ts(t[11], O_, 128.0, A.mult, t[9], A.add)
-    ts(t[27], Q1, 32.0, A.mult)
-    ts(B("rln"), B("i32"), N3, A.add, t[27], A.add)
-    ts(B("rlo"), B("i32"), t[11], A.add, t[27], A.add)
+    ts(t[27], Q1, 32.0, A.mult, 64.0, A.add)
+    ts(t[28], N3, 288.0, A.add)
+    ts(B("rll", 0, 2), B("i32"), t[11], A.add, t[27], A.add)
+    ts(B("rll", 2, 4), B("i32"), t[28], A.add, t[27], A.add)
     cp(B("ptn"), N3)
     ts(B("pto"), S2, 32.0, A.mult, t[10], A.add)
     iota(B("llf"), [[16, 2], [1, 8]])
     ts(t[12], I_, 8.0, A.mult)
-    ts(B("lln"), B("llf", 0, 8), t[12], A.add)
+    ts(B("lln", 2, 10), B("llf", 0, 8), t[12], A.add)
     ts(t[13], O_, 8.0, A.mult)
     ts(t[14], J1, 32.0, A.mult, t[13], A.add)
-    ts(B("llo"), B("llf"), t[14], A.add)
-    ts(t[18], V_, 8.0, A.add)
-    ts(t[19], V_, 24.0, A.add)
-    ts(B("p4", 0, 2), B("i32"), 0.0, A.mult, t[18], A.add)
-    ts(B("p4", 2, 4), B("i32"), 0.0, A.mult, t[19], A.add)
+    ts(B("llo", 4, 20), B("llf"), t[14], A.add)
+    for o, at in ((B("lln", 0, 2), 120.0), (B("llo", 0, 2), 232.0), (B("llo", 2, 4), 248.0)):
+        ts(o, B("ob", 0, 2), V_, A.add, at, A.add)
+    iota(B("a16", 0, 32), [[0, 2], [16, 4], [0, 4]])
+    fill(B("a16", 32, 64), 0.0)
     ts(t[20], KH, 16.0, A.mult)
     ts(A16, HB, 32.0, A.mult, t[20], A.add)
     ts(O64, O_, 64.0, A.mult)
@@ -441,18 +509,17 @@ def rank_program(g, core, T, topo):
     ts(B("bs", 0, 20, 2), B("i16", 0, 20, 2), t[21], A.add)
     ts(B("bs", 1, 20, 2), B("i16", 1, 20, 2), t[22], A.add)
     tt(B("dlo", 15, 320, 16), B("dlo", 15, 320, 16), B("bs"), A.add)
-    iota(B("oc0"), [[0, 14], [32767, 2], [KEY, 8]], 160)
-    fill(B("oc", 88, 96), BIG), fill(B("oc", 312, 320), BIG)
+    iota(B("oc0"), [[0, 15], [32767, 2], [KEY, 8]], 160)
+    fill(B("oc", 88, 96), BIG), fill(B("pfo", 224, 232), BIG)
+    ts(t[29], I_, -float(KEY), A.mult, -32927.0, A.add)
+    ts(CO, CN, t[29], A.add)
     iota(B("sd"), [[1, 320]], -160)
-    fill(B("ob", 0, 16), 0.0), fill(B("ob", 336, 352), 0.0)
-    dma("y", "z1", [B("zb", 0, 320)], [B("ob", 16, 336)], view(B("ob", 16, 336)), view(B("zb", 0, 320)))
-    for n in ("mkn", "mko"):
-        fill(B(n, 0, 512, 16), BIG)
-    fill(B("acl"), 0.0)
+    fill(B("mk", 0, 1024, 16), BIG)
+    fill(B("acl"), 0.0), fill(B("jv", 6060, 6080), 0.0)
     fill(B("rw0"), 0.0)
     iota(B("xo", 0, 32), [[0, 4], [1, 8]])
     iota(B("xn", 0, 16), [[0, 2], [1, 8]])
-    iota(B("a2", 0, 64), [[16, 4], [0, 2], [1, 8]])
+    iota(B("a2", 0, 64), [[0, 8], [1, 8]])
     iota(B("h1"), [[1, 4], [0, 2]])
     iota(B("h2"), [[0, 4], [16, 2]])
     ts(B("h3"), B("h1"), KQ, A.subtract, 4.0, A.mult)
@@ -471,43 +538,42 @@ def rank_program(g, core, T, topo):
         iota(B("ico", 128 + j, 256, 2), [[16, 4], [-1000, 2], [1, 8]], 1016 + 8 * j)
     iota(B("ico", 256, 384), [[8, 4], [32, 2], [1, 16]])
     ts(W8, O_, -7.0, A.mult, 8.0, A.add)
-    fill(B("cab", 3, 1536, 4), 0.0)
+    clear(B("cab", 3, 1536, 4))
+    ts(B("ico"), B("ico"), PH, A.is_equal, W8, A.mult)
     for j, w in enumerate((4.0, 2.0, 1.0)):
-        ts(t[15 + j], W8, w, A.mult)
-        ts(B("cab", j, 1536, 4), B("ico"), PH, A.is_equal, t[15 + j], A.mult)
+        ts(B("cab", j, 1536, 4), B("ico"), w, A.mult)
     quant("ca", 0, 384, "cab", 0)
     iota(B("m64"), [[1, 8], [0, 64]])
     ts(B("ccb"), B("m64"), G_, A.is_equal, -1.0, A.mult)
     quant("cc", 0, 128, "ccb", 0)
     op({"g": 350.0}, [B("chi")], [B("chb")], lambda e: e.partition_broadcast(view(B("chb")), T.chi[0:1, 0:64], 128))
     iota(B("m8"), [[0, 8], [1, 8]])
+    K["sooner"](2, MORE[0])
     cp(B("chf"), B("chb"))
     ts(B("k8"), B("m8"), V_, A.is_equal)
-    ts(B("d8"), B("m8"), 0.0, A.is_gt)
+    act(B("d8"), B("m8"), ACT.Sign)
     tt(B("cht"), B("chf"), B("k8"), A.mult)
     scan(B("chs"), B("d8"), B("cht"), A.mult, A.add)
     ts(VL, V_, NMI, A.mult)
     ts(B("lt"), B("chs", 7, 64, 8), MI, A.mult, VL, A.add)
     for a in range(8):
-        cp(B("tf", 128 * a, 128 * a + 128), ("@", B("chf", 8 * a, 8 * a + 8), B("lt")))
+        cp(B("tf", 128 * a, 128 * a + 128), ("@", B("chf", 8 * a, 8 * a + 8), B("lt")), "s")
     for a in range(4):
-        latch(B("tl", 256 * a, 256 * a + 256), B("tf", 256 * a, 256 * a + 256), B("dlb"))
+        latch(B("tl", 256 * a, 256 * a + 256), B("tf", 256 * a, 256 * a + 256), B("dlb", 0, 256))
     for j in range(2):
         ts(t[24 + j], C8, 8.0 + 16 * j, A.add)
         ts(B("tab", 64 * j, 64 * j + 64), B("tl", 15, 1024, 16), t[24 + j], A.add)
-    ts(t[26], GL, 16.0, A.mult, I_, A.add)
-    iota(B("i64"), [[1, 64]])
-    ts(B("eye"), B("i64"), t[26], A.is_equal)
+    iota(B("li"), [[-128, 2], [1, 64], [64, 4]])
+    ts(t[32], KH, 1024.0, A.mult, B("pi"), A.add)
+    ts(t[33], KH, -1088.0, A.mult, 1024.0, A.add)
+    ts(t[34], t[33], B("pi"), A.add)
     for k in range(4):
-        for e in range(2):
-            q = (64 * (k // 2), 64 * (k // 2) + 64)
-            cp(B("lb", 512 * k + 258 * e + k % 2, 512 * k + 256 * e + 256, 4, q), B("eye", p=q), "s")
+        ts(B("lb", 512 * k, 512 * k + 512), B("li"), -64.0 * (k % 2), A.add, t[32 + 2 * (k // 2)], A.is_equal)
     quant("lq", 0, 512, "lb", 0)
     for b in range(4):
         o = B("eb", 512 * b, 512 * b + 512)
         op({"g": 1020.0}, [B("one")], [o], lambda e, o=o, b=b: e.affine_select(view(o), view(B("one")), [[-4, 128], [-1, 4]], A.is_equal, 0.0, b, 4))
     quant("eq", 0, 512, "eb", 0)
-    quant("vq", 0, 128, "vb", 0)
 
     def calls(p, x):
         if p == "o":
@@ -515,9 +581,9 @@ def rank_program(g, core, T, topo):
                 mm(2 + j, 128, x, lo, "uq", 0)
                 ts(B("bt", 8 * j, 8 * j + 3), ps(2 + j, 1, 4), 0.0, A.is_gt)
             quant("bqo", 0, 130, "bt", 0)
-            mm(1, 128, "ca", 0, "bqo", 0, True, False)
-            mm(1, 128, "ca", 128, "bqo", 2, False, True)
-            ts(B("ixo"), ps(1, 0, 1), O64, A.add)
+            mm(2, 128, "ca", 0, "bqo", 0, True, False)
+            mm(2, 128, "ca", 128, "bqo", 2, False, True)
+            ts(B("ixo"), ps(2, 0, 1), O64, A.add)
             cp(B("lio"), ("@", B("tab"), B("ixo")))
         else:
             mm(1, 128, x, 0, "uq", 0)
@@ -532,46 +598,45 @@ def rank_program(g, core, T, topo):
         w = 16 * n
         for e in range(8):
             cp(B(x, w * e + w, w * e + 2 * w), ("@", B(x, w * e, w * e + w), B("li" + p, 2 * e, 2 * e + n)), PIN["chain"])
-        last = ("@", B(x, 8 * w, 9 * w), B("p4", 0, 2 * n))
+        got = ("@", B(x, w, 9 * w), B("ll" + p))
         if p == "o":
-            ts(B("ppo"), last, A16, A.add, qs=PIN["chain"])
+            ts(B("zo"), got, A16, A.add, qs=PIN["rows"])
         else:
-            cp(B("ppn"), last, PIN["chain"])
-        turn(B("to" + p), B("pp" + p))
-        share("to" + p, 2 * w)
+            cp(B("zn"), got, PIN["rows"])
+        turn(B("rt" + p), B("z" + p))
+        share("rt" + p, 10 * w)
         if p == "o":
-            cp(B("lpo"), ("@", B("too"), B("pto")))
+            cp(B("lpo"), ("@", B("rto"), B("pto")))
             for j in range(4):
                 cp(B("a2", 64 * j + 64, 64 * j + 128), ("@", B("a2", 64 * j, 64 * j + 64), B("lpo", 4 * j, 4 * j + 4)), PIN["chain"])
-            latch(B("wa"), B("a2"), B("dlf"))
+            latch(B("wa"), B("a2"), B("dlb"))
             ts(B("l2", 0, 6, 2), B("wa", 271, 304, 16), CW, A.add)
-            for j in range(4):
-                ts(B("lf", j, 16, 4), B("wa", 64 * j + 15, 64 * j + 64, 16), CW, A.add)
+            for a in range(4):
+                ts(B("lf", 4 * a, 4 * a + 4), B("wa", 16 * a + 15, 256, 64), CW, A.add, 16.0 * a, A.add)
         else:
-            ts(B("lpn", 0, 32, 2), ("@", B("ton"), B("ptn")), M8, A.add)
+            ts(B("lpn", 0, 32, 2), ("@", B("rtn"), B("ptn")), M8, A.add)
             for e in range(6):
                 cp(B("pfn", 16 * e + 16, 16 * e + 32), ("@", B("pfn", 16 * e, 16 * e + 16), B("lpn", 2 * e, 2 * e + 1)), PIN["chain"])
             for a in range(3):
-                cp(B("pfn", 112 + 16 * a, 128 + 16 * a), ("@", B("pfn", 96, 112 + 16 * a), B("l2", 2 * a, 2 * a + 1)), PIN["chain"])
-            cp(B("pfo"), ("@", B("pfn", 96, 160), B("lf", 0, 14)), PIN["rows"])
-            for pf, lo, hi in (("pfn", 0, 96), ("pfo", 96, 320)):
+                cp(B("pfn", 112 + 16 * a, 128 + 16 * a), ("@", B("pfn", 96 + 16 * a, 112 + 16 * a), B("l2", 2 * a, 2 * a + 1)), PIN["chain"])
+            tt(B("pfo", 0, 224), ("@", B("pfn", 96, 160), B("lf", 0, 14)), B("oc0", 8, 232), A.add)
+            tt(B("oc", 0, 88), B("pfn", 8, 96), B("oc0", 0, 88), A.add)
+            for pf, lo, hi, c in (("pfn", 0, 96, CN), ("pfo", 96, 320, CO)):
                 latch(B("wl", lo, hi), B(pf, 0, hi - lo), B("dlo", lo, hi))
-                ts(B("otl", lo // 16, hi // 16), B("wl", lo + 15, hi, 16), CN, A.add, NMI, A.mult)
-                tt(B("oc", lo, hi - 8), B(pf, 8, hi - lo), B("oc0", 0, hi - lo - 8), A.add)
-        cp(B("z" + p), ("@", B(x, w, 9 * w), B("ll" + p)), PIN["rows"])
-        turn(B("rt" + p), B("z" + p))
-        share("rt" + p, 8 * w)
-        i = B("rr" + p)
-        cp(i, ("@", B("rt" + p), B("rl" + p)), PIN["rows"])
+                ts(B("otl", lo // 16, hi // 16), B("wl", lo + 15, hi, 16), c, A.add, NMI, A.mult)
+        if p == "o":
+            return
+        i = B("rr")
+        tt(i, ("@", B("rto", 0, 480), B("rll")), B("a16"), A.subtract)
         for e in range(1, 8):
-            o = B("mk" + p, e, 512, 16)
+            o = B("mk", e, 1024, 16)
 
             def fn(q, o=o, e=e):
                 if q is g.vector:
                     return q.tensor_scalar(view(o), view(i), float(e), BIG, A.is_ge, A.mult)
                 return q.activation(view(o), view(i), ACT.Relu, bias=BIG * (0.5 - e), scale=BIG)
             op(costs(PIN["mask"], o, [i]), [i], [o], fn)
-        ts(B("mk" + p, 8, 512, 16), i, -float(KEY), A.mult, qs=PIN["mask"])
+        ts(B("mk", 8, 1024, 16), i, -float(KEY), A.mult, qs=PIN["mask"])
 
     turns = []
 
@@ -597,24 +662,37 @@ def rank_program(g, core, T, topo):
         tt(B("y" + p), ps(bank, 0, n), B("yc", 0, n), A.add)
         if p == "o":
             cp(B("sco"), ps(bank, 0, n), "s")
-        scan(B("so" + p), B("d0", 0, n), B("y" + p), A.add, A.max)
+        scan(B("so" + p), B("d0", 0, n), B("y" + p), A.add, A.min)
+
+    def within(p):
+        c0, n = (96, 224) if p == "o" else (0, 96)
+        d = slot("g" + p, 0, 0, c0, c0 + n)
+        tt(d, ps(0 if p == "o" else 2, 0, n), B("so" + p), A.is_gt)
+        scan(B("dcs", c0, c0 + n), B("dr", 0, n), d, A.mult, A.add)
 
     def compare(p):
-        c0, n = (96, 224) if p == "o" else (0, 96)
+        c0 = 96 if p == "o" else 0
 
         def row(lo, hi):
             return B("sco", lo - c0, hi - c0) if p == "o" else ps(2, lo, hi)
-        d = slot("g" + p, 0, 0, c0, c0 + n)
-        tt(d, row(c0, c0 + n), B("so" + p), A.is_gt)
-        scan(B("dcs", c0, c0 + n), B("dr", 0, n), d, A.mult, A.add)
         for k in range(13 if p == "o" else 6):
             lo = c0 + 16 * k + 16
             if p == "o" and k > 10:
                 o = slot("gn", k - 11, 3 * (k - 11), lo, 320)
             else:
                 o = slot("g" + p, (k + 1) // 4, (k + 1) % 4, lo, 320)
-            ts(o, row(lo, 320), B("so" + p, 16 * k + 15, 16 * k + 16), A.is_gt)
-            count(o, B("acl", c0 // 16 + k, c0 // 16 + k + 1))
+            own, acc = B("so" + p, 16 * k + 15, 16 * k + 16), B("acl", c0 // 16 + k, c0 // 16 + k + 1)
+            if p == "o" and k in ALONE:
+                i, j = row(lo, 320), B("sg", 208 * (k % 2), 208 * (k % 2) + 320 - lo)
+                op(costs("s", j, [i]), [i, own], [j], lambda e, i=i, j=j, own=own: e.activation(view(j), view(i), ACT.Sign, bias=view(own), scale=-1.0))
+                op({"s": 20 + ac(j, [])}, [j], [o, acc], lambda e, j=j, o=o, acc=acc: e.activation(view(o), view(j), ACT.Relu, scale=-1.0, accum_out=view(acc)))
+            else:
+                ts(o, row(lo, 320), own, A.is_gt)
+                m = c0 // 16 + k
+                if m in SCAN:
+                    scan(B("jv", 6080 - 20 * (320 - lo) + m, 6080, 20), B("one", 0, 320 - lo), o, A.mult, A.add)
+                else:
+                    count(o, acc)
         for q, (at, lo) in enumerate(GO if p == "o" else GN):
             j = 320 * (q if p == "o" else 3 + q)
             quant("gq", j + lo, j + 320, "g" + p, at)
@@ -626,6 +704,7 @@ def rank_program(g, core, T, topo):
             mm(4 + k, max(n, 128), "lq", 128 * k, x, c0)
         for k in range(4):
             cp(B("win", 4 * c0 + k, 4 * (c0 + n), 4), ps(4 + k, 0, n), PIN["win"])
+        K["sooner"](8, MORE[1 if p == "o" else 2])
         lo, hi = 4 * c0, 4 * (c0 + n)
         for s in range(1, 4):
             for h in (0, 64):
@@ -638,17 +717,22 @@ def rank_program(g, core, T, topo):
         calls("o", x)
         scores("o", x)
         pieces("o")
+        within("o")
+        window("o", x, r)
         if r:
             arrive(r)
         compare("o")
-        window("o", x, r)
         calls("n", x)
         scores("n", x)
+        within("n")
         compare("n")
         window("n", x, r)
+        if r == 1:
+            later_loads()
         pieces("n")
         tt(B("rc1"), B("dcs", 15, 320, 16), B("cm"), A.add)
-        tt(B("rc2"), B("rc1"), B("acl"), A.add)
+        tt(B("rc3"), B("rc1"), B("jv", 6060, 6080), A.add)
+        tt(B("rc2"), B("rc3"), B("acl"), A.add)
         latch(B("cl"), ps(3, 0, 320), B("dlf"))
         tt(B("rkf"), B("cl", 15, 320, 16), B("rc2"), A.add)
         cp(B("rk"), B("rkf"))
@@ -658,11 +742,11 @@ def rank_program(g, core, T, topo):
         turn(B("tr", 320, 672), B("ob"))
         share("tr", 672)
         for p, m0, n, l0 in (("n", 0, 6, 0), ("o", 6, 14, 24)):
-            ot = B("ot", 16 * m0, 16 * (m0 + n))
-            tt(ot, ("@", B("tr"), B("otl", m0, m0 + n)), B("oc", 16 * m0, 16 * (m0 + n)), A.add)
+            ot, m1 = B("ot", 16 * m0, 16 * (m0 + n)), 512 if p == "n" else 0
+            tt(ot, ("@", B("tr"), B("otl", m0, m0 + n)), B("oc") if p == "n" else B("pfo", 8, 232), A.add)
             for G in range(2):
                 o = 8 * l0 + 16 * n * G
-                scan(B("sc", o, o + 16 * n), B("mk" + p, 256 * G, 256 * G + 16 * n), ot, A.add, A.min)
+                scan(B("sc", o, o + 16 * n), B("mk", 256 * G + m1, 256 * G + m1 + 16 * n), ot, A.add, A.min)
             for e in range(2):
                 ts(B("il", l0 + 2 * n * e, l0 + 2 * n * (e + 1)), B("sc", 8 * l0 + 15, 8 * l0 + 32 * n, 16), 4.0, A.mult, float(e), A.add)
             step = 12 if p == "n" else 14
@@ -698,10 +782,10 @@ def rank_program(g, core, T, topo):
         frm = T.cores[(rank - r) % len(T.cores)]
         n = 2 * len(topo.engines(frm, core))
         raw("t", [("sent%d" % r, 0, 1, 1, 0, 128)], [B("ld%dc" % r, 0, 96), B("ld%ds" % r, 0, 96)], lambda: K["wait"]("t", "rc%d" % r, n, {}), 1.0)
+        bank = (1, 3, 0, 2)
         for b in range(4):
             mm(4 + b, 128, "wq", 128 * b, "ld%d" % r, 0)
-            mm((3, 2, 0, 1)[b], 128, "eq", 128 * b, "ld%d" % r, 0)
-        for b in range(4):
+            mm(bank[b], 128, "eq", 128 * b, "ld%d" % r, 0)
             o, i = B("rl", 96 * b, 96 * b + 96), ps(4 + b, 0, 96)
 
             def fn(e, o=o, i=i):
@@ -709,7 +793,7 @@ def rank_program(g, core, T, topo):
                     return e.tensor_scalar(view(o), view(i), 0.0, 0.03125, A.max, A.mult)
                 return e.activation(view(o), view(i), ACT.Relu, scale=0.03125)
             op(costs(PIN["relu"], o, [i]), [i], [o], fn)
-            tt(B("tb", b, 384, 4), o, ps((3, 2, 0, 1)[b], 0, 96), A.add)
+            tt(B("tb", b, 384, 4), o, ps(bank[b], 0, 96), A.add)
         quant("qx%d" % r, 0, 128, "tb", 0)
 
     def store(lo, hi, bank):

@@ -1,25 +1,33 @@
+import math
 import numpy as np
 from concourse.mybir import dt, AluOpType, AxisListType, ActivationFunctionType
 
 CY = 0.83
-SLACK, HOP, WORSE, TRIES = 0.0, 200.0, 0.5, 1500
-SPAN, SIGMA, HEAT = 30, 300.0, 100.0
-ALONE = (0, 1)
-MORE = [3000.0, 0.0, 0.0]
-IDLE = 3.0
-SCAN = (9, 10, 11, 12, 13)
-DEAR = {"v": 2.0, "s": 1.0, "g": 1.0}
+HOP = 200.0
+TRIES = 4000
+MOVES = 80000
+SEED = 1
+REACH, MEAN, WARM = 40, 1.0, 5.0
+SPAN, SIGMA, HEAT = 0.04, 800.0, 20.0
+ALONE = (0, 1, 6, 7, 8)
+COUNT = ()
+HOLD = True
+DEAR = {"v": 1.6, "s": 1.0, "g": 1.0, "t": 1.0, "y": 1.0}
 ROUNDS = 3
-STEP, LOW = 65536.0, 2097152.0
+STEP, LOW = 1024.0, 131072.0
 STEP8, LOW8 = 8.0, 256.0
-BIG, KEY, HUGE = 65536.0, 4096, 2.0 ** 92
-FIELDS = ((5, 2), (4, 1), (3, 1), (2, 1), (0, 2), (0, 4), (0, 3), (1, 6), (0, 1), (4, 3), (1, 2), (1, 3), (1, 1), (6, 1), (5, 1), (4, 2))
+KEY, HUGE = 8192, 2.0 ** 92
+POS = (0, 8, 4, 12)
+FIELDS = ((4, 1), (3, 1), (0, 4), (0, 3), (1, 6), (0, 1), (4, 3), (1, 3), (6, 1), (5, 1), (4, 2))
 F32, BF, I32, U16 = "float32", "bfloat16", "int32", "uint16"
 CODE, SC = "float8_e4m3fn_x4", "uint8"
 SIZE = {F32: 4, BF: 2, I32: 4, U16: 2, CODE: 4, SC: 1}
 GO = ((0, 96), (896, 160), (1536, 192))
 GN = ((0, 0), (1280, 64))
-PIN = {"chain": "vs", "count": "vs", "shift": "vs", "lay": "vs", "win": "vs", "pick": "vs", "mask": "vs", "rows": "vs", "relu": "vs"}
+PAD = 32
+FIRST = False
+BANK = {"co": (1, 2), "so": 0, "wo": (4, 5, 6, 7), "lw": (4, 5, 6, 7), "le": (1, 2, 3, 4), "cn": 5, "sn": 6, "sn2": 7, "wn": (1, 2, 4, 1)}
+PIN = {"chain": "vs", "count": "vs", "shift": "vsg", "lay": "vsg", "win": "vs", "pick": "vs", "mask": "vs", "rows": "vs", "relu": "vs"}
 
 
 def _scratch():
@@ -33,31 +41,30 @@ def _scratch():
         sb(name + "s", n, SC)
     for b in range(8):
         d["ps%d" % b] = ("psum", [128, 512], F32)
-    for n, w in (("xb", 1280), ("ub", 512), ("vb", 512), ("eb", 2048), ("lb", 2048), ("zb", 768), ("ccb", 512), ("cab", 1536), ("one", 512),
-                 ("bt", 528), ("li", 512), ("ta", 512), ("tb", 1280), ("st", 1280), ("win", 5120), ("go", 2048), ("gn", 2304), ("jk", 1280),
-                 ("m64", 512), ("ico", 384), ("mk", 1024)):
+    for n, w in (("xb", 1408), ("ub", 512), ("vb", 512), ("lb", 2048), ("zb", 768), ("ccb", 512), ("cab", 512), ("one", 512),
+                 ("bt", 512), ("bs", 512), ("ta", 512), ("tb", 1408), ("st", 1280), ("win", 5120), ("go", 2048), ("gn", 2304), ("jk", 1280),
+                 ("m16", 128), ("ico", 128)):
         sb(n, w, BF)
-    for n, w in (("uq", 128), ("ur", 128), ("vq", 128), ("eq", 512), ("lq", 512), ("wq", 512), ("cc", 128), ("ca", 384), ("bqo", 130),
+    for n, w in (("uq", 128), ("ur", 128), ("vq", 128), ("lq", 768), ("wq", 512), ("cc", 128), ("ca", 128), ("bqo", 128),
                  ("bqn", 128), ("gq", 1600)):
         mx(n, w)
     for r in range(ROUNDS + 1):
-        mx("qx%d" % r, 320)
+        mx("qx%d" % r, PAD + 320)
         if r:
             mx("ld%d" % r, 128)
             mx("qs%d" % r, 128)
     sb("bi", 7, I32), sb("pi", 1), sb("half", 7), sb("pw", 7), sb("fl", 7), sb("chi", 64, I32), sb("chb", 64, I32), sb("rwi", 64, I32), sb("rwj", 64, I32)
-    for n, w in (("cf", 80), ("ulf", 8), ("i32", 2), ("llf", 16), ("cm", 20), ("i16", 20), ("bs", 20), ("oc0", 240), ("oc", 96), ("dlf", 320), ("dlo", 320),
+    for n, w in (("cf", 48), ("ulf", 8), ("llf", 30), ("dlp", 21), ("oc", 112), ("dlf", 128), ("dlc", 320),
                  ("yc", 224), ("d0", 224), ("chf", 64), ("m8", 64), ("k8", 64), ("d8", 64), ("cht", 64), ("chs", 64), ("yo", 224), ("soo", 224), ("sco", 224),
-                 ("yn", 96), ("son", 96), ("acl", 20), ("rc1", 20), ("rc2", 20), ("cl", 320), ("rkf", 20), ("ot", 320), ("sc", 640), ("rl", 384),
-                 ("yb", 320), ("rw0", 64), ("rw1", 64), ("rw2", 64), ("rw3", 64), ("rwb", 64), ("wl", 320), ("h1", 8), ("h2", 8),
-                 ("h3", 8), ("h4", 8), ("h5", 8), ("h6", 8), ("h7", 8), ("h8", 8), ("pfn", 160), ("pfo", 232), ("a16", 64), ("rc3", 20)):
+                 ("yn", 96), ("son", 96), ("acl", 20), ("rc1", 20), ("rc2", 20), ("cl", 320), ("rkf", 20), ("ot", 320), ("sc", 320), ("rl", 384),
+                 ("yb", 320), ("rw0", 64), ("rw1", 64), ("rw2", 64), ("rw3", 64), ("rwb", 64), ("h1", 8), ("h2", 8), ("h3", 8), ("h4", 8), ("wp", 8),
+                 ("pf", 72), ("lo", 144), ("pc", 32), ("pq", 112), ("wn", 48), ("wo", 128), ("wc2", 112), ("tq", 176)):
         sb(n, w)
-    for n, w in (("bm16", 320), ("dr", 224), ("dlb", 320), ("sd", 320), ("ob", 352), ("tr", 672), ("dcs", 320), ("tf", 1024), ("tl", 1024), ("tab", 128),
-                 ("xo", 288), ("xn", 144), ("a2", 320),
-                 ("zo", 320), ("zn", 160), ("rto", 320), ("rtn", 160), ("rr", 64), ("jv", 6080), ("sg", 416), ("wa", 320)):
+    for n, w in (("bm16", 320), ("flo", 320), ("dlb", 256), ("sd", 320), ("ob", 352), ("tr", 704), ("dcs", 320), ("tf", 1024), ("tl", 1024), ("tab", 64),
+                 ("xo", 288), ("xn", 144), ("zo", 320), ("zn", 160), ("rto", 320), ("rtn", 160), ("xp", 224), ("dd", 320), ("jv", 6080), ("sg", 608)):
         sb(n, w, BF + "*")
-    for n, w in (("ul", 8), ("otl", 20), ("rll", 4), ("pto", 1), ("ptn", 1), ("llo", 20), ("lln", 10), ("lt", 8), ("ixo", 1), ("ixn", 1),
-                 ("lio", 16), ("lin", 32), ("lpo", 16), ("lpn", 32), ("l2", 6), ("lf", 16), ("rk", 20), ("il", 80)):
+    for n, w in (("ul", 8), ("otl", 12), ("llo", 20), ("lln", 10), ("dl", 20), ("xl", 12), ("lt", 8), ("ixo", 4), ("ixn", 1),
+                 ("lco", 32), ("lcn", 16), ("lp", 48), ("lf", 8), ("rk", 20), ("il", 80)):
         sb(n, w, U16)
     return d
 
@@ -79,91 +86,151 @@ def _pack(d):
 
 BUFS = _scratch()
 SCRATCH, PLACE = _pack(BUFS)
-SEMAPHORES = (["cv", "ct", "cs", "cg", "dx", "du", "dv", "dw", "dc", "z1", "z4", "z5", "out", "ls"]
+SEMAPHORES = (["cv", "ct", "cs", "cg", "dx", "du", "dv", "dw", "dc", "de", "z1", "z4", "z5", "z6", "out", "ls"]
               + [k + "%d" % r for k in ("so", "sn") for r in range(3)] + ["rc%d" % r for r in range(1, 4)])
 PLANS = {}
 
 
 def _plan(jobs):
     n = len(jobs)
-    after = [[] for _ in jobs]
+    anc, pre, post = [0] * n, [], [[] for _ in jobs]
     for i, j in enumerate(jobs):
-        for k in j["pre"]:
-            after[k].append(i)
-    way, both = [0.0] * n, {}
-    for j in jobs:
-        both[j["sem"]] = both.get(j["sem"], 0.0) + j["dur"]
-    for i in range(n - 1, -1, -1):
-        j = jobs[i]
-        way[i] = min(j["c"].values()) + j["lat"] + (j["dur"] if j["sem"] in ("raw", "out") else both[j["sem"]]) + max([way[k] + HOP for k in after[i]] or [0.0])
+        keep = []
+        for k in sorted(j["pre"], reverse=True):
+            if not anc[i] >> k & 1:
+                keep.append((k, 0.0 if "t" in j["c"] and "t" in jobs[k]["c"] else HOP))
+                post[k].append((i, keep[-1][1]))
+            anc[i] |= anc[k] | 1 << k
+        pre.append(keep)
+    cost, lat, dur = [j["c"] for j in jobs], [j["lat"] for j in jobs], [j["dur"] for j in jobs]
 
-    def once(prio, lean):
-        free, fin, left = {q: 0.0 for q in "vtsgy"}, [0.0] * n, [len(j["pre"]) for j in jobs]
-        t0, order, engines = [0.0] * n, [], 0.0
-        ready = [i for i in range(n) if not left[i]]
-        while ready:
-            best = None
-            for i in ready:
-                c, t = jobs[i]["c"], t0[i]
-                if len(c) == 1 or lean[i]:
-                    qs = lean[i] or c
+    def gap(busy, t, c):
+        a, b = 0, len(busy)
+        while a < b:
+            m = (a + b) // 2
+            if busy[m][1] <= t:
+                a = m + 1
+            else:
+                b = m
+        while a < len(busy) and busy[a][0] < t + c:
+            t = busy[a][1]
+            a += 1
+        return t, a
+
+    def lay(key, dep, lean, back):
+        busy, st, fin, on = {q: [] for q in "vtsgye"}, [0.0] * n, [0.0] * n, [""] * n
+        for i in follow(key, dep):
+            t = max([fin[k] + h for k, h in dep[i]] or [0.0])
+            c, d, best = cost[i], dur[i], None
+            if d and back:
+                t, x = gap(busy["e"], t, d)
+                busy["e"].insert(x, (t, t + d))
+                t += d + lat[i]
+            for q in lean[i] or c:
+                s, x = gap(busy[q], t, c[q])
+                if best is None or s + c[q] * DEAR[q] < best[0]:
+                    best = (s + c[q] * DEAR[q], s, x, q)
+            s, x, q = best[1:]
+            st[i], fin[i], on[i] = s, s + c[q], q
+            busy[q].insert(x, (s, fin[i]))
+            if d and not back:
+                t, x = gap(busy["e"], fin[i] + lat[i], d)
+                busy["e"].insert(x, (t, t + d))
+                fin[i] = t + d
+        return st, fin, on
+
+    def follow(key, dep):
+        done, out = [False] * n, []
+        for i in sorted(range(n), key=lambda x: key[x]):
+            stack = [i]
+            while stack and not done[i]:
+                x = stack[-1]
+                m = [k for k, h in dep[x] if not done[k]]
+                if m:
+                    stack.extend(m)
                 else:
-                    ends = {q: max(free[q], t) + c[q] * DEAR[q] for q in c}
-                    soonest = min(ends.values())
-                    qs = [q for q in c if ends[q] <= soonest + WORSE * c[q]]
-                for q in qs:
-                    key = (max(free[q], t - SLACK), -prio[i])
-                    if best is None or key < best[0]:
-                        best = (key, i, q)
-            key, i, q = best
-            s = max(free[q], t0[i])
-            e = s + jobs[i]["c"][q]
-            for k in ready:
-                if s < t0[k] < e and prio[k] > prio[i] and q in jobs[k]["c"] and lean[k] in ("", q) and (len(jobs[k]["c"]) == 1 or lean[k]):
-                    if max(t0[k] + prio[k], t0[k] + jobs[k]["c"][q] + prio[i]) + IDLE * (t0[k] - s) < max(s + prio[i], e + prio[k]):
-                        i, e = k, t0[k]
-            j = jobs[i]
-            ready.remove(i)
-            free[q] = fin[i] = max(free[q], t0[i]) + j["c"][q]
-            if j["dur"]:
-                engines = fin[i] = max(engines, fin[i] + j["lat"]) + j["dur"]
-            order.append((i, q))
-            for k in after[i]:
-                left[k] -= 1
-                t0[k] = max(t0[k], fin[i] + (0.0 if q == "t" and "t" in jobs[k]["c"] else HOP))
-                if not left[k]:
-                    ready.append(k)
-        return max(fin), order
-    way = [w + j.get("more", 0.0) for w, j in zip(way, jobs)]
-    rng = np.random.RandomState(1)
-    alike = {}
-    for i, j in enumerate(jobs):
-        alike.setdefault(tuple((a[0].rstrip("cs").rstrip("0123") if a[0][0] in "ql" else a[0],) + a[1:] for a in j["w"] + j["r"]), []).append(i)
-    alike = list(alike.values())
-    either = [a for a in alike if len(jobs[a[0]]["c"]) > 1]
-    prio, lean = way, [""] * n
-    best = now = once(prio, lean)
+                    stack.pop()
+                    if not done[x]:
+                        done[x] = True
+                        out.append(x)
+        return out
+
+    def both(key, lean):
+        st, fin, on = lay(key, pre, lean, False)
+        st, fin, on = lay([-x for x in fin], post, on, True)
+        st, fin, on = lay([-x for x in fin], pre, lean, False)
+        seq = follow(st, pre)
+        return max(times(seq, on)[1]), st, on, seq
+
+    def times(seq, on):
+        free, last, fin, why, engines, before = dict.fromkeys("vtsgy", 0.0), dict.fromkeys("vtsgy", -1), [0.0] * n, [-1] * n, 0.0, -1
+        for i in seq:
+            q = on[i]
+            t, w = free[q], last[q]
+            for k, h in pre[i]:
+                x = fin[k] + h
+                if x > t:
+                    t, w = x, k
+            t += cost[i][q]
+            free[q], last[q] = t, i
+            if dur[i]:
+                t += lat[i]
+                if engines > t:
+                    t, w = engines, before
+                t += dur[i]
+                engines, before = t, i
+            fin[i], why[i] = t, w
+        return max(fin) + MEAN * sum(fin) / n, fin, why
+    way = [0.0] * n
+    for i in range(n - 1, -1, -1):
+        way[i] = min(cost[i].values()) + lat[i] + dur[i] + max([way[k] + h for k, h in post[i]] or [0.0])
+    best = now = both([-w for w in way], [""] * n)
+    rng = np.random.RandomState(SEED)
     for step in range(TRIES):
-        p2, l2 = list(prio), list(lean)
-        one = rng.randint(6)
-        if step % 2:
-            lo = rng.randint(len(alike))
-            for a in alike[lo:lo + rng.randint(1, SPAN)]:
-                d = float(rng.normal()) * SIGMA
-                for i in (a if one > 2 else a[one:one + 1]):
-                    p2[i] += d
-        else:
-            lo = rng.randint(len(either))
-            for a in either[lo:lo + rng.randint(1, 4)]:
-                q = ([""] + list(jobs[a[0]]["c"]))[rng.randint(len(jobs[a[0]]["c"]) + 1)]
-                for i in (a if one > 2 else a[one:one + 1]):
-                    l2[i] = q
-        got = once(p2, l2)
-        if got[0] <= now[0] + HEAT * (1.0 - step / TRIES):
-            now, prio, lean = got, p2, l2
+        lo = rng.rand() * now[0]
+        key, lean = list(now[1]), list(now[2])
+        for i in [i for i in range(n) if lo <= key[i] <= lo + SPAN * now[0]]:
+            key[i] += float(rng.normal()) * SIGMA
+            r = rng.rand()
+            if r < 0.3 and len(cost[i]) > 1:
+                lean[i] = list(cost[i])[int(r * 10 * len(cost[i]))] if r < 0.1 else ""
+        got = both(key, lean)
+        if got[0] <= now[0] - HEAT * (1.0 - step / TRIES) * math.log(rng.rand() + 1e-9):
+            now = got
             if got[0] < best[0]:
                 best = got
-    return best
+    seq, on = best[3], best[2]
+    now, fin, why = times(seq, on)
+    best, path = (max(fin), seq, on), None
+    for step, (a, b, c, d, e) in enumerate(np.random.RandomState(2).rand(MOVES, 5).tolist()):
+        if path is None:
+            i, path = fin.index(max(fin)), []
+            while i >= 0:
+                path.append(i)
+                i = why[i]
+        i = path[int(b / 0.7 * len(path))] if b < 0.7 else int((b - 0.7) / 0.3 * n)
+        s2, o2, k = seq, on, why[i]
+        if a < 0.3:
+            if len(cost[i]) < 2:
+                continue
+            qs = [q for q in cost[i] if q != on[i]]
+            o2 = on[:i] + [qs[int(c * len(qs))]] + on[i + 1:]
+        elif a < 0.65:
+            p = seq.index(i)
+            to = max(0, p - 1 - int(c * REACH)) if k < 0 or anc[i] >> k & 1 else seq.index(k)
+            mid = seq[to:p]
+            s2 = seq[:to] + [x for x in mid if anc[i] >> x & 1] + [i] + [x for x in mid if not anc[i] >> x & 1] + seq[p + 1:]
+        else:
+            i = k if k >= 0 and d < 0.5 else i
+            p = seq.index(i)
+            mid = seq[p + 1:p + 2 + int(c * REACH)]
+            s2 = seq[:p] + [x for x in mid if not anc[x] >> i & 1] + [i] + [x for x in mid if anc[x] >> i & 1] + seq[p + 1 + len(mid):]
+        got, f2, w2 = times(s2, o2)
+        if got <= now - (1.0 + WARM * (1.0 - step / MOVES)) * math.log(e + 1e-12):
+            seq, on, now, fin, why, path = s2, o2, got, f2, w2, None
+            if max(fin) < best[0]:
+                best = (max(fin), seq, on)
+    return best[0], [(i, best[2][i]) for i in best[1]]
 
 
 def _make(g, T):
@@ -237,12 +304,8 @@ def _make(g, T):
     def raw(q, reads, writes, fn, cost, lat=0.0, dur=0.0):
         jobs.append(dict(c={q: cost}, r=reads, w=writes, fn=fn, lat=lat, dur=dur, sem="raw"))
 
-    def sooner(count, ns):
-        for j in jobs[-count:]:
-            j["more"] = ns
-
     def run():
-        table, groups = {}, {}
+        table, groups, alone = {}, {}, [False]
         for i, j in enumerate(jobs):
             pre = set()
             grp = j["sem"] if j["sem"] not in (None, "raw") else None
@@ -273,6 +336,11 @@ def _make(g, T):
                 continue
             sem = j["sem"] or comp[q]
             need(q, j["r"], j["w"], sem, j["sem"] is None)
+            if q == "g":
+                shifted = any(a[4:] != (0, 128) for a in j["w"])
+                if shifted or alone[0]:
+                    wait(q, sem, total.get(sem, 0), {})
+                alone[0] = shifted
             if j["sem"]:
                 total[sem] = total.get(sem, 0) + 16
                 queues[q].dma_start(*j["fn"]).then_inc(T.sem[sem], 16)
@@ -280,7 +348,7 @@ def _make(g, T):
                 total[sem] = total.get(sem, 0) + 1
                 j["fn"](queues[q]).then_inc(T.sem[sem], 1)
             note(q, j["r"], j["w"], sem, total[sem])
-    return dict(view=view, wait=wait, need=need, op=op, dma=dma, raw=raw, run=run, total=total, sooner=sooner)
+    return dict(view=view, wait=wait, need=need, op=op, dma=dma, raw=raw, run=run, total=total)
 
 
 def rank_program(g, core, T, topo):
@@ -319,7 +387,7 @@ def rank_program(g, core, T, topo):
         return (65 + 1.5 * CY * width(out)) if any(a[0] == "@" for a in ins) else 60 + CY * width(out)
 
     def costs(qs, out, ins):
-        return {q: vc(out, ins) if q == "v" else ac(out, ins) for q in qs}
+        return {q: vc(out, ins) if q == "v" else ac(out, ins) if q == "s" else 170 + HOP + 2 * CY * width(out) for q in qs}
 
     def sc(x):
         return (view(x), [x]) if isinstance(x, tuple) else (x, [])
@@ -353,6 +421,8 @@ def rank_program(g, core, T, topo):
         def fn(e):
             if e is g.vector:
                 return e.tensor_copy(view(out), iv)
+            if e is g:
+                return e.affine_select(view(out), iv, [[0, width(out)]], A.is_ge, 0.0, 0, 0)
             return e.activation(view(out), iv, ACT.Copy)
         op(costs(qs if kind(out) in (F32, BF) and kind(in_) in (F32, BF) else "v", out, [in_]), ir, [out], fn)
 
@@ -360,17 +430,16 @@ def rank_program(g, core, T, topo):
         op({"v": vc(out, [d0, d1])}, [d0, d1], [out], lambda e: e.tensor_tensor_scan(view(out), view(d0), view(d1), first, o0, o1))
 
     def latch(out, d1, d):
-        scan(out, d, d1, A.add, A.max)
+        scan(out, d1, d, A.max, A.add, -LOW)
 
     def turn(out, in_):
         op({"v": vc(out, [in_])}, [in_], [out], lambda e: e.transpose(view(out), view(in_)))
 
     def share(n, w):
-        for a, b in (((0, 64), (64, 128)), ((64, 128), (0, 64))):
-            cp(B(n, 8, w, 16, a), B(n, 0, w, 16, b), PIN["shift"])
         for k in range(4):
-            k1 = (k + 1) % 4
-            cp(B(n, 4, w, 8, (32 * k, 32 * k + 32)), B(n, 0, w, 8, (32 * k1, 32 * k1 + 32)), PIN["shift"])
+            cp(B(n, POS[k], w, 16, (32 * (k ^ 1), 32 * (k ^ 1) + 32)), B(n, POS[k], w, 16, (32 * k, 32 * k + 32)), PIN["shift"])
+        for k in range(2):
+            cp(B(n, 4 * k, w, 8, (64 - 64 * k, 128 - 64 * k)), B(n, 4 * k, w, 8, (64 * k, 64 * k + 64)), PIN["shift"])
 
     def fill(out, x):
         if x != int(x):
@@ -408,7 +477,7 @@ def rank_program(g, core, T, topo):
         op(costs("s", out, [in_]), [in_] + r, [out], lambda e: e.activation(view(out), view(in_), f, bias=x, scale=scale))
 
     dma("s", "dc", [], [B("chi", p=(0, 1))], T.chi[0:1, 0:64], T.ch[:, :])
-    dma("y", "dx", [], [B("xb")], view(B("xb")), T.x[:, :])
+    dma("y", "dx", [], [B("xb", 128)], view(B("xb", 128)), T.x[:, :])
     dma("y", "du", [], [B("ub")], view(B("ub")), T.u[:, :])
     fill(B("zb"), 0.0)
     quant("gq", 640, 832, "zb", 0)
@@ -417,9 +486,8 @@ def rank_program(g, core, T, topo):
             o, i = B("gq" + k, lo, hi), B("gq" + k, 640, 640 + hi - lo)
             dma("y", "z4", [i], [o], bits(o), bits(i))
     for a in (B("go", 0, 192), B("go", 896, 1088), B("go", 1536, 1856), B("gn", 0, 192), B("gn", 384, 1152, 4), B("gn", 1280, 1408), B("gn", 1283, 2240, 4),
-              B("ta", 384, 512), B("bt")):
+              B("ta", 384, 512), B("bt"), B("bs"), B("xb", 0, 128), B("tb", 0, 128)):
         clear(a)
-    clear(B("mk", 0, 512)), clear(B("mk", 512, 1024))
 
     def beside(r, sem, after):
         for k in "cs":
@@ -429,20 +497,28 @@ def rank_program(g, core, T, topo):
     dma("y", "dw", [B("gqc", 640, 672)], [B("wqc")], T.wqc[:, 0:512].bitcast(dt.uint8), T.wc[:, :])
     dma("y", "dw", [B("gqc", 640, 672)], [B("wqs")], view(B("wqs")), T.ws[:, :])
 
-    def later_loads():
-        after = [B("qx1c", 0, 96)]
-        beside(2, "z5", after), beside(3, "z5", after)
-        dma("y", "dv", after, [B("vb")], view(B("vb")), T.v[:, :])
-        quant("vq", 0, 128, "vb", 0)
+    def later_loads(r):
+        after = [B("win", 1280, 1296)]
+        if r == 0:
+            for e in range(2):
+                for to, frm in ((0, 3), (5, 2)):
+                    for k in "cs":
+                        o, i = (B("lq" + k, 384 * e + 64 * c, 384 * e + 64 * c + 64) for c in (to, frm))
+                        dma("y", "de", [i] + after, [o], bits(o), bits(i))
+        if r < 2:
+            beside(r + 2, "z%d" % (5 + r), after)
+        if r == 1:
+            dma("y", "dv", after, [B("vb")], view(B("vb")), T.v[:, :])
+            quant("vq", 0, 128, "vb", 0)
 
     iota(B("pi"), [[1, 1]], 0, 1)
     fill(B("half"), 0.5)
     iota(B("ulf"), [[16, 8]])
     iota(B("bm16"), [[0, 20], [1, 16]])
-    ts(B("one"), B("zb", 0, 512), 1.0, A.add, qs="s")
+    fill(B("one"), 1.0)
     cp(B("ul"), B("ulf"))
     quant("uq", 0, 128, "ub", 0)
-    quant("qx0", 0, 320, "xb", 0)
+    quant("qx0", 0, PAD + 320, "xb", 0)
     op({"v": 210.0}, [B("uqc"), B("ul")], [B("urc")], lambda e: e.tensor_copy(T.urc[:, 0:128].bitcast(dt.uint32), T.uqc[:, 0:128].bitcast(dt.uint32).indirect(view(B("ul")))))
     op({"s": 225.0}, [B("uqs"), B("ul")], [B("urs")], lambda e: e.activation(T.urs[:, 0:128], T.uqs[:, 0:128].indirect(view(B("ul"))), ACT.Copy))
     scan(B("pw"), B("half"), B("zb", 0, 7), A.mult, A.add, 2.0)
@@ -455,100 +531,75 @@ def rank_program(g, core, T, topo):
             return B("fl", s, s + 1)
         ts(cf(j), B("fl", s + w, s + w + 1), -float(1 << w), A.mult, B("fl", s, s + 1), A.add)
         return cf(j)
-    KQ, HB, MI, S2, K0, I_, V_, PH, O_, G_, K1, J1, SA, KH, Q1, GL = (field(j, s, w) for j, (s, w) in enumerate(FIELDS))
-    NMI, C8, CF_, CN, CW, N3, W8, VL, A16, O64, M8, RB, KA, CO = (cf(j) for j in range(16, 30))
-    t = [cf(j) for j in range(31, 80)]
-    ts(t[30], I_, HUGE, A.mult)
-    ts(t[31], I_, 4 * HUGE, A.mult, 2 * HUGE, A.add)
-    act(B("yc"), B("bm16", 0, 224), ACT.Abs, t[30], -HUGE)
-    act(B("d0"), B("bm16", 0, 224), ACT.Relu, t[31], -4 * HUGE)
-    act(B("dr"), B("bm16", 0, 224), ACT.Sign)
-    ts(B("dlb"), B("bm16"), I_, A.is_gt, LOW8 + STEP8, A.mult)
+    HB, MI, I_, V_, PH, O_, G_, J1, KH, Q1, GL = (field(j, s, w) for j, (s, w) in enumerate(FIELDS))
+    NMI, C8, CF_, CN, W8, VL, O64, RB, BS = (cf(j) for j in range(11, 20))
+    t = [cf(j) for j in range(20, 48)]
+    ts(t[0], I_, HUGE, A.mult)
+    ts(t[1], I_, 4 * HUGE, A.mult, 2 * HUGE, A.add)
+    act(B("yc"), B("bm16", 0, 224), ACT.Abs, t[0], -HUGE)
+    act(B("d0"), B("bm16", 0, 224), ACT.Relu, t[1], -4 * HUGE)
+    ts(B("dlb"), B("bm16", 0, 256), I_, A.is_gt, LOW8 + STEP8, A.mult)
     ts(B("dlb"), B("dlb"), -LOW8, A.add)
-    ts(B("dlf"), B("dlb"), STEP / STEP8, A.mult)
-    ts(B("dlo"), B("dlb"), STEP / STEP8, A.mult)
+    ts(t[9], I_, -STEP, A.mult, STEP / 2, A.add)
+    ts(B("dlc"), B("bm16"), STEP, A.mult, t[9], A.add)
+    ts(B("dlf"), B("bm16", 0, 128), STEP, A.mult, t[9], A.add)
+    fill(B("dlf", 15, 128, 16), -LOW)
     ts(NMI, MI, -1.0, A.mult, 1.0, A.add)
-    ts(M8, MI, 8.0, A.mult)
-    ts(C8, I_, STEP8, A.mult, -15.0 * STEP8, A.add)
-    ts(CN, I_, STEP, A.mult, -15.0 * STEP, A.add)
-    ts(CF_, CN, I_, A.add)
-    ts(CW, C8, M8, A.add)
-    ts(KA, O_, 2.0, A.mult, MI, A.add)
-    for k, s, o, j in ((K0, S2, N3, 0), (K1, MI, t[9], 3), (KA, SA, t[10], 6)):
-        ts(t[j], k, KQ, A.subtract, 4.0, A.mult)
-        ts(t[j + 1], k, KQ, A.is_lt, 16.0, A.mult)
-        ts(t[j + 2], s, 16.0, A.mult, t[j], A.add)
-        ts(o, t[j + 2], t[j + 1], A.add)
-    iota(B("i32"), [[64, 2]])
-    fill(B("ob", 0, 16), 0.0), fill(B("ob", 336, 352), 0.0)
-    ts(t[11], O_, 128.0, A.mult, t[9], A.add)
-    ts(t[27], Q1, 32.0, A.mult, 64.0, A.add)
-    ts(t[28], N3, 288.0, A.add)
-    ts(B("rll", 0, 2), B("i32"), t[11], A.add, t[27], A.add)
-    ts(B("rll", 2, 4), B("i32"), t[28], A.add, t[27], A.add)
-    cp(B("ptn"), N3)
-    ts(B("pto"), S2, 32.0, A.mult, t[10], A.add)
-    iota(B("llf"), [[16, 2], [1, 8]])
-    ts(t[12], I_, 8.0, A.mult)
-    ts(B("lln", 2, 10), B("llf", 0, 8), t[12], A.add)
-    ts(t[13], O_, 8.0, A.mult)
-    ts(t[14], J1, 32.0, A.mult, t[13], A.add)
-    ts(B("llo", 4, 20), B("llf"), t[14], A.add)
-    for o, at in ((B("lln", 0, 2), 120.0), (B("llo", 0, 2), 232.0), (B("llo", 2, 4), 248.0)):
-        ts(o, B("ob", 0, 2), V_, A.add, at, A.add)
-    iota(B("a16", 0, 32), [[0, 2], [16, 4], [0, 4]])
-    fill(B("a16", 32, 64), 0.0)
-    ts(t[20], KH, 16.0, A.mult)
-    ts(A16, HB, 32.0, A.mult, t[20], A.add)
-    ts(O64, O_, 64.0, A.mult)
-    ts(RB, GL, 320.0, A.mult, -159.75, A.add)
-    iota(B("i16"), [[16, 20]])
-    ts(B("cm"), B("i16"), CF_, A.add)
-    ts(t[21], HB, 320.0, A.mult)
-    ts(t[22], HB, -352.0, A.mult, 336.0, A.add)
-    ts(B("bs", 0, 20, 2), B("i16", 0, 20, 2), t[21], A.add)
-    ts(B("bs", 1, 20, 2), B("i16", 1, 20, 2), t[22], A.add)
-    tt(B("dlo", 15, 320, 16), B("dlo", 15, 320, 16), B("bs"), A.add)
-    iota(B("oc0"), [[0, 15], [32767, 2], [KEY, 8]], 160)
-    fill(B("oc", 88, 96), BIG), fill(B("pfo", 224, 232), BIG)
-    ts(t[29], I_, -float(KEY), A.mult, -32927.0, A.add)
-    ts(CO, CN, t[29], A.add)
-    iota(B("sd"), [[1, 320]], -160)
-    fill(B("mk", 0, 1024, 16), BIG)
-    fill(B("acl"), 0.0), fill(B("jv", 6060, 6080), 0.0)
+    ts(C8, I_, STEP8, A.mult, 8.0 - 15.0 * STEP8, A.add)
+    ts(t[10], I_, -1.0, A.mult, 15.0, A.add)
+    ts(t[11], I_, STEP / 2, A.mult, -7.5 * STEP, A.add)
+    ts(t[12], t[10], t[11], A.mult)
+    ts(CN, t[12], LOW, A.add)
+    ts(t[13], I_, LOW + 160.0, A.add)
+    ts(CF_, t[12], t[13], A.add)
+    fill(B("ob", 0, 16), 0.0), fill(B("ob", 336, 352), 0.0), fill(B("tr", 672, 704), 0.0)
+    iota(B("llf", 0, 16), [[16, 2], [1, 8]])
+    iota(B("llf", 16, 20), [[16, 2], [0, 2]], 232)
+    ts(t[2], I_, 8.0, A.mult)
+    ts(t[3], J1, 16.0, A.mult, t[2], A.add)
+    ts(B("llo", 0, 16), B("llf", 0, 16), t[3], A.add)
+    ts(B("llo", 16, 20), B("llf", 16, 20), V_, A.add)
+    ts(B("lln", 0, 8), B("llf", 0, 8), t[2], A.add)
+    ts(B("lln", 8, 10), B("llf", 16, 18), V_, A.add, -112.0, A.add)
+    for at, base in ((17, 192), (14, 64), (10, 128), (7, 0), (3, 64), (0, 0)):
+        iota(B("dlp", at, at + 4), [[4, 2], [8, 2]], base)
+    ts(t[4], Q1, 32.0, A.mult)
+    ts(t[5], MI, 16.0, A.mult, t[4], A.add)
+    ts(B("dl"), B("dlp", 1, 21), t[5], A.add)
+    ts(B("xl"), B("ob", 0, 12), V_, A.add)
+    ts(RB, GL, 1280.0, A.mult, -639.0, A.add)
+    ts(t[7], HB, -168.0, A.mult, 88.0, A.add)
+    ts(t[8], HB, 80.0, A.mult, CN, A.add)
+    ts(BS, MI, t[7], A.mult, t[8], A.add)
+    iota(B("oc"), [[8, 7], [0, 16]])
+    iota(B("xp"), [[0, 28], [KEY, 8]])
+    iota(B("sd"), [[4, 320]], -640)
+    iota(B("flo"), [[16, 20], [0, 16]], -160)
+    fill(B("acl", 0, 19), 128.0 - LOW), fill(B("acl", 19, 20), 0.0), fill(B("jv", 6060, 6080), -LOW)
     fill(B("rw0"), 0.0)
-    iota(B("xo", 0, 32), [[0, 4], [1, 8]])
-    iota(B("xn", 0, 16), [[0, 2], [1, 8]])
-    iota(B("a2", 0, 64), [[0, 8], [1, 8]])
-    iota(B("h1"), [[1, 4], [0, 2]])
-    iota(B("h2"), [[0, 4], [16, 2]])
-    ts(B("h3"), B("h1"), KQ, A.subtract, 4.0, A.mult)
-    ts(B("h4"), B("h1"), KQ, A.is_lt, 16.0, A.mult)
+    iota(B("xo", 0, 32), [[0, 4], [-KEY, 8]])
+    iota(B("xn", 0, 16), [[0, 2], [-KEY, 8]])
+    iota(B("lo", 0, 8), [[1, 8]])
+    iota(B("lo", 64, 72), [[1, 8]])
+    iota(B("pf", 0, 8), [[1, 2], [2, 2], [4, 2]])
+    iota(B("h1"), [[1, 2], [2, 2], [0, 2]])
+    iota(B("h2"), [[0, 4], [2, 2]], 640)
+    ts(B("h3"), B("h1"), GL, A.subtract, 1280.0, A.mult)
+    ts(B("h4"), B("h1"), GL, A.is_lt, 5120.0, A.mult)
     tt(B("h3"), B("h3"), B("h2"), A.add)
-    tt(B("pfn", 0, 8), B("h3"), B("h4"), A.add)
-    iota(B("h5"), [[0, 2], [1, 4]])
-    iota(B("h6"), [[1, 2], [0, 4]])
-    ts(B("h7"), B("h5"), GL, A.subtract, 320.0, A.mult)
-    ts(B("h8"), B("h5"), GL, A.is_lt, 1280.0, A.mult)
-    ts(B("h6"), B("h6"), 0.5, A.mult)
-    tt(B("h7"), B("h7"), B("h6"), A.add)
-    tt(B("pfn", 8, 16), B("h7"), B("h8"), A.add)
-    for j in range(2):
-        iota(B("ico", j, 128, 2), [[16, 4], [1000, 2], [1, 8]], 8 * j)
-        iota(B("ico", 128 + j, 256, 2), [[16, 4], [-1000, 2], [1, 8]], 1016 + 8 * j)
-    iota(B("ico", 256, 384), [[8, 4], [32, 2], [1, 16]])
+    tt(B("wp"), B("h3"), B("h4"), A.add)
+    iota(B("ico"), [[1, 64], [0, 2]])
     ts(W8, O_, -7.0, A.mult, 8.0, A.add)
-    clear(B("cab", 3, 1536, 4))
     ts(B("ico"), B("ico"), PH, A.is_equal, W8, A.mult)
-    for j, w in enumerate((4.0, 2.0, 1.0)):
-        ts(B("cab", j, 1536, 4), B("ico"), w, A.mult)
-    quant("ca", 0, 384, "cab", 0)
-    iota(B("m64"), [[1, 8], [0, 64]])
-    ts(B("ccb"), B("m64"), G_, A.is_equal, -1.0, A.mult)
+    for j, w in enumerate((4.0, 2.0, 1.0, 0.0)):
+        ts(B("cab", j, 512, 4), B("ico"), w, A.mult)
+    quant("ca", 0, 128, "cab", 0)
+    iota(B("m16"), [[1, 8], [0, 16]])
+    for j in range(4):
+        ts(B("ccb", j, 512, 4), B("m16"), G_, A.is_equal, -1.0, A.mult)
     quant("cc", 0, 128, "ccb", 0)
     op({"g": 350.0}, [B("chi")], [B("chb")], lambda e: e.partition_broadcast(view(B("chb")), T.chi[0:1, 0:64], 128))
     iota(B("m8"), [[0, 8], [1, 8]])
-    K["sooner"](2, MORE[0])
     cp(B("chf"), B("chb"))
     ts(B("k8"), B("m8"), V_, A.is_equal)
     act(B("d8"), B("m8"), ACT.Sign)
@@ -559,84 +610,71 @@ def rank_program(g, core, T, topo):
     for a in range(8):
         cp(B("tf", 128 * a, 128 * a + 128), ("@", B("chf", 8 * a, 8 * a + 8), B("lt")), "s")
     for a in range(4):
-        latch(B("tl", 256 * a, 256 * a + 256), B("tf", 256 * a, 256 * a + 256), B("dlb", 0, 256))
-    for j in range(2):
-        ts(t[24 + j], C8, 8.0 + 16 * j, A.add)
-        ts(B("tab", 64 * j, 64 * j + 64), B("tl", 15, 1024, 16), t[24 + j], A.add)
-    iota(B("li"), [[-128, 2], [1, 64], [64, 4]])
-    ts(t[32], KH, 1024.0, A.mult, B("pi"), A.add)
-    ts(t[33], KH, -1088.0, A.mult, 1024.0, A.add)
-    ts(t[34], t[33], B("pi"), A.add)
-    for k in range(4):
-        ts(B("lb", 512 * k, 512 * k + 512), B("li"), -64.0 * (k % 2), A.add, t[32 + 2 * (k // 2)], A.is_equal)
-    quant("lq", 0, 512, "lb", 0)
-    for b in range(4):
-        o = B("eb", 512 * b, 512 * b + 512)
-        op({"g": 1020.0}, [B("one")], [o], lambda e, o=o, b=b: e.affine_select(view(o), view(B("one")), [[-4, 128], [-1, 4]], A.is_equal, 0.0, b, 4))
-    quant("eq", 0, 512, "eb", 0)
+        scan(B("tl", 256 * a, 256 * a + 256), B("dlb"), B("tf", 256 * a, 256 * a + 256), A.add, A.max)
+    ts(B("tab"), B("tl", 15, 1024, 16), C8, A.add)
+    for e in range(2):
+        for a in range(2):
+            o = B("lb", 1024 * e + 512 * (1 - a), 1024 * e + 512 * (2 - a))
+            op({"g": 1020.0}, [B("one")], [o], lambda q, o=o, e=e, a=a: q.affine_select(view(o), view(B("one")), [[-2, 2], [-8, 64], [1, 4]], A.is_equal, 0.0, -512 * a - e, 8))
+        quant("lq", 384 * e + 64, 384 * e + 320, "lb", 1024 * e)
 
     def calls(p, x):
         if p == "o":
+            bk = BANK["co"]
             for j, lo in enumerate((96, 192)):
-                mm(2 + j, 128, x, lo, "uq", 0)
-                ts(B("bt", 8 * j, 8 * j + 3), ps(2 + j, 1, 4), 0.0, A.is_gt)
-            quant("bqo", 0, 130, "bt", 0)
-            mm(2, 128, "ca", 0, "bqo", 0, True, False)
-            mm(2, 128, "ca", 128, "bqo", 2, False, True)
-            ts(B("ixo"), ps(2, 0, 1), O64, A.add)
-            cp(B("lio"), ("@", B("tab"), B("ixo")))
+                mm(bk[j], 128, x, PAD + lo, "uq", 0)
+                ts(B("bt", 8 * j, 8 * j + 3), ps(bk[j], 1, 4), 0.0, A.is_gt)
+            quant("bqo", 0, 128, "bt", 0)
+            mm(bk[0], 128, "ca", 0, "bqo", 0)
+            cp(B("ixo", 0, 4, 2), ("ps%d" % bk[0], 0, 4, 2, 0, 128))
+            for j in range(2):
+                ts(B("lco", j, 32, 2), ("@", B("tab"), B("ixo", 2 * j, 2 * j + 1)), 16.0 * j, A.add)
         else:
-            mm(1, 128, x, 0, "uq", 0)
-            ts(B("bt", 16, 19), ps(1, 1, 4), 0.0, A.is_gt)
-            quant("bqn", 0, 128, "bt", 16)
-            mm(1, 128, "ca", 256, "bqn", 0)
-            cp(B("ixn"), ps(1, 0, 1))
-            cp(B("lin", 0, 32, 2), ("@", B("tab"), B("ixn")))
+            bk = BANK["cn"]
+            mm(bk, 128, x, 0, "uq", 0)
+            ts(B("bs", 0, 3), ps(bk, 1, 4), 0.0, A.is_gt)
+            quant("bqn", 0, 128, "bs", 0)
+            mm(bk, 128, "ca", 0, "bqn", 0)
+            cp(B("ixn"), ps(bk, 0, 1))
+            cp(B("lcn"), ("@", B("tab"), B("ixn")))
 
-    def pieces(p):
-        x, n = "x" + p, 2 if p == "o" else 1
+    def product(m):
+        j, grp = (0, m + 2) if m < 6 else (1, m - 6) if m < 14 else (2, m - 12)
+        at = 2 * (8 * j + 4 * (grp % 2) + POS[grp // 2] // 4)
+        return B("lp", at, at + 1)
+
+    def step(n, at, m, add=0.0):
+        o, i = B(n, at + 8, at + 24), ("@", B(n, at, at + 8), product(m))
+        if add:
+            ts(o, i, add, A.add, qs=PIN["chain"])
+        else:
+            cp(o, i, PIN["chain"])
+
+    def rows(p):
+        x, n, lo, hi = ("xo", 2, 6, 20) if p == "o" else ("xn", 1, 0, 6)
         w = 16 * n
         for e in range(8):
-            cp(B(x, w * e + w, w * e + 2 * w), ("@", B(x, w * e, w * e + w), B("li" + p, 2 * e, 2 * e + n)), PIN["chain"])
-        got = ("@", B(x, w, 9 * w), B("ll" + p))
-        if p == "o":
-            ts(B("zo"), got, A16, A.add, qs=PIN["rows"])
-        else:
-            cp(B("zn"), got, PIN["rows"])
+            cp(B(x, w * e + w, w * e + 2 * w), ("@", B(x, w * e, w * e + w), B("lc" + p, 2 * n * e, 2 * n * e + n)), PIN["chain"])
+        cp(B("z" + p), ("@", B(x, w, 9 * w), B("ll" + p)), PIN["rows"])
         turn(B("rt" + p), B("z" + p))
         share("rt" + p, 10 * w)
+        ts(B("lp", w - 16, 2 * w - 16, 2), B("rt" + p, 8 * w, 10 * w, 4), -1.0 / KEY, A.mult)
+        tt(B("dd", 16 * lo, 16 * hi), ("@", B("rt" + p), B("dl", lo, hi)), B("xp", 0, 16 * (hi - lo)), A.add)
         if p == "o":
-            cp(B("lpo"), ("@", B("rto"), B("pto")))
-            for j in range(4):
-                cp(B("a2", 64 * j + 64, 64 * j + 128), ("@", B("a2", 64 * j, 64 * j + 64), B("lpo", 4 * j, 4 * j + 4)), PIN["chain"])
-            latch(B("wa"), B("a2"), B("dlb"))
-            ts(B("l2", 0, 6, 2), B("wa", 271, 304, 16), CW, A.add)
-            for a in range(4):
-                ts(B("lf", 4 * a, 4 * a + 4), B("wa", 16 * a + 15, 256, 64), CW, A.add, 16.0 * a, A.add)
-        else:
-            ts(B("lpn", 0, 32, 2), ("@", B("rtn"), B("ptn")), M8, A.add)
-            for e in range(6):
-                cp(B("pfn", 16 * e + 16, 16 * e + 32), ("@", B("pfn", 16 * e, 16 * e + 16), B("lpn", 2 * e, 2 * e + 1)), PIN["chain"])
-            for a in range(3):
-                cp(B("pfn", 112 + 16 * a, 128 + 16 * a), ("@", B("pfn", 96 + 16 * a, 112 + 16 * a), B("l2", 2 * a, 2 * a + 1)), PIN["chain"])
-            tt(B("pfo", 0, 224), ("@", B("pfn", 96, 160), B("lf", 0, 14)), B("oc0", 8, 232), A.add)
-            tt(B("oc", 0, 88), B("pfn", 8, 96), B("oc0", 0, 88), A.add)
-            for pf, lo, hi, c in (("pfn", 0, 96, CN), ("pfo", 96, 320, CO)):
-                latch(B("wl", lo, hi), B(pf, 0, hi - lo), B("dlo", lo, hi))
-                ts(B("otl", lo // 16, hi // 16), B("wl", lo + 15, hi, 16), c, A.add, NMI, A.mult)
-        if p == "o":
+            for m in range(6, 19):
+                step("lo", 8 * (m - 6 if m < 12 else m - 4), m)
+            latch(B("wo"), B("lo", 0, 128), B("dlf", 0, 128))
+            ts(B("lf"), B("wo", 15, 128, 16), CN, A.add)
             return
-        i = B("rr")
-        tt(i, ("@", B("rto", 0, 480), B("rll")), B("a16"), A.subtract)
-        for e in range(1, 8):
-            o = B("mk", e, 1024, 16)
-
-            def fn(q, o=o, e=e):
-                if q is g.vector:
-                    return q.tensor_scalar(view(o), view(i), float(e), BIG, A.is_ge, A.mult)
-                return q.activation(view(o), view(i), ACT.Relu, bias=BIG * (0.5 - e), scale=BIG)
-            op(costs(PIN["mask"], o, [i]), [i], [o], fn)
-        ts(B("mk", 8, 1024, 16), i, -float(KEY), A.mult, qs=PIN["mask"])
+        for m in range(6):
+            step("pf", 8 * m, m, 8.0 * (m % 2))
+        latch(B("wn"), B("pf", 0, 48), B("dlf", 0, 48))
+        ts(B("otl", 0, 3), B("wn", 15, 48, 16), BS, A.add)
+        cp(B("pc"), ("@", B("pf", 48, 56), B("lf", 2, 4)), PIN["chain"])
+        tt(B("pq", 0, 48), ("@", B("pf", 48, 56), B("lf", 0, 3)), B("oc", 0, 48), A.add)
+        tt(B("pq", 48, 112), ("@", B("pc", 16, 24), B("lf", 4, 8)), B("oc", 48, 112), A.add)
+        latch(B("wc2"), B("pq"), B("dlf", 0, 112))
+        ts(B("otl", 4, 11), B("wc2", 15, 112, 16), BS, A.add)
 
     turns = []
 
@@ -657,8 +695,10 @@ def rank_program(g, core, T, topo):
         return B(tile, at + 4 * (lo - c0) + e, at + 4 * (hi - c0), 4)
 
     def scores(p, x):
-        bank, c0, n, w = (0, 96, 224, 224) if p == "o" else (2, 0, 96, 320)
-        mm(bank, w, "ur", 0, x, c0)
+        bank, c0, n, w = (BANK["so"], 96, 224, 224) if p == "o" else (BANK["sn"], 0, 96, 320)
+        mm(bank, w, "ur", 0, x, PAD + c0)
+        if p == "n" and min(ALONE) < 6:
+            mm(BANK["sn2"], w, "ur", 0, x, PAD + c0)
         tt(B("y" + p), ps(bank, 0, n), B("yc", 0, n), A.add)
         if p == "o":
             cp(B("sco"), ps(bank, 0, n), "s")
@@ -667,30 +707,32 @@ def rank_program(g, core, T, topo):
     def within(p):
         c0, n = (96, 224) if p == "o" else (0, 96)
         d = slot("g" + p, 0, 0, c0, c0 + n)
-        tt(d, ps(0 if p == "o" else 2, 0, n), B("so" + p), A.is_gt)
-        scan(B("dcs", c0, c0 + n), B("dr", 0, n), d, A.mult, A.add)
+        tt(d, ps(BANK["s" + p], 0, n), B("so" + p), A.is_gt)
+        scan(B("dcs", c0, c0 + n), d, B("flo", c0, c0 + n), A.add, A.max, -1000.0)
 
     def compare(p):
         c0 = 96 if p == "o" else 0
 
-        def row(lo, hi):
-            return B("sco", lo - c0, hi - c0) if p == "o" else ps(2, lo, hi)
+        def row(lo, hi, q):
+            if p == "n":
+                return ps(BANK["sn" if q == "v" else "sn2"], lo, hi)
+            return ps(BANK["so"], lo - c0, hi - c0) if q == "v" and HOLD else B("sco", lo - c0, hi - c0)
         for k in range(13 if p == "o" else 6):
-            lo = c0 + 16 * k + 16
+            lo, m = c0 + 16 * k + 16, c0 // 16 + k
             if p == "o" and k > 10:
                 o = slot("gn", k - 11, 3 * (k - 11), lo, 320)
             else:
                 o = slot("g" + p, (k + 1) // 4, (k + 1) % 4, lo, 320)
-            own, acc = B("so" + p, 16 * k + 15, 16 * k + 16), B("acl", c0 // 16 + k, c0 // 16 + k + 1)
-            if p == "o" and k in ALONE:
-                i, j = row(lo, 320), B("sg", 208 * (k % 2), 208 * (k % 2) + 320 - lo)
+            own, acc = B("so" + p, 16 * k + 15, 16 * k + 16), B("acl", m, m + 1)
+            if m in ALONE:
+                at = 304 * (ALONE.index(m) % 2)
+                i, j = row(lo, 320, "s"), B("sg", at, at + 320 - lo)
                 op(costs("s", j, [i]), [i, own], [j], lambda e, i=i, j=j, own=own: e.activation(view(j), view(i), ACT.Sign, bias=view(own), scale=-1.0))
                 op({"s": 20 + ac(j, [])}, [j], [o, acc], lambda e, j=j, o=o, acc=acc: e.activation(view(o), view(j), ACT.Relu, scale=-1.0, accum_out=view(acc)))
             else:
-                ts(o, row(lo, 320), own, A.is_gt)
-                m = c0 // 16 + k
-                if m in SCAN:
-                    scan(B("jv", 6080 - 20 * (320 - lo) + m, 6080, 20), B("one", 0, 320 - lo), o, A.mult, A.add)
+                ts(o, row(lo, 320, "v"), own, A.is_gt)
+                if m not in COUNT:
+                    scan(B("jv", 6080 - 20 * (320 - lo) + m, 6080, 20), B("one", 0, 320 - lo), o, A.mult, A.add, -128.0)
                 else:
                     count(o, acc)
         for q, (at, lo) in enumerate(GO if p == "o" else GN):
@@ -700,11 +742,10 @@ def rank_program(g, core, T, topo):
 
     def window(p, x, r):
         c0, n = (96, 224) if p == "o" else (0, 96)
+        bk, skip = BANK["w" + p], 0 if p == "o" else PAD
         for k in range(4):
-            mm(4 + k, max(n, 128), "lq", 128 * k, x, c0)
-        for k in range(4):
-            cp(B("win", 4 * c0 + k, 4 * (c0 + n), 4), ps(4 + k, 0, n), PIN["win"])
-        K["sooner"](8, MORE[1 if p == "o" else 2])
+            mm(bk[k], n + skip, "lq", 384 * (k % 2) + 192 - 128 * (k // 2), x, PAD + c0 - skip)
+            cp(B("win", 4 * c0 + k, 4 * (c0 + n), 4), ps(bk[k], skip, skip + n), PIN["win"])
         lo, hi = 4 * c0, 4 * (c0 + n)
         for s in range(1, 4):
             for h in (0, 64):
@@ -714,12 +755,14 @@ def rank_program(g, core, T, topo):
 
     def one_round(r):
         x = "qx%d" % r
+        if r and FIRST:
+            arrive(r)
         calls("o", x)
+        rows("o")
         scores("o", x)
-        pieces("o")
         within("o")
         window("o", x, r)
-        if r:
+        if r and not FIRST:
             arrive(r)
         compare("o")
         calls("n", x)
@@ -727,40 +770,39 @@ def rank_program(g, core, T, topo):
         within("n")
         compare("n")
         window("n", x, r)
-        if r == 1:
-            later_loads()
-        pieces("n")
-        tt(B("rc1"), B("dcs", 15, 320, 16), B("cm"), A.add)
-        tt(B("rc3"), B("rc1"), B("jv", 6060, 6080), A.add)
-        tt(B("rc2"), B("rc3"), B("acl"), A.add)
-        latch(B("cl"), ps(3, 0, 320), B("dlf"))
-        tt(B("rkf"), B("cl", 15, 320, 16), B("rc2"), A.add)
-        cp(B("rk"), B("rkf"))
+        later_loads(r)
+        rows("n")
+        tt(B("rc1"), B("dcs", 15, 320, 16), B("jv", 6060, 6080), A.add)
+        tt(B("dlc", 15, 320, 16), B("rc1"), B("acl"), A.add)
+        latch(B("cl"), ps(3, 0, 320), B("dlc"))
+        ts(B("rk"), B("cl", 15, 320, 16), CF_, A.add)
         w = B("ob", 16, 336)
         op({"v": 50 + 3.3 * CY * 320}, [B("rk"), B("sd")], [w], lambda e: e.tensor_copy(view(w).indirect(view(B("rk"))), view(B("sd"))))
         turn(B("tr", 0, 320), w)
         turn(B("tr", 320, 672), B("ob"))
         share("tr", 672)
+        tt(B("tq"), ("@", B("wp"), B("xl", 0, 11)), B("tr", 0, 704, 4), A.add)
         for p, m0, n, l0 in (("n", 0, 6, 0), ("o", 6, 14, 24)):
-            ot, m1 = B("ot", 16 * m0, 16 * (m0 + n)), 512 if p == "n" else 0
-            tt(ot, ("@", B("tr"), B("otl", m0, m0 + n)), B("oc") if p == "n" else B("pfo", 8, 232), A.add)
+            lo, hi, at = 16 * m0, 16 * (m0 + n), 0 if p == "n" else 4
             for G in range(2):
-                o = 8 * l0 + 16 * n * G
-                scan(B("sc", o, o + 16 * n), B("mk", 256 * G + m1, 256 * G + m1 + 16 * n), ot, A.add, A.min)
+                o = lo + 8 * n * G
+                tt(B("ot", o, o + 8 * n), ("@", B("tq"), B("otl", at, at + n // 2)), B("dd", o, o + 8 * n), A.subtract)
+            scan(B("sc", lo, hi), B("dd", lo, hi), B("ot", lo, hi), A.min, A.max)
             for e in range(2):
-                ts(B("il", l0 + 2 * n * e, l0 + 2 * n * (e + 1)), B("sc", 8 * l0 + 15, 8 * l0 + 32 * n, 16), 4.0, A.mult, float(e), A.add)
+                ts(B("il", l0 + 2 * n * e, l0 + 2 * n * (e + 1)), B("sc", lo + 7, hi, 8), float(e), A.add)
             step = 12 if p == "n" else 14
             for l in range(l0, l0 + 4 * n, step):
                 cp(B("st", 16 * l, 16 * (l + step)), ("@", B("win"), B("il", l, l + step)), PIN["pick"])
             for e in range(4):
                 for G in range(2):
-                    o, l = B("ta" if p == "n" else "tb", 64 * m0 + e, 64 * (m0 + n), 4, (64 * G, 64 * G + 64)), l0 + n * (2 * (e % 2) + G)
+                    c = 0 if p == "n" else 512
+                    o, l = B("ta" if p == "n" else "tb", c + e, c + 64 * n, 4, (64 * G, 64 * G + 64)), l0 + n * (2 * (e % 2) + G)
                     cp(o, B("st", 16 * l, 16 * (l + n), 1, (64 * (e // 2), 64 * (e // 2) + 64)), PIN["lay"])
             if p == "n":
                 quant("qs%d" % (r + 1), 0, 128, "ta", 0)
                 send(r + 1)
             else:
-                quant("qx%d" % (r + 1), 96, 320, "tb", 384)
+                quant("qx%d" % (r + 1), 128, 352, "tb", 512)
 
     def send(r):
         t = "qs%d" % r
@@ -782,37 +824,39 @@ def rank_program(g, core, T, topo):
         frm = T.cores[(rank - r) % len(T.cores)]
         n = 2 * len(topo.engines(frm, core))
         raw("t", [("sent%d" % r, 0, 1, 1, 0, 128)], [B("ld%dc" % r, 0, 96), B("ld%ds" % r, 0, 96)], lambda: K["wait"]("t", "rc%d" % r, n, {}), 1.0)
-        bank = (1, 3, 0, 2)
+        bw, be = BANK["lw"], BANK["le"]
         for b in range(4):
-            mm(4 + b, 128, "wq", 128 * b, "ld%d" % r, 0)
-            mm(bank[b], 128, "eq", 128 * b, "ld%d" % r, 0)
-            o, i = B("rl", 96 * b, 96 * b + 96), ps(4 + b, 0, 96)
+            mm(bw[b], 128, "wq", 128 * b, "ld%d" % r, 0)
+            o, i = B("rl", 96 * b, 96 * b + 96), ps(bw[b], 0, 96)
 
             def fn(e, o=o, i=i):
                 if e is g.vector:
                     return e.tensor_scalar(view(o), view(i), 0.0, 0.03125, A.max, A.mult)
                 return e.activation(view(o), view(i), ACT.Relu, scale=0.03125)
             op(costs(PIN["relu"], o, [i]), [i], [o], fn)
-            tt(B("tb", b, 384, 4), o, ps(bank[b], 0, 96), A.add)
+            mm(be[b], 128, "lq", 384 * (b % 2) + 256 * (b // 2), "ld%d" % r, 0)
+            tt(B("tb", 128 + b, 512, 4), o, ps(be[b], 0, 96), A.add)
         quant("qx%d" % r, 0, 128, "tb", 0)
 
     def store(lo, hi, bank):
-        x = "qx%d" % ROUNDS
-        mm(bank, hi - lo, "vq", 0, x, lo)
-        cp(B("yb", lo, hi), ps(bank, 0, hi - lo))
-        dma("s" if lo == 0 else "y", "out", [B(x + "c", lo, hi)], [], T.oc[:, 4 * lo:4 * hi], view(B(x + "c", lo, hi)).bitcast(dt.uint8))
+        x, skip = "qx%d" % ROUNDS, 0 if lo else PAD
+        mm(bank, hi - lo + skip, "vq", 0, x, PAD + lo - skip)
+        cp(B("yb", lo, hi), ps(bank, skip, skip + hi - lo))
+        c = B(x + "c", PAD + lo, PAD + hi)
+        dma("s" if lo == 0 else "y", "out", [c], [], T.oc[:, 4 * lo:4 * hi], bits(c))
         for k in range(4):
-            dma("y", "out", [B(x + "s", lo, hi, 1, (32 * k, 32 * k + 4))], [], T.osc[4 * k:4 * k + 4, lo:hi], T[x + "s"][32 * k:32 * k + 4, lo:hi])
+            s = B(x + "s", PAD + lo, PAD + hi, 1, (32 * k, 32 * k + 4))
+            dma("y", "out", [s], [], T.osc[4 * k:4 * k + 4, lo:hi], view(s))
         dma("y", "out", [B("yb", lo, hi)], [], T.y[:, lo:hi], T.yb[:, lo:hi])
 
     for r in range(ROUNDS):
         one_round(r)
     for m0, n, l0 in ((0, 6, 0), (6, 14, 24)):
         for G in range(2):
-            o = 8 * l0 + 16 * n * G
-            cp(B("rw0", 32 * G + m0, 32 * G + m0 + n), B("sc", o + 15, o + 16 * n, 16))
-    ts(B("rw1"), B("rw0"), RB, A.add, 1.0 / 320, A.mult)
-    ts(B("rw2"), B("rw0"), 2.0, A.mult)
+            o = 16 * m0 + 8 * n * G
+            cp(B("rw0", 32 * G + m0, 32 * G + m0 + n), B("sc", o + 7, o + 8 * n, 8))
+    ts(B("rw1"), B("rw0"), RB, A.add, 1.0 / 1280, A.mult)
+    ts(B("rw2"), B("rw0"), 0.5, A.mult)
     for n, f, m in (("rwi", "rw1", 3), ("rwj", "rw2", 1)):
         cp(B(n), B(f))
         ts(B(n), B(n), m, A.bitwise_and)
@@ -822,9 +866,12 @@ def rank_program(g, core, T, topo):
     for h in range(8):
         q, c = 32 * (h // 2 % 2), 32 * (h // 4) + 16 * (h % 2)
         dma("y", "out", [B("rwb", c, c + 16, 1, (q, q + 20))], [], T.rw[h, :], T.rwb[q:q + 20, c:c + 16])
-    store(128, 320, 0)
-    arrive(3)
-    store(0, 128, 1)
+    if FIRST:
+        arrive(3)
+    store(96, 320, BANK["so"])
+    if not FIRST:
+        arrive(3)
+    store(0, 96, BANK["cn"])
     K["run"]()
     for sem, n in sorted(K["total"].items()):
         K["wait"]("g", sem, n, {})

@@ -3,22 +3,21 @@ import numpy as np
 from concourse.mybir import dt, AluOpType, AxisListType, ActivationFunctionType
 
 CY = 0.83
-HOP = 200.0
-TRIES = 4000
-MOVES = 80000
+HOP = 250.0
+TRIES = 6000
+MOVES = 100000
 SEED = 1
 REACH, MEAN, WARM = 40, 1.0, 5.0
 SPAN, SIGMA, HEAT = 0.04, 800.0, 20.0
 ALONE = (0, 1, 6, 7, 8)
 COUNT = ()
-HOLD = True
-DEAR = {"v": 1.6, "s": 1.0, "g": 1.0, "t": 1.0, "y": 1.0}
+DEAR = {"v": 2.5, "s": 1.0, "g": 1.0, "t": 1.0, "y": 1.0}
 ROUNDS = 3
 STEP, LOW = 1024.0, 131072.0
 STEP8, LOW8 = 8.0, 256.0
-KEY, HUGE = 8192, 2.0 ** 92
+KEY, HUGE = 8192.0, 2.0 ** 92
 POS = (0, 8, 4, 12)
-FIELDS = ((4, 1), (3, 1), (0, 4), (0, 3), (1, 6), (0, 1), (4, 3), (1, 3), (6, 1), (5, 1), (4, 2))
+FIELDS = ((4, 1), (3, 1), (0, 4), (0, 3), (1, 6), (0, 1), (4, 3), (1, 3), (5, 2), (4, 2), (5, 1), (6, 1))
 F32, BF, I32, U16 = "float32", "bfloat16", "int32", "uint16"
 CODE, SC = "float8_e4m3fn_x4", "uint8"
 SIZE = {F32: 4, BF: 2, I32: 4, U16: 2, CODE: 4, SC: 1}
@@ -27,7 +26,7 @@ GN = ((0, 0), (1280, 64))
 PAD = 32
 FIRST = False
 BANK = {"co": (1, 2), "so": 0, "wo": (4, 5, 6, 7), "lw": (4, 5, 6, 7), "le": (1, 2, 3, 4), "cn": 5, "sn": 6, "sn2": 7, "wn": (1, 2, 4, 1)}
-PIN = {"chain": "vs", "count": "vs", "shift": "vsg", "lay": "vsg", "win": "vs", "pick": "vs", "mask": "vs", "rows": "vs", "relu": "vs"}
+PIN = {"swap": "vs", "chain": "vs", "count": "vs", "shift": "vsg", "lay": "vsg", "win": "vs", "pick": "vs", "mask": "vs", "rows": "vs", "relu": "vs"}
 
 
 def _scratch():
@@ -41,30 +40,30 @@ def _scratch():
         sb(name + "s", n, SC)
     for b in range(8):
         d["ps%d" % b] = ("psum", [128, 512], F32)
-    for n, w in (("xb", 1408), ("ub", 512), ("vb", 512), ("lb", 2048), ("zb", 768), ("ccb", 512), ("cab", 512), ("one", 512),
-                 ("bt", 512), ("bs", 512), ("ta", 512), ("tb", 1408), ("st", 1280), ("win", 5120), ("go", 2048), ("gn", 2304), ("jk", 1280),
+    for n, w in (("xb", 1472), ("ub", 512), ("vb", 512), ("lb", 2048), ("zb", 768), ("ccb", 512), ("cab", 512),
+                 ("bt", 528), ("ta", 512), ("tb", 1472), ("st", 1280), ("win", 8960), ("go", 2048), ("gn", 2304), ("jk", 1280),
                  ("m16", 128), ("ico", 128)):
         sb(n, w, BF)
     for n, w in (("uq", 128), ("ur", 128), ("vq", 128), ("lq", 768), ("wq", 512), ("cc", 128), ("ca", 128), ("bqo", 128),
                  ("bqn", 128), ("gq", 1600)):
         mx(n, w)
     for r in range(ROUNDS + 1):
-        mx("qx%d" % r, PAD + 320)
+        mx("qx%d" % r, PAD + 336)
         if r:
             mx("ld%d" % r, 128)
             mx("qs%d" % r, 128)
     sb("bi", 7, I32), sb("pi", 1), sb("half", 7), sb("pw", 7), sb("fl", 7), sb("chi", 64, I32), sb("chb", 64, I32), sb("rwi", 64, I32), sb("rwj", 64, I32)
-    for n, w in (("cf", 48), ("ulf", 8), ("llf", 30), ("dlp", 21), ("oc", 112), ("dlf", 128), ("dlc", 320),
+    for n, w in (("cf", 48), ("ulf", 8), ("llf", 30), ("dlp", 21), ("dlf", 112), ("dlc", 320),
                  ("yc", 224), ("d0", 224), ("chf", 64), ("m8", 64), ("k8", 64), ("d8", 64), ("cht", 64), ("chs", 64), ("yo", 224), ("soo", 224), ("sco", 224),
                  ("yn", 96), ("son", 96), ("acl", 20), ("rc1", 20), ("rc2", 20), ("cl", 320), ("rkf", 20), ("ot", 320), ("sc", 320), ("rl", 384),
-                 ("yb", 320), ("rw0", 64), ("rw1", 64), ("rw2", 64), ("rw3", 64), ("rwb", 64), ("h1", 8), ("h2", 8), ("h3", 8), ("h4", 8), ("wp", 8),
-                 ("pf", 72), ("lo", 144), ("pc", 32), ("pq", 112), ("wn", 48), ("wo", 128), ("wc2", 112), ("tq", 176)):
+                 ("yb", 320), ("rw0", 64), ("rw1", 64), ("rw2", 64), ("rw3", 64), ("rwb", 64),
+                 ("pf", 64), ("lo", 128), ("l2", 112), ("pq", 112), ("ro", 112), ("wn", 64), ("wo", 112), ("r32", 7), ("sd", 320), ("ob", 352), ("trn", 224), ("tro", 480)):
         sb(n, w)
-    for n, w in (("bm16", 320), ("flo", 320), ("dlb", 256), ("sd", 320), ("ob", 352), ("tr", 704), ("dcs", 320), ("tf", 1024), ("tl", 1024), ("tab", 64),
-                 ("xo", 288), ("xn", 144), ("zo", 320), ("zn", 160), ("rto", 320), ("rtn", 160), ("xp", 224), ("dd", 320), ("jv", 6080), ("sg", 608)):
+    for n, w in (("bm16", 320), ("flo", 320), ("dlb", 256), ("dcs", 320), ("tf", 1024), ("tl", 1024), ("tab", 64),
+                 ("xo", 288), ("xn", 144), ("zo", 288), ("zn", 160), ("rto", 288), ("rtn", 160), ("xp", 224), ("dd", 208), ("d8o", 112), ("jv", 6080), ("sg", 608)):
         sb(n, w, BF + "*")
-    for n, w in (("ul", 8), ("otl", 12), ("llo", 20), ("lln", 10), ("dl", 20), ("xl", 12), ("lt", 8), ("ixo", 4), ("ixn", 1),
-                 ("lco", 32), ("lcn", 16), ("lp", 48), ("lf", 8), ("rk", 20), ("il", 80)):
+    for n, w in (("ul", 8), ("otl", 12), ("llo", 18), ("lln", 10), ("dl", 14), ("lt", 8), ("ixo", 4), ("ixn", 1),
+                 ("lco", 32), ("lcn", 16), ("lp", 48), ("lf", 8), ("nl", 8), ("rk", 20), ("il", 80)):
         sb(n, w, U16)
     return d
 
@@ -299,7 +298,7 @@ def _make(g, T):
     def dma(q, sem, reads, writes, out, in_):
         a = (writes or reads)[0]
         rows, row = a[5] - a[4], (a[2] - a[1]) * SIZE[SCRATCH[a[0]][2]]
-        jobs.append(dict(c={q: 60.0}, r=reads, w=writes, fn=(out, in_), lat=1300.0, dur=-(-rows // 16) * (30 + row / 12.0), sem=sem))
+        jobs.append(dict(c=dict.fromkeys(q, 60.0), r=reads, w=writes, fn=(out, in_), lat=1300.0, dur=-(-rows // 16) * (30 + row / 12.0), sem=sem))
 
     def raw(q, reads, writes, fn, cost, lat=0.0, dur=0.0):
         jobs.append(dict(c={q: cost}, r=reads, w=writes, fn=fn, lat=lat, dur=dur, sem="raw"))
@@ -477,7 +476,7 @@ def rank_program(g, core, T, topo):
         op(costs("s", out, [in_]), [in_] + r, [out], lambda e: e.activation(view(out), view(in_), f, bias=x, scale=scale))
 
     dma("s", "dc", [], [B("chi", p=(0, 1))], T.chi[0:1, 0:64], T.ch[:, :])
-    dma("y", "dx", [], [B("xb", 128)], view(B("xb", 128)), T.x[:, :])
+    dma("y", "dx", [], [B("xb", 128, 1408)], view(B("xb", 128, 1408)), T.x[:, :])
     dma("y", "du", [], [B("ub")], view(B("ub")), T.u[:, :])
     fill(B("zb"), 0.0)
     quant("gq", 640, 832, "zb", 0)
@@ -486,7 +485,7 @@ def rank_program(g, core, T, topo):
             o, i = B("gq" + k, lo, hi), B("gq" + k, 640, 640 + hi - lo)
             dma("y", "z4", [i], [o], bits(o), bits(i))
     for a in (B("go", 0, 192), B("go", 896, 1088), B("go", 1536, 1856), B("gn", 0, 192), B("gn", 384, 1152, 4), B("gn", 1280, 1408), B("gn", 1283, 2240, 4),
-              B("ta", 384, 512), B("bt"), B("bs"), B("xb", 0, 128), B("tb", 0, 128)):
+              B("ta", 384, 512), B("bt"), B("xb", 0, 128), B("tb", 0, 128), B("xb", 1408), B("tb", 1408)):
         clear(a)
 
     def beside(r, sem, after):
@@ -498,7 +497,7 @@ def rank_program(g, core, T, topo):
     dma("y", "dw", [B("gqc", 640, 672)], [B("wqs")], view(B("wqs")), T.ws[:, :])
 
     def later_loads(r):
-        after = [B("win", 1280, 1296)]
+        after = [B("win", 5120, 5136)]
         if r == 0:
             for e in range(2):
                 for to, frm in ((0, 3), (5, 2)):
@@ -515,10 +514,9 @@ def rank_program(g, core, T, topo):
     fill(B("half"), 0.5)
     iota(B("ulf"), [[16, 8]])
     iota(B("bm16"), [[0, 20], [1, 16]])
-    fill(B("one"), 1.0)
     cp(B("ul"), B("ulf"))
     quant("uq", 0, 128, "ub", 0)
-    quant("qx0", 0, PAD + 320, "xb", 0)
+    quant("qx0", 0, PAD + 336, "xb", 0)
     op({"v": 210.0}, [B("uqc"), B("ul")], [B("urc")], lambda e: e.tensor_copy(T.urc[:, 0:128].bitcast(dt.uint32), T.uqc[:, 0:128].bitcast(dt.uint32).indirect(view(B("ul")))))
     op({"s": 225.0}, [B("uqs"), B("ul")], [B("urs")], lambda e: e.activation(T.urs[:, 0:128], T.uqs[:, 0:128].indirect(view(B("ul"))), ACT.Copy))
     scan(B("pw"), B("half"), B("zb", 0, 7), A.mult, A.add, 2.0)
@@ -531,8 +529,8 @@ def rank_program(g, core, T, topo):
             return B("fl", s, s + 1)
         ts(cf(j), B("fl", s + w, s + w + 1), -float(1 << w), A.mult, B("fl", s, s + 1), A.add)
         return cf(j)
-    HB, MI, I_, V_, PH, O_, G_, J1, KH, Q1, GL = (field(j, s, w) for j, (s, w) in enumerate(FIELDS))
-    NMI, C8, CF_, CN, W8, VL, O64, RB, BS = (cf(j) for j in range(11, 20))
+    HB, MI, I_, V_, PH, O_, G_, J1, KQ, GL, Q1, KH = (field(j, s, w) for j, (s, w) in enumerate(FIELDS))
+    NMI, C8, CF_, CN, W8, VL, M8, BN, BO = (cf(j) for j in range(11, 20))
     t = [cf(j) for j in range(20, 48)]
     ts(t[0], I_, HUGE, A.mult)
     ts(t[1], I_, 4 * HUGE, A.mult, 2 * HUGE, A.add)
@@ -542,8 +540,8 @@ def rank_program(g, core, T, topo):
     ts(B("dlb"), B("dlb"), -LOW8, A.add)
     ts(t[9], I_, -STEP, A.mult, STEP / 2, A.add)
     ts(B("dlc"), B("bm16"), STEP, A.mult, t[9], A.add)
-    ts(B("dlf"), B("bm16", 0, 128), STEP, A.mult, t[9], A.add)
-    fill(B("dlf", 15, 128, 16), -LOW)
+    ts(B("dlf"), B("bm16", 0, 112), STEP, A.mult, t[9], A.add)
+    fill(B("dlf", 15, 112, 16), -LOW)
     ts(NMI, MI, -1.0, A.mult, 1.0, A.add)
     ts(C8, I_, STEP8, A.mult, 8.0 - 15.0 * STEP8, A.add)
     ts(t[10], I_, -1.0, A.mult, 15.0, A.add)
@@ -552,42 +550,48 @@ def rank_program(g, core, T, topo):
     ts(CN, t[12], LOW, A.add)
     ts(t[13], I_, LOW + 160.0, A.add)
     ts(CF_, t[12], t[13], A.add)
-    fill(B("ob", 0, 16), 0.0), fill(B("ob", 336, 352), 0.0), fill(B("tr", 672, 704), 0.0)
+    fill(B("ob", 0, 16), 0.0), fill(B("ob", 336, 352), 0.0)
     iota(B("llf", 0, 16), [[16, 2], [1, 8]])
-    iota(B("llf", 16, 20), [[16, 2], [0, 2]], 232)
     ts(t[2], I_, 8.0, A.mult)
     ts(t[3], J1, 16.0, A.mult, t[2], A.add)
+    ts(t[21], MI, 16.0, A.mult, V_, A.add)
     ts(B("llo", 0, 16), B("llf", 0, 16), t[3], A.add)
-    ts(B("llo", 16, 20), B("llf", 16, 20), V_, A.add)
+    ts(B("llo", 16, 18), B("ob", 0, 2), t[21], A.add, 232.0, A.add)
     ts(B("lln", 0, 8), B("llf", 0, 8), t[2], A.add)
-    ts(B("lln", 8, 10), B("llf", 16, 18), V_, A.add, -112.0, A.add)
-    for at, base in ((17, 192), (14, 64), (10, 128), (7, 0), (3, 64), (0, 0)):
-        iota(B("dlp", at, at + 4), [[4, 2], [8, 2]], base)
-    ts(t[4], Q1, 32.0, A.mult)
-    ts(t[5], MI, 16.0, A.mult, t[4], A.add)
-    ts(B("dl"), B("dlp", 1, 21), t[5], A.add)
-    ts(B("xl"), B("ob", 0, 12), V_, A.add)
-    ts(RB, GL, 1280.0, A.mult, -639.0, A.add)
-    ts(t[7], HB, -168.0, A.mult, 88.0, A.add)
-    ts(t[8], HB, 80.0, A.mult, CN, A.add)
-    ts(BS, MI, t[7], A.mult, t[8], A.add)
-    iota(B("oc"), [[8, 7], [0, 16]])
-    iota(B("xp"), [[0, 28], [KEY, 8]])
-    iota(B("sd"), [[4, 320]], -640)
+    ts(B("lln", 8, 10), B("ob", 0, 2), V_, A.add, 120.0, A.add)
+    iota(B("pf", 0, 8), [[4, 2], [8, 2], [16, 2]])
+    ts(t[4], MI, 16.0, A.mult)
+    ts(t[5], Q1, 32.0, A.mult, t[4], A.add)
+    ts(t[18], MI, 128.0, A.mult)
+    ts(t[6], KQ, 32.0, A.mult, t[18], A.add)
+    for G in range(2):
+        ts(B("dl", 3 * G, 3 * G + 3), B("pf", 2, 8, 2), t[5], A.add, 64.0 * G, A.add)
+    ts(B("dl", 6, 13), B("pf", 0, 7), t[6], A.add)
+    ts(M8, MI, 8.0, A.mult)
+    ts(t[7], MI, -1.0, A.mult, HB, A.add)
+    ts(t[8], t[7], t[7], A.mult)
+    ts(t[14], MI, 32.0, A.mult, 96.0, A.add)
+    ts(BN, t[8], t[14], A.mult, CN, A.add)
+    ts(t[15], t[8], 128.0, A.mult, -96.0, A.add)
+    ts(BO, t[15], BN, A.add)
+    iota(B("r32"), [[32, 7]])
+    ts(B("nl", 0, 3), B("r32", 0, 3), t[4], A.add, 7.0, A.add)
+    ts(B("nl", 3, 4), MI, -88.0, A.mult, 103.0, A.add)
+    ts(B("nl", 4, 7), B("r32", 4, 7), t[4], A.add, -97.0, A.add)
+    iota(B("xp", 0, 112), [[0, 14], [1, 8]])
+    iota(B("xp", 112, 224), [[0, 14], [8, 8]])
+    iota(B("sd"), [[4, 320]])
+    ts(t[16], KH, -2.0 / KEY, A.mult)
+    ts(t[17], GL, -1280.0 / KEY, A.mult, t[16], A.add)
+    ts(B("sd"), B("sd"), -1.0 / KEY, A.mult, t[17], A.add)
+    for e in range(2):
+        ts(t[19 + e], GL, -1280.0, A.mult, 3840.0 + e, A.add)
     iota(B("flo"), [[16, 20], [0, 16]], -160)
     fill(B("acl", 0, 19), 128.0 - LOW), fill(B("acl", 19, 20), 0.0), fill(B("jv", 6060, 6080), -LOW)
     fill(B("rw0"), 0.0)
-    iota(B("xo", 0, 32), [[0, 4], [-KEY, 8]])
-    iota(B("xn", 0, 16), [[0, 2], [-KEY, 8]])
-    iota(B("lo", 0, 8), [[1, 8]])
-    iota(B("lo", 64, 72), [[1, 8]])
-    iota(B("pf", 0, 8), [[1, 2], [2, 2], [4, 2]])
-    iota(B("h1"), [[1, 2], [2, 2], [0, 2]])
-    iota(B("h2"), [[0, 4], [2, 2]], 640)
-    ts(B("h3"), B("h1"), GL, A.subtract, 1280.0, A.mult)
-    ts(B("h4"), B("h1"), GL, A.is_lt, 5120.0, A.mult)
-    tt(B("h3"), B("h3"), B("h2"), A.add)
-    tt(B("wp"), B("h3"), B("h4"), A.add)
+    iota(B("xo", 0, 32), [[0, 4], [-8, 8]])
+    iota(B("xn", 0, 16), [[0, 2], [1, 8]])
+    iota(B("lo", 0, 16), [[112, 2], [1, 8]])
     iota(B("ico"), [[1, 64], [0, 2]])
     ts(W8, O_, -7.0, A.mult, 8.0, A.add)
     ts(B("ico"), B("ico"), PH, A.is_equal, W8, A.mult)
@@ -615,13 +619,14 @@ def rank_program(g, core, T, topo):
     for e in range(2):
         for a in range(2):
             o = B("lb", 1024 * e + 512 * (1 - a), 1024 * e + 512 * (2 - a))
-            op({"g": 1020.0}, [B("one")], [o], lambda q, o=o, e=e, a=a: q.affine_select(view(o), view(B("one")), [[-2, 2], [-8, 64], [1, 4]], A.is_equal, 0.0, -512 * a - e, 8))
+            z = B("zb", 0, 512)
+            op({"g": 1020.0}, [z], [o], lambda q, o=o, e=e, a=a, z=z: q.affine_select(view(o), view(z), [[-2, 2], [-8, 64], [1, 4]], A.not_equal, 1.0, -512 * a - e, 8))
         quant("lq", 384 * e + 64, 384 * e + 320, "lb", 1024 * e)
 
     def calls(p, x):
         if p == "o":
             bk = BANK["co"]
-            for j, lo in enumerate((96, 192)):
+            for j, lo in enumerate((96, 208)):
                 mm(bk[j], 128, x, PAD + lo, "uq", 0)
                 ts(B("bt", 8 * j, 8 * j + 3), ps(bk[j], 1, 4), 0.0, A.is_gt)
             quant("bqo", 0, 128, "bt", 0)
@@ -632,14 +637,14 @@ def rank_program(g, core, T, topo):
         else:
             bk = BANK["cn"]
             mm(bk, 128, x, 0, "uq", 0)
-            ts(B("bs", 0, 3), ps(bk, 1, 4), 0.0, A.is_gt)
-            quant("bqn", 0, 128, "bs", 0)
+            ts(B("bt", 16, 19), ps(bk, 1, 4), 0.0, A.is_gt)
+            quant("bqn", 0, 128, "bt", 16)
             mm(bk, 128, "ca", 0, "bqn", 0)
             cp(B("ixn"), ps(bk, 0, 1))
             cp(B("lcn"), ("@", B("tab"), B("ixn")))
 
     def product(m):
-        j, grp = (0, m + 2) if m < 6 else (1, m - 6) if m < 14 else (2, m - 12)
+        j, grp = (0, m + 2) if m < 6 else (1, m - 6)
         at = 2 * (8 * j + 4 * (grp % 2) + POS[grp // 2] // 4)
         return B("lp", at, at + 1)
 
@@ -651,30 +656,36 @@ def rank_program(g, core, T, topo):
             cp(o, i, PIN["chain"])
 
     def rows(p):
-        x, n, lo, hi = ("xo", 2, 6, 20) if p == "o" else ("xn", 1, 0, 6)
+        x, n, lo, hi = ("xo", 2, 6, 13) if p == "o" else ("xn", 1, 0, 6)
         w = 16 * n
         for e in range(8):
             cp(B(x, w * e + w, w * e + 2 * w), ("@", B(x, w * e, w * e + w), B("lc" + p, 2 * n * e, 2 * n * e + n)), PIN["chain"])
         cp(B("z" + p), ("@", B(x, w, 9 * w), B("ll" + p)), PIN["rows"])
         turn(B("rt" + p), B("z" + p))
-        share("rt" + p, 10 * w)
-        ts(B("lp", w - 16, 2 * w - 16, 2), B("rt" + p, 8 * w, 10 * w, 4), -1.0 / KEY, A.mult)
-        tt(B("dd", 16 * lo, 16 * hi), ("@", B("rt" + p), B("dl", lo, hi)), B("xp", 0, 16 * (hi - lo)), A.add)
+        share("rt" + p, 8 * w + 32)
+        got = ("@", B("rt" + p), B("dl", lo, hi))
+        if p == "n":
+            cp(B("lp", 0, 16, 2), B("rtn", 128, 160, 4))
+        else:
+            ts(B("lp", 16, 32, 2), B("rto", 256, 288, 4), -0.125, A.mult, M8, A.add)
+            tt(B("d8o"), got, B("xp", 112, 224), A.add)
+            for m in range(7):
+                cp(B("lo", 16 * m + 16, 16 * m + 32), ("@", B("lo", 16 * m, 16 * m + 16), product(6 + m)), PIN["chain"])
+            latch(B("wo"), B("lo", 0, 112), B("dlf"))
+            ts(B("lf", 0, 7), B("wo", 15, 112, 16), CN, A.add)
+            cp(B("l2"), ("@", B("lo"), B("lf", 0, 7)), PIN["chain"])
+            tt(B("pq"), B("l2"), B("d8o"), A.subtract)
+            scan(B("ro"), B("d8o"), B("pq"), A.min, A.max)
+            got = ("@", B("ro"), B("nl", 0, 7))
+        tt(B("dd", 16 * lo, 16 * hi), got, B("xp", 0, 16 * (hi - lo)), A.subtract)
         if p == "o":
-            for m in range(6, 19):
-                step("lo", 8 * (m - 6 if m < 12 else m - 4), m)
-            latch(B("wo"), B("lo", 0, 128), B("dlf", 0, 128))
-            ts(B("lf"), B("wo", 15, 128, 16), CN, A.add)
             return
         for m in range(6):
-            step("pf", 8 * m, m, 8.0 * (m % 2))
-        latch(B("wn"), B("pf", 0, 48), B("dlf", 0, 48))
-        ts(B("otl", 0, 3), B("wn", 15, 48, 16), BS, A.add)
-        cp(B("pc"), ("@", B("pf", 48, 56), B("lf", 2, 4)), PIN["chain"])
-        tt(B("pq", 0, 48), ("@", B("pf", 48, 56), B("lf", 0, 3)), B("oc", 0, 48), A.add)
-        tt(B("pq", 48, 112), ("@", B("pc", 16, 24), B("lf", 4, 8)), B("oc", 48, 112), A.add)
-        latch(B("wc2"), B("pq"), B("dlf", 0, 112))
-        ts(B("otl", 4, 11), B("wc2", 15, 112, 16), BS, A.add)
+            step("pf", 8 * m, m, 32.0 * (m % 2))
+        latch(B("wn", 0, 48), B("pf", 0, 48), B("dlf", 0, 48))
+        ts(B("otl", 0, 3), B("wn", 15, 48, 16), BN, A.add)
+        latch(B("wn", 48, 64), B("pf", 48, 64), B("dlf", 0, 16))
+        ts(B("otl", 4, 11), B("r32"), B("wn", 63, 64), A.add, BO, A.add)
 
     turns = []
 
@@ -700,7 +711,7 @@ def rank_program(g, core, T, topo):
         if p == "n" and min(ALONE) < 6:
             mm(BANK["sn2"], w, "ur", 0, x, PAD + c0)
         tt(B("y" + p), ps(bank, 0, n), B("yc", 0, n), A.add)
-        if p == "o":
+        if p == "o" and max(ALONE) > 5:
             cp(B("sco"), ps(bank, 0, n), "s")
         scan(B("so" + p), B("d0", 0, n), B("y" + p), A.add, A.min)
 
@@ -716,7 +727,7 @@ def rank_program(g, core, T, topo):
         def row(lo, hi, q):
             if p == "n":
                 return ps(BANK["sn" if q == "v" else "sn2"], lo, hi)
-            return ps(BANK["so"], lo - c0, hi - c0) if q == "v" and HOLD else B("sco", lo - c0, hi - c0)
+            return ps(BANK["so"], lo - c0, hi - c0) if q == "v" else B("sco", lo - c0, hi - c0)
         for k in range(13 if p == "o" else 6):
             lo, m = c0 + 16 * k + 16, c0 // 16 + k
             if p == "o" and k > 10:
@@ -732,7 +743,7 @@ def rank_program(g, core, T, topo):
             else:
                 ts(o, row(lo, 320, "v"), own, A.is_gt)
                 if m not in COUNT:
-                    scan(B("jv", 6080 - 20 * (320 - lo) + m, 6080, 20), B("one", 0, 320 - lo), o, A.mult, A.add, -128.0)
+                    scan(B("jv", 6080 - 20 * (320 - lo) + m, 6080, 20), o, B("zb", 0, 320 - lo), A.add, A.add, -128.0)
                 else:
                     count(o, acc)
         for q, (at, lo) in enumerate(GO if p == "o" else GN):
@@ -745,12 +756,12 @@ def rank_program(g, core, T, topo):
         bk, skip = BANK["w" + p], 0 if p == "o" else PAD
         for k in range(4):
             mm(bk[k], n + skip, "lq", 384 * (k % 2) + 192 - 128 * (k // 2), x, PAD + c0 - skip)
-            cp(B("win", 4 * c0 + k, 4 * (c0 + n), 4), ps(bk[k], skip, skip + n), PIN["win"])
-        lo, hi = 4 * c0, 4 * (c0 + n)
+            cp(B("win", 3840 + 4 * c0 + k, 3840 + 4 * (c0 + n), 4), ps(bk[k], skip, skip + n), PIN["win"])
+        lo, hi = 3840 + 4 * c0, 3840 + 4 * (c0 + n)
         for s in range(1, 4):
             for h in (0, 64):
-                for d0, d1, s0 in ((0, 64 - 16 * s, 16 * s), (64 - 16 * s, 64, 0)):
-                    o, i = B("win", 1280 * s + lo, 1280 * s + hi, 1, (h + d0, h + d1)), B("win", lo, hi, 1, (h + s0, h + s0 + d1 - d0))
+                for d0, d1, s0, to in ((0, 64 - 16 * s, 16 * s, 1280 * s), (64 - 16 * s, 64, 0, 1280 * (s - 4))):
+                    o, i = B("win", to + lo, to + hi, 1, (h + d0, h + d1)), B("win", lo, hi, 1, (h + s0, h + s0 + d1 - d0))
                     dma("y", "s%s%d" % (p, r), [i], [o], view(o), view(i))
 
     def one_round(r):
@@ -778,31 +789,32 @@ def rank_program(g, core, T, topo):
         ts(B("rk"), B("cl", 15, 320, 16), CF_, A.add)
         w = B("ob", 16, 336)
         op({"v": 50 + 3.3 * CY * 320}, [B("rk"), B("sd")], [w], lambda e: e.tensor_copy(view(w).indirect(view(B("rk"))), view(B("sd"))))
-        turn(B("tr", 0, 320), w)
-        turn(B("tr", 320, 672), B("ob"))
-        share("tr", 672)
-        tt(B("tq"), ("@", B("wp"), B("xl", 0, 11)), B("tr", 0, 704, 4), A.add)
         for p, m0, n, l0 in (("n", 0, 6, 0), ("o", 6, 14, 24)):
-            lo, hi, at = 16 * m0, 16 * (m0 + n), 0 if p == "n" else 4
-            for G in range(2):
-                o = lo + 8 * n * G
-                tt(B("ot", o, o + 8 * n), ("@", B("tq"), B("otl", at, at + n // 2)), B("dd", o, o + 8 * n), A.subtract)
-            scan(B("sc", lo, hi), B("dd", lo, hi), B("ot", lo, hi), A.min, A.max)
+            lo, hi, at, tr = 16 * m0, 16 * (m0 + n), 0 if p == "n" else 4, "tr" + p
+            turn(B(tr, 0, 16 * n), B("ob", lo + 16, hi + 16))
+            turn(B(tr, 16 * n, 32 * n + 32), B("ob", lo, hi + 32))
+            share(tr, 32 * n + 32)
+            mid = hi if p == "n" else lo + 8 * n
+            for o in range(lo, mid, 8 * n):
+                tt(B("ot", o, o + 8 * n), ("@", B(tr), B("otl", at, at + n // 2)), B("dd", o, o + 8 * n), A.subtract)
+            scan(B("sc", lo, mid), B("dd", lo, mid), B("ot", lo, mid), A.max, A.min)
+            for h in (0, 64) if p == "o" else ():
+                cp(B("sc", mid + 7, hi, 8, (h, h + 64)), B("sc", lo + 7, mid, 8, (64 - h, 128 - h)), PIN["swap"])
             for e in range(2):
-                ts(B("il", l0 + 2 * n * e, l0 + 2 * n * (e + 1)), B("sc", lo + 7, hi, 8), float(e), A.add)
+                ts(B("il", l0 + 2 * n * e, l0 + 2 * n * (e + 1)), B("sc", lo + 7, hi, 8), -KEY, A.mult, t[19 + e], A.add)
             step = 12 if p == "n" else 14
             for l in range(l0, l0 + 4 * n, step):
                 cp(B("st", 16 * l, 16 * (l + step)), ("@", B("win"), B("il", l, l + step)), PIN["pick"])
             for e in range(4):
                 for G in range(2):
                     c = 0 if p == "n" else 512
-                    o, l = B("ta" if p == "n" else "tb", c + e, c + 64 * n, 4, (64 * G, 64 * G + 64)), l0 + n * (2 * (e % 2) + G)
+                    o, l = B("ta" if p == "n" else "tb", c + e, c + 64 * n, 4, (64 * G, 64 * G + 64)), l0 + n * (2 * (e % 2) + (G if p == "n" else G ^ e // 2))
                     cp(o, B("st", 16 * l, 16 * (l + n), 1, (64 * (e // 2), 64 * (e // 2) + 64)), PIN["lay"])
             if p == "n":
                 quant("qs%d" % (r + 1), 0, 128, "ta", 0)
                 send(r + 1)
             else:
-                quant("qx%d" % (r + 1), 128, 352, "tb", 512)
+                quant("qx%d" % (r + 1), 128, 368, "tb", 512)
 
     def send(r):
         t = "qs%d" % r
@@ -843,11 +855,11 @@ def rank_program(g, core, T, topo):
         mm(bank, hi - lo + skip, "vq", 0, x, PAD + lo - skip)
         cp(B("yb", lo, hi), ps(bank, skip, skip + hi - lo))
         c = B(x + "c", PAD + lo, PAD + hi)
-        dma("s" if lo == 0 else "y", "out", [c], [], T.oc[:, 4 * lo:4 * hi], bits(c))
+        dma("ys", "out", [c], [], T.oc[:, 4 * lo:4 * hi], bits(c))
         for k in range(4):
             s = B(x + "s", PAD + lo, PAD + hi, 1, (32 * k, 32 * k + 4))
-            dma("y", "out", [s], [], T.osc[4 * k:4 * k + 4, lo:hi], view(s))
-        dma("y", "out", [B("yb", lo, hi)], [], T.y[:, lo:hi], T.yb[:, lo:hi])
+            dma("ys", "out", [s], [], T.osc[4 * k:4 * k + 4, lo:hi], view(s))
+        dma("ys", "out", [B("yb", lo, hi)], [], T.y[:, lo:hi], T.yb[:, lo:hi])
 
     for r in range(ROUNDS):
         one_round(r)
@@ -855,11 +867,10 @@ def rank_program(g, core, T, topo):
         for G in range(2):
             o = 16 * m0 + 8 * n * G
             cp(B("rw0", 32 * G + m0, 32 * G + m0 + n), B("sc", o + 7, o + 8 * n, 8))
-    ts(B("rw1"), B("rw0"), RB, A.add, 1.0 / 1280, A.mult)
-    ts(B("rw2"), B("rw0"), 0.5, A.mult)
-    for n, f, m in (("rwi", "rw1", 3), ("rwj", "rw2", 1)):
-        cp(B(n), B(f))
-        ts(B(n), B(n), m, A.bitwise_and)
+    ts(B("rw1"), B("rw0"), -KEY / 1280, A.mult, -639.0 / 1280, A.add)
+    cp(B("rwi"), B("rw1"))
+    ts(B("rwj"), B("rw0"), -KEY / 2, A.mult)
+    ts(B("rwj"), B("rwj"), 1, A.bitwise_and)
     ts(B("rw3"), B("rwj"), 4.0, A.mult)
     tt(B("rw3"), B("rw3"), B("rwi"), A.add)
     turn(B("rwb"), B("rw3"))

import math
import numpy as np
from concourse.mybir import dt, AluOpType, AxisListType, ActivationFunctionType

CY = 0.83
HOP = 250.0
TRIES = 6000
MOVES = 100000
SEED = 1
REACH, MEAN, WARM = 40, 1.0, 5.0
SPAN, SIGMA, HEAT = 0.04, 800.0, 20.0
ALONE = (0, 1, 6, 7, 8)
COUNT = ()
DEAR = {"v": 2.5, "s": 1.0, "g": 1.0, "t": 1.0, "y": 1.0}
ROUNDS = 3
STEP, LOW = 1024.0, 131072.0
STEP8, LOW8 = 8.0, 256.0
KEY, HUGE = 8192.0, 2.0 ** 92
POS = (0, 8, 4, 12)
FIELDS = ((4, 1), (3, 1), (0, 4), (0, 3), (1, 6), (0, 1), (4, 3), (1, 3), (5, 2), (4, 2), (5, 1), (6, 1))
F32, BF, I32, U16 = "float32", "bfloat16", "int32", "uint16"
CODE, SC = "float8_e4m3fn_x4", "uint8"
SIZE = {F32: 4, BF: 2, I32: 4, U16: 2, CODE: 4, SC: 1}
GO = ((0, 96), (896, 160), (1536, 192))
GN = ((0, 0), (1280, 64))
PAD = 32
FIRST = False
BANK = {"co": (1, 2), "so": 0, "wo": (4, 5, 6, 7), "lw": (4, 5, 6, 7), "le": (1, 2, 3, 4), "cn": 5, "sn": 6, "sn2": 7, "wn": (1, 2, 4, 1)}
PIN = {"swap": "vs", "chain": "vs", "count": "vs", "shift": "vsg", "lay": "vsg", "win": "vs", "pick": "vs", "mask": "vs", "rows": "vs", "relu": "vs"}


def _scratch():
    d = {}

    def sb(name, n, t=F32):
        d[name] = ("sbuf", [128, n], t)

    def mx(name, n):
        sb(name + "c", n, CODE)
        sb(name + "s", n, SC)
    for b in range(8):
        d["ps%d" % b] = ("psum", [128, 512], F32)
    for n, w in (("xb", 1472), ("ub", 512), ("vb", 512), ("lb", 2048), ("zb", 768), ("ccb", 512), ("cab", 512),
                 ("bt", 528), ("ta", 512), ("tb", 1472), ("st", 1280), ("win", 8960), ("go", 2048), ("gn", 2304), ("jk", 1280),
                 ("m16", 128), ("ico", 128)):
        sb(n, w, BF)
    for n, w in (("uq", 128), ("ur", 128), ("vq", 128), ("lq", 768), ("wq", 512), ("cc", 128), ("ca", 128), ("bqo", 128),
                 ("bqn", 128), ("gq", 1600)):
        mx(n, w)
    for r in range(ROUNDS + 1):
        mx("qx%d" % r, PAD + 336)
        if r:
            mx("ld%d" % r, 128)
            mx("qs%d" % r, 128)
    sb("bi", 7, I32), sb("pi", 1), sb("half", 7), sb("pw", 7), sb("fl", 7), sb("chi", 64, I32), sb("chb", 64, I32), sb("rwi", 64, I32), sb("rwj", 64, I32)
    for n, w in (("cf", 48), ("ulf", 8), ("llf", 30), ("dlp", 21), ("dlf", 112), ("dlc", 320),
                 ("yc", 224), ("d0", 224), ("chf", 64), ("m8", 64), ("k8", 64), ("d8", 64), ("cht", 64), ("chs", 64), ("yo", 224), ("soo", 224), ("sco", 224),
                 ("yn", 96), ("son", 96), ("acl", 20), ("rc1", 20), ("rc2", 20), ("cl", 320), ("rkf", 20), ("ot", 320), ("sc", 320), ("rl", 384),
                 ("yb", 320), ("rw0", 64), ("rw1", 64), ("rw2", 64), ("rw3", 64), ("rwb", 64),
                 ("pf", 64), ("lo", 128), ("l2", 112), ("pq", 112), ("ro", 112), ("wn", 64), ("wo", 112), ("r32", 7), ("sd", 320), ("ob", 352), ("trn", 224), ("tro", 480)):
        sb(n, w)
    for n, w in (("bm16", 320), ("flo", 320), ("dlb", 256), ("dcs", 320), ("tf", 1024), ("tl", 1024), ("tab", 64),
                 ("xo", 288), ("xn", 144), ("zo", 288), ("zn", 160), ("rto", 288), ("rtn", 160), ("xp", 224), ("dd", 208), ("d8o", 112), ("jv", 6080), ("sg", 608)):
        sb(n, w, BF + "*")
    for n, w in (("ul", 8), ("otl", 12), ("llo", 18), ("lln", 10), ("dl", 14), ("lt", 8), ("ixo", 4), ("ixn", 1),
                 ("lco", 32), ("lcn", 16), ("lp", 48), ("lf", 8), ("nl", 8), ("rk", 20), ("il", 80)):
        sb(n, w, U16)
    return d


def _pack(d):
    place, at, rest = {}, {}, {}
    hosts = {F32: "kf", U16: "ku", I32: "ki", BF + "*": "kb"}
    for name, (where, shape, t) in d.items():
        host = hosts.get(t)
        if where != "sbuf" or host is None or name in ("chi", "yb", "rwb"):
            rest[name] = (where, shape, t)
            continue
        place[name] = (host, at.get(host, 0))
        at[host] = at.get(host, 0) + (shape[1] + 15) // 16 * 16
    for t, host in hosts.items():
        rest[host] = ("sbuf", [128, at[host]], t.strip("*"))
    return rest, place


BUFS = _scratch()
SCRATCH, PLACE = _pack(BUFS)
SEMAPHORES = (["cv", "ct", "cs", "cg", "dx", "du", "dv", "dw", "dc", "de", "z1", "z4", "z5", "z6", "out", "ls"]
              + [k + "%d" % r for k in ("so", "sn") for r in range(3)] + ["rc%d" % r for r in range(1, 4)])
PLANS = {}


def _plan(jobs):
    n = len(jobs)
    anc, pre, post = [0] * n, [], [[] for _ in jobs]
    for i, j in enumerate(jobs):
        keep = []
        for k in sorted(j["pre"], reverse=True):
            if not anc[i] >> k & 1:
                keep.append((k, 0.0 if "t" in j["c"] and "t" in jobs[k]["c"] else HOP))
                post[k].append((i, keep[-1][1]))
            anc[i] |= anc[k] | 1 << k
        pre.append(keep)
    cost, lat, dur = [j["c"] for j in jobs], [j["lat"] for j in jobs], [j["dur"] for j in jobs]

    def gap(busy, t, c):
        a, b = 0, len(busy)
        while a < b:
            m = (a + b) // 2
            if busy[m][1] <= t:
                a = m + 1
            else:
                b = m
        while a < len(busy) and busy[a][0] < t + c:
            t = busy[a][1]
            a += 1
        return t, a

    def lay(key, dep, lean, back):
        busy, st, fin, on = {q: [] for q in "vtsgye"}, [0.0] * n, [0.0] * n, [""] * n
        for i in follow(key, dep):
            t = max([fin[k] + h for k, h in dep[i]] or [0.0])
            c, d, best = cost[i], dur[i], None
            if d and back:
                t, x = gap(busy["e"], t, d)
                busy["e"].insert(x, (t, t + d))
                t += d + lat[i]
            for q in lean[i] or c:
                s, x = gap(busy[q], t, c[q])
                if best is None or s + c[q] * DEAR[q] < best[0]:
                    best = (s + c[q] * DEAR[q], s, x, q)
            s, x, q = best[1:]
            st[i], fin[i], on[i] = s, s + c[q], q
            busy[q].insert(x, (s, fin[i]))
            if d and not back:
                t, x = gap(busy["e"], fin[i] + lat[i], d)
                busy["e"].insert(x, (t, t + d))
                fin[i] = t + d
        return st, fin, on

    def follow(key, dep):
        done, out = [False] * n, []
        for i in sorted(range(n), key=lambda x: key[x]):
            stack = [i]
            while stack and not done[i]:
                x = stack[-1]
                m = [k for k, h in dep[x] if not done[k]]
                if m:
                    stack.extend(m)
                else:
                    stack.pop()
                    if not done[x]:
                        done[x] = True
                        out.append(x)
        return out

    def both(key, lean):
        st, fin, on = lay(key, pre, lean, False)
        st, fin, on = lay([-x for x in fin], post, on, True)
        st, fin, on = lay([-x for x in fin], pre, lean, False)
        seq = follow(st, pre)
        return max(times(seq, on)[1]), st, on, seq

    def times(seq, on):
        free, last, fin, why, engines, before = dict.fromkeys("vtsgy", 0.0), dict.fromkeys("vtsgy", -1), [0.0] * n, [-1] * n, 0.0, -1
        for i in seq:
            q = on[i]
            t, w = free[q], last[q]
            for k, h in pre[i]:
                x = fin[k] + h
                if x > t:
                    t, w = x, k
            t += cost[i][q]
            free[q], last[q] = t, i
            if dur[i]:
                t += lat[i]
                if engines > t:
                    t, w = engines, before
                t += dur[i]
                engines, before = t, i
            fin[i], why[i] = t, w
        return max(fin) + MEAN * sum(fin) / n, fin, why
    way = [0.0] * n
    for i in range(n - 1, -1, -1):
        way[i] = min(cost[i].values()) + lat[i] + dur[i] + max([way[k] + h for k, h in post[i]] or [0.0])
    best = now = both([-w for w in way], [""] * n)
    rng = np.random.RandomState(SEED)
    for step in range(TRIES):
        lo = rng.rand() * now[0]
        key, lean = list(now[1]), list(now[2])
        for i in [i for i in range(n) if lo <= key[i] <= lo + SPAN * now[0]]:
            key[i] += float(rng.normal()) * SIGMA
            r = rng.rand()
            if r < 0.3 and len(cost[i]) > 1:
                lean[i] = list(cost[i])[int(r * 10 * len(cost[i]))] if r < 0.1 else ""
        got = both(key, lean)
        if got[0] <= now[0] - HEAT * (1.0 - step / TRIES) * math.log(rng.rand() + 1e-9):
            now = got
            if got[0] < best[0]:
                best = got
    seq, on = best[3], best[2]
    now, fin, why = times(seq, on)
    best, path = (max(fin), seq, on), None
    for step, (a, b, c, d, e) in enumerate(np.random.RandomState(2).rand(MOVES, 5).tolist()):
        if path is None:
            i, path = fin.index(max(fin)), []
            while i >= 0:
                path.append(i)
                i = why[i]
        i = path[int(b / 0.7 * len(path))] if b < 0.7 else int((b - 0.7) / 0.3 * n)
        s2, o2, k = seq, on, why[i]
        if a < 0.3:
            if len(cost[i]) < 2:
                continue
            qs = [q for q in cost[i] if q != on[i]]
            o2 = on[:i] + [qs[int(c * len(qs))]] + on[i + 1:]
        elif a < 0.65:
            p = seq.index(i)
            to = max(0, p - 1 - int(c * REACH)) if k < 0 or anc[i] >> k & 1 else seq.index(k)
            mid = seq[to:p]
            s2 = seq[:to] + [x for x in mid if anc[i] >> x & 1] + [i] + [x for x in mid if not anc[i] >> x & 1] + seq[p + 1:]
        else:
            i = k if k >= 0 and d < 0.5 else i
            p = seq.index(i)
            mid = seq[p + 1:p + 2 + int(c * REACH)]
            s2 = seq[:p] + [x for x in mid if not anc[x] >> i & 1] + [i] + [x for x in mid if anc[x] >> i & 1] + seq[p + 1 + len(mid):]
        got, f2, w2 = times(s2, o2)
        if got <= now - (1.0 + WARM * (1.0 - step / MOVES)) * math.log(e + 1e-12):
            seq, on, now, fin, why, path = s2, o2, got, f2, w2, None
            if max(fin) < best[0]:
                best = (max(fin), seq, on)
    return best[0], [(i, best[2][i]) for i in best[1]]


def _make(g, T):
    queues = {"v": g.vector, "t": g.tensor, "s": g.scalar, "g": g, "y": g.sync}
    comp = {"v": "cv", "t": "ct", "s": "cs", "g": "cg"}
    total, known, recs, jobs = {}, {q: {} for q in queues}, {}, []

    def view(a):
        n, lo, hi, st, p0, p1 = a
        p = slice(None) if (p0, p1) == (0, 128) else slice(p0, p1)
        return T[n][p, lo:hi] if st == 1 else T[n][p, lo:hi:st]

    def span(a):
        return (a[0], 0, 512, 1, 0, 128) if a[0][:2] == "ps" else a

    def meet(a, x):
        return (x[1] < a[2] and a[1] < x[2] and x[4] < a[5] and a[4] < x[5]
                and not (a[3] > 1 and x[3] > 1 and (a[1] - x[1]) % min(a[3], x[3]) and max(a[3], x[3]) % min(a[3], x[3]) == 0))

    def cover(a, x):
        return a[1] <= x[1] and x[2] <= a[2] and a[4] <= x[4] and x[5] <= a[5] and (a[3] == 1 or (x[3] % a[3] == 0 and (a[1] - x[1]) % a[3] == 0))

    def wait(q, sem, val, clk):
        k = known[q]
        if k.get(sem, 0) >= val:
            return
        queues[q].wait_ge(T.sem[sem], int(val))
        k[sem] = val
        for s, x in clk.items():
            if k.get(s, 0) < x:
                k[s] = x

    def need(q, reads, writes, sem, self_ok):
        deps = []
        for lst, isw in ((reads, False), (writes, True)):
            for a in lst:
                a = span(a)
                ps = a[0][:2] == "ps"
                for x, rw, rq, rsem, val, clk in recs.get(a[0], []):
                    if not meet(a, x) or not (isw or rw or (ps and rq != q)):
                        continue
                    if rq == q == "t" and rw and isw:
                        continue
                    if rsem == sem and not self_ok:
                        continue
                    deps.append((rsem, val, clk))
        deps.sort(key=lambda d: -sum(d[2].values()))
        for s, v, c in deps:
            wait(q, s, v if s in comp.values() else total[s], c)

    def note(q, reads, writes, sem, val):
        clk = dict(known[q])
        for lst, isw in ((reads, False), (writes, True)):
            for a in lst:
                a = span(a)
                old = recs.get(a[0], [])
                if isw:
                    old = [x for x in old if not cover(a, x[0]) or (x[3] == sem and sem not in comp.values())]
                else:
                    old = [x for x in old if not (not x[1] and x[2] == q and x[3] == sem and cover(a, x[0]))]
                recs[a[0]] = old + [(a, isw, q, sem, val, clk)]

    def op(cost, reads, writes, fn):
        jobs.append(dict(c=cost, r=reads, w=writes, fn=fn, lat=0.0, dur=0.0, sem=None))

    def dma(q, sem, reads, writes, out, in_):
        a = (writes or reads)[0]
        rows, row = a[5] - a[4], (a[2] - a[1]) * SIZE[SCRATCH[a[0]][2]]
        jobs.append(dict(c=dict.fromkeys(q, 60.0), r=reads, w=writes, fn=(out, in_), lat=1300.0, dur=-(-rows // 16) * (30 + row / 12.0), sem=sem))

    def raw(q, reads, writes, fn, cost, lat=0.0, dur=0.0):
        jobs.append(dict(c={q: cost}, r=reads, w=writes, fn=fn, lat=lat, dur=dur, sem="raw"))

    def run():
        table, groups, alone = {}, {}, [False]
        for i, j in enumerate(jobs):
            pre = set()
            grp = j["sem"] if j["sem"] not in (None, "raw") else None
            acc = [(span(a), False) for a in j["r"]] + [(span(a), True) for a in j["w"]]
            for a, isw in acc:
                for x, xw, k in table.get(a[0], []):
                    bank = a[0][:2] == "ps" and not (len(j["c"]) == 1 and j["c"].keys() == jobs[k]["c"].keys())
                    if k != i and meet(a, x) and (xw or isw or bank) and (grp is None or jobs[k]["sem"] != grp):
                        pre.add(k)
            for a, isw in acc:
                old = table.get(a[0], [])
                if isw and grp is None:
                    old = [x for x in old if not cover(a, x[0])]
                table[a[0]] = old + [(a, isw, i)]
            for k in list(pre):
                if jobs[k]["sem"] not in (None, "raw"):
                    pre.update(groups[jobs[k]["sem"]])
            pre.discard(i)
            j["pre"] = pre
            if grp:
                groups.setdefault(grp, []).append(i)
        if len(jobs) not in PLANS:
            PLANS[len(jobs)] = _plan(jobs)
        for i, q in PLANS[len(jobs)][1]:
            j = jobs[i]
            if j["sem"] == "raw":
                j["fn"]()
                continue
            sem = j["sem"] or comp[q]
            need(q, j["r"], j["w"], sem, j["sem"] is None)
            if q == "g":
                shifted = any(a[4:] != (0, 128) for a in j["w"])
                if shifted or alone[0]:
                    wait(q, sem, total.get(sem, 0), {})
                alone[0] = shifted
            if j["sem"]:
                total[sem] = total.get(sem, 0) + 16
                queues[q].dma_start(*j["fn"]).then_inc(T.sem[sem], 16)
            else:
                total[sem] = total.get(sem, 0) + 1
                j["fn"](queues[q]).then_inc(T.sem[sem], 1)
            note(q, j["r"], j["w"], sem, total[sem])
    return dict(view=view, wait=wait, need=need, op=op, dma=dma, raw=raw, run=run, total=total)


def rank_program(g, core, T, topo):
    rank = T.rank_of(core)
    if rank is None:
        return
    K = _make(g, T)
    view, op, dma, raw = K["view"], K["op"], K["dma"], K["raw"]
    A, ACT = AluOpType, ActivationFunctionType

    def B(n, lo=0, hi=None, st=1, p=(0, 128)):
        h, at = PLACE.get(n, (n, 0))
        return (h, at + lo, at + (BUFS[n][1][1] if hi is None else hi), st, p[0], p[1])

    def cf(j):
        return B("cf", j, j + 1)

    def ps(b, lo, hi):
        return ("ps%d" % b, lo, hi, 1, 0, 128)

    def width(a):
        return (a[2] - a[1] + a[3] - 1) // a[3]

    def kind(a):
        return SCRATCH[a[1][0] if a[0] == "@" else a[0]][2]

    def vc(out, ins, two=False):
        n = width(out)
        if any(a[0] == "@" for a in ins):
            return 50 + 1.5 * CY * n
        if two and not any(a[0][:2] == "ps" for a in ins):
            return max(64, 2 * n) * CY
        return max(64, n * (0.5 if all(kind(a) in (BF, U16) for a in [out] + ins) else 1.0)) * CY

    def ac(out, ins):
        return (65 + 1.5 * CY * width(out)) if any(a[0] == "@" for a in ins) else 60 + CY * width(out)

    def costs(qs, out, ins):
        return {q: vc(out, ins) if q == "v" else ac(out, ins) if q == "s" else 170 + HOP + 2 * CY * width(out) for q in qs}

    def sc(x):
        return (view(x), [x]) if isinstance(x, tuple) else (x, [])

    def src(a):
        if a[0] == "@":
            return view(a[1]).indirect(view(a[2])), [a[1], a[2]]
        return view(a), [a]

    def ts(out, in0, s1, op0, s2=None, op1=None, qs="vs"):
        iv, ir = src(in0)
        (x1, r1), (x2, r2) = sc(s1), sc(s2)

        def fn(e):
            if e is g.vector:
                if op1 is None:
                    return e.tensor_scalar(view(out), iv, x1, None, op0)
                return e.tensor_scalar(view(out), iv, x1, x2, op0, op1)
            m, a = (x1, 0.0 if op1 is None else x2) if op0 == A.mult else (1.0, x1)
            return e.activation(view(out), iv, ACT.Identity, bias=a, scale=m)
        plain = kind(out) in (F32, BF) and kind(in0) in (F32, BF) and (op0 == A.mult and op1 in (None, A.add) or op0 == A.add and op1 is None)
        op(costs(qs if plain else "v", out, [in0]), ir + r1 + r2, [out], fn)

    def tt(out, in0, in1, o):
        iv, ir = src(in0)
        op({"v": vc(out, [in0, in1], True)}, ir + [in1], [out], lambda e: e.tensor_tensor(view(out), iv, view(in1), o))

    def cp(out, in_, qs="vs"):
        iv, ir = src(in_)

        def fn(e):
            if e is g.vector:
                return e.tensor_copy(view(out), iv)
            if e is g:
                return e.affine_select(view(out), iv, [[0, width(out)]], A.is_ge, 0.0, 0, 0)
            return e.activation(view(out), iv, ACT.Copy)
        op(costs(qs if kind(out) in (F32, BF) and kind(in_) in (F32, BF) else "v", out, [in_]), ir, [out], fn)

    def scan(out, d0, d1, o0, o1, first=0.0):
        op({"v": vc(out, [d0, d1])}, [d0, d1], [out], lambda e: e.tensor_tensor_scan(view(out), view(d0), view(d1), first, o0, o1))

    def latch(out, d1, d):
        scan(out, d1, d, A.max, A.add, -LOW)

    def turn(out, in_):
        op({"v": vc(out, [in_])}, [in_], [out], lambda e: e.transpose(view(out), view(in_)))

    def share(n, w):
        for k in range(4):
            cp(B(n, POS[k], w, 16, (32 * (k ^ 1), 32 * (k ^ 1) + 32)), B(n, POS[k], w, 16, (32 * k, 32 * k + 32)), PIN["shift"])
        for k in range(2):
            cp(B(n, 4 * k, w, 8, (64 - 64 * k, 128 - 64 * k)), B(n, 4 * k, w, 8, (64 * k, 64 * k + 64)), PIN["shift"])

    def fill(out, x):
        if x != int(x):
            return op({"v": vc(out, [])}, [], [out], lambda e: e.memset(view(out), x))
        op({"v": vc(out, []), "g": 130 + 2 * CY * width(out)}, [], [out], lambda e: e.memset(view(out), x) if e is g.vector else same(out, x))

    def same(out, x):
        return g.iota(view(out), [[0, width(out)]], int(x), 0, allow_small_or_imprecise_dtypes=True)

    def iota(out, pat, base=0, cm=0):
        if kind(out) == I32:
            op({"g": 140.0}, [], [out], lambda e: e.iota(view(out), pat, base, cm))
        else:
            op({"g": 130 + 2 * CY * width(out)}, [], [out], lambda e: e.iota(view(out), pat, base, cm, allow_small_or_imprecise_dtypes=True))

    def quant(name, lo, hi, tile, tlo):
        t, c, s = B(tile, tlo, tlo + 4 * (hi - lo)), B(name + "c", lo, hi), B(name + "s", lo, hi)
        op({"v": 12 + 0.88 * (hi - lo)}, [t], [c, s], lambda e: e.quantize_mx(view(c), view(s), view(t)))

    def mm(bank, n, w, wlo, x, xlo, start=True, stop=True):
        lc, ls, rc, rs = B(w + "c", wlo, wlo + 128), B(w + "s", wlo, wlo + 128), B(x + "c", xlo, xlo + n), B(x + "s", xlo, xlo + n)
        o = ps(bank, 0, n)
        op({"t": 0.6 * (n + 16)}, [lc, ls, rc, rs], [o], lambda e: e.matmul_mx(view(o), view(lc), view(ls), view(rc), view(rs), start, stop))

    def bits(a):
        return view(a).bitcast(dt.uint8) if kind(a) == CODE else view(a)

    def clear(out):
        z = B("zb", 0, width(out))
        op({"v": vc(out, []), "s": ac(out, []), "g": 130 + 2 * CY * width(out)}, [z], [out],
           lambda e: same(out, 0) if e is g else e.memset(view(out), 0.0) if e is g.vector else e.activation(view(out), view(z), ACT.Copy))

    def act(out, in_, f, bias=0.0, scale=1.0):
        x, r = sc(bias)
        op(costs("s", out, [in_]), [in_] + r, [out], lambda e: e.activation(view(out), view(in_), f, bias=x, scale=scale))

    dma("s", "dc", [], [B("chi", p=(0, 1))], T.chi[0:1, 0:64], T.ch[:, :])
    dma("y", "dx", [], [B("xb", 128, 1408)], view(B("xb", 128, 1408)), T.x[:, :])
    dma("y", "du", [], [B("ub")], view(B("ub")), T.u[:, :])
    fill(B("zb"), 0.0)
    quant("gq", 640, 832, "zb", 0)
    for lo, hi in ((0, 96), (320, 480), (1280, 1344)):
        for k in "cs":
            o, i = B("gq" + k, lo, hi), B("gq" + k, 640, 640 + hi - lo)
            dma("y", "z4", [i], [o], bits(o), bits(i))
    for a in (B("go", 0, 192), B("go", 896, 1088), B("go", 1536, 1856), B("gn", 0, 192), B("gn", 384, 1152, 4), B("gn", 1280, 1408), B("gn", 1283, 2240, 4),
              B("ta", 384, 512), B("bt"), B("xb", 0, 128), B("tb", 0, 128), B("xb", 1408), B("tb", 1408)):
        clear(a)

    def beside(r, sem, after):
        for k in "cs":
            o, i = B("ld%d%s" % (r, k), 96, 128), B("gq" + k, 640, 672)
            dma("y", sem, [i] + after, [o], bits(o), bits(i))
    beside(1, "z1", [])
    dma("y", "dw", [B("gqc", 640, 672)], [B("wqc")], T.wqc[:, 0:512].bitcast(dt.uint8), T.wc[:, :])
    dma("y", "dw", [B("gqc", 640, 672)], [B("wqs")], view(B("wqs")), T.ws[:, :])

    def later_loads(r):
        after = [B("win", 5120, 5136)]
        if r == 0:
            for e in range(2):
                for to, frm in ((0, 3), (5, 2)):
                    for k in "cs":
                        o, i = (B("lq" + k, 384 * e + 64 * c, 384 * e + 64 * c + 64) for c in (to, frm))
                        dma("y", "de", [i] + after, [o], bits(o), bits(i))
        if r < 2:
            beside(r + 2, "z%d" % (5 + r), after)
        if r == 1:
            dma("y", "dv", after, [B("vb")], view(B("vb")), T.v[:, :])
            quant("vq", 0, 128, "vb", 0)

    iota(B("pi"), [[1, 1]], 0, 1)
    fill(B("half"), 0.5)
    iota(B("ulf"), [[16, 8]])
    iota(B("bm16"), [[0, 20], [1, 16]])
    cp(B("ul"), B("ulf"))
    quant("uq", 0, 128, "ub", 0)
    quant("qx0", 0, PAD + 336, "xb", 0)
    op({"v": 210.0}, [B("uqc"), B("ul")], [B("urc")], lambda e: e.tensor_copy(T.urc[:, 0:128].bitcast(dt.uint32), T.uqc[:, 0:128].bitcast(dt.uint32).indirect(view(B("ul")))))
    op({"s": 225.0}, [B("uqs"), B("ul")], [B("urs")], lambda e: e.activation(T.urs[:, 0:128], T.uqs[:, 0:128].indirect(view(B("ul"))), ACT.Copy))
    scan(B("pw"), B("half"), B("zb", 0, 7), A.mult, A.add, 2.0)
    ts(B("pw"), B("pw"), B("pi"), A.mult, -0.49, A.add, qs="v")
    cp(B("bi"), B("pw"))
    cp(B("fl"), B("bi"))

    def field(j, s, w):
        if s + w == 7:
            return B("fl", s, s + 1)
        ts(cf(j), B("fl", s + w, s + w + 1), -float(1 << w), A.mult, B("fl", s, s + 1), A.add)
        return cf(j)
    HB, MI, I_, V_, PH, O_, G_, J1, KQ, GL, Q1, KH = (field(j, s, w) for j, (s, w) in enumerate(FIELDS))
    NMI, C8, CF_, CN, W8, VL, M8, BN, BO = (cf(j) for j in range(11, 20))
    t = [cf(j) for j in range(20, 48)]
    ts(t[0], I_, HUGE, A.mult)
    ts(t[1], I_, 4 * HUGE, A.mult, 2 * HUGE, A.add)
    act(B("yc"), B("bm16", 0, 224), ACT.Abs, t[0], -HUGE)
    act(B("d0"), B("bm16", 0, 224), ACT.Relu, t[1], -4 * HUGE)
    ts(B("dlb"), B("bm16", 0, 256), I_, A.is_gt, LOW8 + STEP8, A.mult)
    ts(B("dlb"), B("dlb"), -LOW8, A.add)
    ts(t[9], I_, -STEP, A.mult, STEP / 2, A.add)
    ts(B("dlc"), B("bm16"), STEP, A.mult, t[9], A.add)
    ts(B("dlf"), B("bm16", 0, 112), STEP, A.mult, t[9], A.add)
    fill(B("dlf", 15, 112, 16), -LOW)
    ts(NMI, MI, -1.0, A.mult, 1.0, A.add)
    ts(C8, I_, STEP8, A.mult, 8.0 - 15.0 * STEP8, A.add)
    ts(t[10], I_, -1.0, A.mult, 15.0, A.add)
    ts(t[11], I_, STEP / 2, A.mult, -7.5 * STEP, A.add)
    ts(t[12], t[10], t[11], A.mult)
    ts(CN, t[12], LOW, A.add)
    ts(t[13], I_, LOW + 160.0, A.add)
    ts(CF_, t[12], t[13], A.add)
    fill(B("ob", 0, 16), 0.0), fill(B("ob", 336, 352), 0.0)
    iota(B("llf", 0, 16), [[16, 2], [1, 8]])
    ts(t[2], I_, 8.0, A.mult)
    ts(t[3], J1, 16.0, A.mult, t[2], A.add)
    ts(t[21], MI, 16.0, A.mult, V_, A.add)
    ts(B("llo", 0, 16), B("llf", 0, 16), t[3], A.add)
    ts(B("llo", 16, 18), B("ob", 0, 2), t[21], A.add, 232.0, A.add)
    ts(B("lln", 0, 8), B("llf", 0, 8), t[2], A.add)
    ts(B("lln", 8, 10), B("ob", 0, 2), V_, A.add, 120.0, A.add)
    iota(B("pf", 0, 8), [[4, 2], [8, 2], [16, 2]])
    ts(t[4], MI, 16.0, A.mult)
    ts(t[5], Q1, 32.0, A.mult, t[4], A.add)
    ts(t[18], MI, 128.0, A.mult)
    ts(t[6], KQ, 32.0, A.mult, t[18], A.add)
    for G in range(2):
        ts(B("dl", 3 * G, 3 * G + 3), B("pf", 2, 8, 2), t[5], A.add, 64.0 * G, A.add)
    ts(B("dl", 6, 13), B("pf", 0, 7), t[6], A.add)
    ts(M8, MI, 8.0, A.mult)
    ts(t[7], MI, -1.0, A.mult, HB, A.add)
    ts(t[8], t[7], t[7], A.mult)
    ts(t[14], MI, 32.0, A.mult, 96.0, A.add)
    ts(BN, t[8], t[14], A.mult, CN, A.add)
    ts(t[15], t[8], 128.0, A.mult, -96.0, A.add)
    ts(BO, t[15], BN, A.add)
    iota(B("r32"), [[32, 7]])
    ts(B("nl", 0, 3), B("r32", 0, 3), t[4], A.add, 7.0, A.add)
    ts(B("nl", 3, 4), MI, -88.0, A.mult, 103.0, A.add)
    ts(B("nl", 4, 7), B("r32", 4, 7), t[4], A.add, -97.0, A.add)
    iota(B("xp", 0, 112), [[0, 14], [1, 8]])
    iota(B("xp", 112, 224), [[0, 14], [8, 8]])
    iota(B("sd"), [[4, 320]])
    ts(t[16], KH, -2.0 / KEY, A.mult)
    ts(t[17], GL, -1280.0 / KEY, A.mult, t[16], A.add)
    ts(B("sd"), B("sd"), -1.0 / KEY, A.mult, t[17], A.add)
    for e in range(2):
        ts(t[19 + e], GL, -1280.0, A.mult, 3840.0 + e, A.add)
    iota(B("flo"), [[16, 20], [0, 16]], -160)
    fill(B("acl", 0, 19), 128.0 - LOW), fill(B("acl", 19, 20), 0.0), fill(B("jv", 6060, 6080), -LOW)
    fill(B("rw0"), 0.0)
    iota(B("xo", 0, 32), [[0, 4], [-8, 8]])
    iota(B("xn", 0, 16), [[0, 2], [1, 8]])
    iota(B("lo", 0, 16), [[112, 2], [1, 8]])
    iota(B("ico"), [[1, 64], [0, 2]])
    ts(W8, O_, -7.0, A.mult, 8.0, A.add)
    ts(B("ico"), B("ico"), PH, A.is_equal, W8, A.mult)
    for j, w in enumerate((4.0, 2.0, 1.0, 0.0)):
        ts(B("cab", j, 512, 4), B("ico"), w, A.mult)
    quant("ca", 0, 128, "cab", 0)
    iota(B("m16"), [[1, 8], [0, 16]])
    for j in range(4):
        ts(B("ccb", j, 512, 4), B("m16"), G_, A.is_equal, -1.0, A.mult)
    quant("cc", 0, 128, "ccb", 0)
    op({"g": 350.0}, [B("chi")], [B("chb")], lambda e: e.partition_broadcast(view(B("chb")), T.chi[0:1, 0:64], 128))
    iota(B("m8"), [[0, 8], [1, 8]])
    cp(B("chf"), B("chb"))
    ts(B("k8"), B("m8"), V_, A.is_equal)
    act(B("d8"), B("m8"), ACT.Sign)
    tt(B("cht"), B("chf"), B("k8"), A.mult)
    scan(B("chs"), B("d8"), B("cht"), A.mult, A.add)
    ts(VL, V_, NMI, A.mult)
    ts(B("lt"), B("chs", 7, 64, 8), MI, A.mult, VL, A.add)
    for a in range(8):
        cp(B("tf", 128 * a, 128 * a + 128), ("@", B("chf", 8 * a, 8 * a + 8), B("lt")), "s")
    for a in range(4):
        scan(B("tl", 256 * a, 256 * a + 256), B("dlb"), B("tf", 256 * a, 256 * a + 256), A.add, A.max)
    ts(B("tab"), B("tl", 15, 1024, 16), C8, A.add)
    for e in range(2):
        for a in range(2):
            o = B("lb", 1024 * e + 512 * (1 - a), 1024 * e + 512 * (2 - a))
            z = B("zb", 0, 512)
            op({"g": 1020.0}, [z], [o], lambda q, o=o, e=e, a=a, z=z: q.affine_select(view(o), view(z), [[-2, 2], [-8, 64], [1, 4]], A.not_equal, 1.0, -512 * a - e, 8))
        quant("lq", 384 * e + 64, 384 * e + 320, "lb", 1024 * e)

    def calls(p, x):
        if p == "o":
            bk = BANK["co"]
            for j, lo in enumerate((96, 208)):
                mm(bk[j], 128, x, PAD + lo, "uq", 0)
                ts(B("bt", 8 * j, 8 * j + 3), ps(bk[j], 1, 4), 0.0, A.is_gt)
            quant("bqo", 0, 128, "bt", 0)
            mm(bk[0], 128, "ca", 0, "bqo", 0)
            cp(B("ixo", 0, 4, 2), ("ps%d" % bk[0], 0, 4, 2, 0, 128))
            for j in range(2):
                ts(B("lco", j, 32, 2), ("@", B("tab"), B("ixo", 2 * j, 2 * j + 1)), 16.0 * j, A.add)
        else:
            bk = BANK["cn"]
            mm(bk, 128, x, 0, "uq", 0)
            ts(B("bt", 16, 19), ps(bk, 1, 4), 0.0, A.is_gt)
            quant("bqn", 0, 128, "bt", 16)
            mm(bk, 128, "ca", 0, "bqn", 0)
            cp(B("ixn"), ps(bk, 0, 1))
            cp(B("lcn"), ("@", B("tab"), B("ixn")))

    def product(m):
        j, grp = (0, m + 2) if m < 6 else (1, m - 6)
        at = 2 * (8 * j + 4 * (grp % 2) + POS[grp // 2] // 4)
        return B("lp", at, at + 1)

    def step(n, at, m, add=0.0):
        o, i = B(n, at + 8, at + 24), ("@", B(n, at, at + 8), product(m))
        if add:
            ts(o, i, add, A.add, qs=PIN["chain"])
        else:
            cp(o, i, PIN["chain"])

    def rows(p):
        x, n, lo, hi = ("xo", 2, 6, 13) if p == "o" else ("xn", 1, 0, 6)
        w = 16 * n
        for e in range(8):
            cp(B(x, w * e + w, w * e + 2 * w), ("@", B(x, w * e, w * e + w), B("lc" + p, 2 * n * e, 2 * n * e + n)), PIN["chain"])
        cp(B("z" + p), ("@", B(x, w, 9 * w), B("ll" + p)), PIN["rows"])
        turn(B("rt" + p), B("z" + p))
        share("rt" + p, 8 * w + 32)
        got = ("@", B("rt" + p), B("dl", lo, hi))
        if p == "n":
            cp(B("lp", 0, 16, 2), B("rtn", 128, 160, 4))
        else:
            ts(B("lp", 16, 32, 2), B("rto", 256, 288, 4), -0.125, A.mult, M8, A.add)
            tt(B("d8o"), got, B("xp", 112, 224), A.add)
            for m in range(7):
                cp(B("lo", 16 * m + 16, 16 * m + 32), ("@", B("lo", 16 * m, 16 * m + 16), product(6 + m)), PIN["chain"])
            latch(B("wo"), B("lo", 0, 112), B("dlf"))
            ts(B("lf", 0, 7), B("wo", 15, 112, 16), CN, A.add)
            cp(B("l2"), ("@", B("lo"), B("lf", 0, 7)), PIN["chain"])
            tt(B("pq"), B("l2"), B("d8o"), A.subtract)
            scan(B("ro"), B("d8o"), B("pq"), A.min, A.max)
            got = ("@", B("ro"), B("nl", 0, 7))
        tt(B("dd", 16 * lo, 16 * hi), got, B("xp", 0, 16 * (hi - lo)), A.subtract)
        if p == "o":
            return
        for m in range(6):
            step("pf", 8 * m, m, 32.0 * (m % 2))
        latch(B("wn", 0, 48), B("pf", 0, 48), B("dlf", 0, 48))
        ts(B("otl", 0, 3), B("wn", 15, 48, 16), BN, A.add)
        latch(B("wn", 48, 64), B("pf", 48, 64), B("dlf", 0, 16))
        ts(B("otl", 4, 11), B("r32"), B("wn", 63, 64), A.add, BO, A.add)

    turns = []

    def count(i, acc):
        n = 320 * (len(turns) % 4)
        turns.append(0)
        j = B("jk", n, n + width(i))

        def fn(e):
            if e is g.vector:
                return e.tensor_reduce(view(acc), view(i), AxisListType.X, A.add)
            return e.activation(view(j), view(i), ACT.Copy, accum_out=view(acc))
        c = {"s": 20 + ac(j, []), "v": max(64, width(i)) * CY}
        op({q: c[q] for q in PIN["count"]}, [i], [j, acc], fn)

    def slot(tile, q, e, lo, hi):
        at, c0 = (GO if tile == "go" else GN)[q]
        return B(tile, at + 4 * (lo - c0) + e, at + 4 * (hi - c0), 4)

    def scores(p, x):
        bank, c0, n, w = (BANK["so"], 96, 224, 224) if p == "o" else (BANK["sn"], 0, 96, 320)
        mm(bank, w, "ur", 0, x, PAD + c0)
        if p == "n" and min(ALONE) < 6:
            mm(BANK["sn2"], w, "ur", 0, x, PAD + c0)
        tt(B("y" + p), ps(bank, 0, n), B("yc", 0, n), A.add)
        if p == "o" and max(ALONE) > 5:
            cp(B("sco"), ps(bank, 0, n), "s")
        scan(B("so" + p), B("d0", 0, n), B("y" + p), A.add, A.min)

    def within(p):
        c0, n = (96, 224) if p == "o" else (0, 96)
        d = slot("g" + p, 0, 0, c0, c0 + n)
        tt(d, ps(BANK["s" + p], 0, n), B("so" + p), A.is_gt)
        scan(B("dcs", c0, c0 + n), d, B("flo", c0, c0 + n), A.add, A.max, -1000.0)

    def compare(p):
        c0 = 96 if p == "o" else 0

        def row(lo, hi, q):
            if p == "n":
                return ps(BANK["sn" if q == "v" else "sn2"], lo, hi)
            return ps(BANK["so"], lo - c0, hi - c0) if q == "v" else B("sco", lo - c0, hi - c0)
        for k in range(13 if p == "o" else 6):
            lo, m = c0 + 16 * k + 16, c0 // 16 + k
            if p == "o" and k > 10:
                o = slot("gn", k - 11, 3 * (k - 11), lo, 320)
            else:
                o = slot("g" + p, (k + 1) // 4, (k + 1) % 4, lo, 320)
            own, acc = B("so" + p, 16 * k + 15, 16 * k + 16), B("acl", m, m + 1)
            if m in ALONE:
                at = 304 * (ALONE.index(m) % 2)
                i, j = row(lo, 320, "s"), B("sg", at, at + 320 - lo)
                op(costs("s", j, [i]), [i, own], [j], lambda e, i=i, j=j, own=own: e.activation(view(j), view(i), ACT.Sign, bias=view(own), scale=-1.0))
                op({"s": 20 + ac(j, [])}, [j], [o, acc], lambda e, j=j, o=o, acc=acc: e.activation(view(o), view(j), ACT.Relu, scale=-1.0, accum_out=view(acc)))
            else:
                ts(o, row(lo, 320, "v"), own, A.is_gt)
                if m not in COUNT:
                    scan(B("jv", 6080 - 20 * (320 - lo) + m, 6080, 20), o, B("zb", 0, 320 - lo), A.add, A.add, -128.0)
                else:
                    count(o, acc)
        for q, (at, lo) in enumerate(GO if p == "o" else GN):
            j = 320 * (q if p == "o" else 3 + q)
            quant("gq", j + lo, j + 320, "g" + p, at)
            mm(3, 320, "cc", 0, "gq", j, p == "o" and q == 0, p == "n" and q == 1)

    def window(p, x, r):
        c0, n = (96, 224) if p == "o" else (0, 96)
        bk, skip = BANK["w" + p], 0 if p == "o" else PAD
        for k in range(4):
            mm(bk[k], n + skip, "lq", 384 * (k % 2) + 192 - 128 * (k // 2), x, PAD + c0 - skip)
            cp(B("win", 3840 + 4 * c0 + k, 3840 + 4 * (c0 + n), 4), ps(bk[k], skip, skip + n), PIN["win"])
        lo, hi = 3840 + 4 * c0, 3840 + 4 * (c0 + n)
        for s in range(1, 4):
            for h in (0, 64):
                for d0, d1, s0, to in ((0, 64 - 16 * s, 16 * s, 1280 * s), (64 - 16 * s, 64, 0, 1280 * (s - 4))):
                    o, i = B("win", to + lo, to + hi, 1, (h + d0, h + d1)), B("win", lo, hi, 1, (h + s0, h + s0 + d1 - d0))
                    dma("y", "s%s%d" % (p, r), [i], [o], view(o), view(i))

    def one_round(r):
        x = "qx%d" % r
        if r and FIRST:
            arrive(r)
        calls("o", x)
        rows("o")
        scores("o", x)
        within("o")
        window("o", x, r)
        if r and not FIRST:
            arrive(r)
        compare("o")
        calls("n", x)
        scores("n", x)
        within("n")
        compare("n")
        window("n", x, r)
        later_loads(r)
        rows("n")
        tt(B("rc1"), B("dcs", 15, 320, 16), B("jv", 6060, 6080), A.add)
        tt(B("dlc", 15, 320, 16), B("rc1"), B("acl"), A.add)
        latch(B("cl"), ps(3, 0, 320), B("dlc"))
        ts(B("rk"), B("cl", 15, 320, 16), CF_, A.add)
        w = B("ob", 16, 336)
        op({"v": 50 + 3.3 * CY * 320}, [B("rk"), B("sd")], [w], lambda e: e.tensor_copy(view(w).indirect(view(B("rk"))), view(B("sd"))))
        for p, m0, n, l0 in (("n", 0, 6, 0), ("o", 6, 14, 24)):
            lo, hi, at, tr = 16 * m0, 16 * (m0 + n), 0 if p == "n" else 4, "tr" + p
            turn(B(tr, 0, 16 * n), B("ob", lo + 16, hi + 16))
            turn(B(tr, 16 * n, 32 * n + 32), B("ob", lo, hi + 32))
            share(tr, 32 * n + 32)
            mid = hi if p == "n" else lo + 8 * n
            for o in range(lo, mid, 8 * n):
                tt(B("ot", o, o + 8 * n), ("@", B(tr), B("otl", at, at + n // 2)), B("dd", o, o + 8 * n), A.subtract)
            scan(B("sc", lo, mid), B("dd", lo, mid), B("ot", lo, mid), A.max, A.min)
            for h in (0, 64) if p == "o" else ():
                cp(B("sc", mid + 7, hi, 8, (h, h + 64)), B("sc", lo + 7, mid, 8, (64 - h, 128 - h)), PIN["swap"])
            for e in range(2):
                ts(B("il", l0 + 2 * n * e, l0 + 2 * n * (e + 1)), B("sc", lo + 7, hi, 8), -KEY, A.mult, t[19 + e], A.add)
            step = 12 if p == "n" else 14
            for l in range(l0, l0 + 4 * n, step):
                cp(B("st", 16 * l, 16 * (l + step)), ("@", B("win"), B("il", l, l + step)), PIN["pick"])
            for e in range(4):
                for G in range(2):
                    c = 0 if p == "n" else 512
                    o, l = B("ta" if p == "n" else "tb", c + e, c + 64 * n, 4, (64 * G, 64 * G + 64)), l0 + n * (2 * (e % 2) + (G if p == "n" else G ^ e // 2))
                    cp(o, B("st", 16 * l, 16 * (l + n), 1, (64 * (e // 2), 64 * (e // 2) + 64)), PIN["lay"])
            if p == "n":
                quant("qs%d" % (r + 1), 0, 128, "ta", 0)
                send(r + 1)
            else:
                quant("qx%d" % (r + 1), 128, 368, "tb", 512)

    def send(r):
        t = "qs%d" % r
        dst = T.cores[(rank + r) % len(T.cores)]
        rid, pid = topo.addr(dst)[:2]
        m = topo.mask(core, dst)

        def fn():
            K["need"]("g", [B(t + "c", 0, 96), B(t + "s", 0, 96)], [], "ls", True)
            for k in "cs":
                o, i = T["ld%d%s" % (r, k)][:, 0:96], T[t + k][:, 0:96]
                if k == "c":
                    o, i = o.bitcast(dt.uint8), i.bitcast(dt.uint8)
                g.remote_dma(o, i, T.sem["rc%d" % r], T.sem["ls"], pid, rid, m)
                K["total"]["ls"] = K["total"].get("ls", 0) + len(topo.engines(core, dst))
        raw("g", [B(t + "c", 0, 96), B(t + "s", 0, 96)], [("sent%d" % r, 0, 1, 1, 0, 128)], fn, 600.0, 1200.0, 800.0)

    def arrive(r):
        frm = T.cores[(rank - r) % len(T.cores)]
        n = 2 * len(topo.engines(frm, core))
        raw("t", [("sent%d" % r, 0, 1, 1, 0, 128)], [B("ld%dc" % r, 0, 96), B("ld%ds" % r, 0, 96)], lambda: K["wait"]("t", "rc%d" % r, n, {}), 1.0)
        bw, be = BANK["lw"], BANK["le"]
        for b in range(4):
            mm(bw[b], 128, "wq", 128 * b, "ld%d" % r, 0)
            o, i = B("rl", 96 * b, 96 * b + 96), ps(bw[b], 0, 96)

            def fn(e, o=o, i=i):
                if e is g.vector:
                    return e.tensor_scalar(view(o), view(i), 0.0, 0.03125, A.max, A.mult)
                return e.activation(view(o), view(i), ACT.Relu, scale=0.03125)
            op(costs(PIN["relu"], o, [i]), [i], [o], fn)
            mm(be[b], 128, "lq", 384 * (b % 2) + 256 * (b // 2), "ld%d" % r, 0)
            tt(B("tb", 128 + b, 512, 4), o, ps(be[b], 0, 96), A.add)
        quant("qx%d" % r, 0, 128, "tb", 0)

    def store(lo, hi, bank):
        x, skip = "qx%d" % ROUNDS, 0 if lo else PAD
        mm(bank, hi - lo + skip, "vq", 0, x, PAD + lo - skip)
        cp(B("yb", lo, hi), ps(bank, skip, skip + hi - lo))
        c = B(x + "c", PAD + lo, PAD + hi)
        dma("ys", "out", [c], [], T.oc[:, 4 * lo:4 * hi], bits(c))
        for k in range(4):
            s = B(x + "s", PAD + lo, PAD + hi, 1, (32 * k, 32 * k + 4))
            dma("ys", "out", [s], [], T.osc[4 * k:4 * k + 4, lo:hi], view(s))
        dma("ys", "out", [B("yb", lo, hi)], [], T.y[:, lo:hi], T.yb[:, lo:hi])

    for r in range(ROUNDS):
        one_round(r)
    for m0, n, l0 in ((0, 6, 0), (6, 14, 24)):
        for G in range(2):
            o = 16 * m0 + 8 * n * G
            cp(B("rw0", 32 * G + m0, 32 * G + m0 + n), B("sc", o + 7, o + 8 * n, 8))
    ts(B("rw1"), B("rw0"), -KEY / 1280, A.mult, -639.0 / 1280, A.add)
    cp(B("rwi"), B("rw1"))
    ts(B("rwj"), B("rw0"), -KEY / 2, A.mult)
    ts(B("rwj"), B("rwj"), 1, A.bitwise_and)
    ts(B("rw3"), B("rwj"), 4.0, A.mult)
    tt(B("rw3"), B("rw3"), B("rwi"), A.add)
    turn(B("rwb"), B("rw3"))
    for h in range(8):
        q, c = 32 * (h // 2 % 2), 32 * (h // 4) + 16 * (h % 2)
        dma("y", "out", [B("rwb", c, c + 16, 1, (q, q + 20))], [], T.rw[h, :], T.rwb[q:q + 20, c:c + 16])
    if FIRST:
        arrive(3)
    store(96, 320, BANK["so"])
    if not FIRST:
        arrive(3)
    store(0, 96, BANK["cn"])
    K["run"]()
    for sem, n in sorted(K["total"].items()):
        K["wait"]("g", sem, n, {})
